import numpy as np, ml_dtypes
CORES = [83,85,87,115,117,119]
N = 6
BF = ml_dtypes.bfloat16
LN, B, SQ, KN, RO, SH = 192, 8, 64, 16, 5, 3
KS = KN * SQ; W = B * KS
def draw(rng):
    fe = np.clip(rng.integers(-6, 10, (N, 8, 16, 1, 1, 1), dtype=np.int8) + rng.integers(-3, 4, (N, 8, 1, 1, KN, 1), dtype=np.int8) + rng.integers(-9, 10, (N, 8, 16, B, KN, SQ), dtype=np.int8), -15, 15)
    kind = rng.integers(1, KN, (N, 8, 16, LN)); sq = rng.integers(0, SQ, (N, 8, 16, LN)); gone = rng.random((N, 8, 16, LN)) < 0.2
    near = (rng.integers(0, SQ, (1, 8, LN)) + rng.integers(0, 3, (N, 8, LN))) & (SQ - 1)
    sq[:, :, 0] = np.where(rng.random((N, 8, LN)) < 0.7, near, sq[:, :, 0])
    st = rng.integers(1, SQ, (N, 8, 16)); u = rng.integers(-127, 128, (N, 8, 16, 16)); v = rng.integers(-127, 128, (N, 8, 16, 16))
    u[..., 0] = np.where(rng.random((N, 8, 1)) < 0.5, np.abs(u[..., 0]), u[..., 0])
    return fe, kind, sq, gone, st, u, v
def pack(fe, kind, sq, gone, st, u, v):
    fe = fe.copy(); fe[:, :, :, :, 0] = 0
    po = np.where(gone & (np.arange(16) > 0)[None, None, :, None], 0, kind * SQ + sq)
    return {"feat": fe.reshape(N, 128, W).astype(np.float32).astype(BF), "pos": np.ascontiguousarray(po.reshape(N, 128, LN)).astype(np.int32), "step": np.ascontiguousarray(st.reshape(N, 128, 1)).astype(np.int32),
            "u": u.reshape(N, 128, 16).astype(np.float32).astype(BF), "v": v.reshape(N, 128, 16).astype(np.float32).astype(BF)}
def setup_inputs(rng):
    return pack(*draw(rng))
def setup_inputs_ends(rng):
    fe, kind, sq, gone, st, u, v = draw(rng); mode = np.array([0, 1, 2, 0, 1, 2, 1, 2])
    fe = (30 * rng.integers(0, 2, (N, 8, 16, B, KN, SQ), dtype=np.int8) - 15).astype(np.int8)
    fe[:, mode == 1] = (30 * rng.integers(0, 2, (N, 3, 1, B, KN, SQ)) - 15).astype(np.int8)
    kind[:] = KN - 1; sq[:] = SQ - 1; gone = rng.random(gone.shape) < 0.5
    low = rng.random((N, 8, LN)) < 0.5; kind[:, :, 0] = np.where(low, 1, KN - 1); sq[:, :, 0] = np.where(low, 0, SQ - 1)
    st = np.where(rng.random(st.shape) < 0.5, 1, SQ - 1); st[:, 0, 0] = 1; st[:, 0, 1] = SQ - 1
    u = 254 * rng.integers(0, 2, u.shape) - 127; v = 254 * rng.integers(0, 2, v.shape) - 127
    u[:, mode == 1] = 254 * rng.integers(0, 2, (N, 3, 1, 16)) - 127; v[:, mode == 1] = 254 * rng.integers(0, 2, (N, 3, 1, 16)) - 127
    for q in range(N):
        for g in (2, 5, 7):
            mine = KN - 1 - (q & 1); other = KN - 2 + (q & 1)
            fe[q, g, :, :, mine] = -15; fe[q, g, :, :, other] = 15; fe[q, g, :, :, KN - 3] = 14
            kind[q, g, :, 3::4] = mine; sq[q, g, :, 3::4] = SQ - 1 - (q & 1); gone[q, g, :, 3::4] = False
            w = np.arange(3, LN, 8); w = w[(((w >> 3) + q) & 1) == 1]; kind[q, g, 0, w] = KN - 3
            sq[q, g, 0, 15::16] = SQ - 1 if q == N - 2 else (B - 1) << SH if q == N - 1 else 1 << (SH - 1)
            st[q, g, 0] = SQ - 1
            u[q, g] = -127; u[q, g][:, [5, 10, 15, int(rng.integers(1, 15))]] = 127
            v[q, g] = 254 * rng.integers(0, 2, (1, 16)) - 127; v[q, g, :, 0] = -127; v[q, g][:, [7, 15]] = 127
    return pack(fe, kind, sq, gone, st, u, v)
def setup_inputs_corners(rng):
    fe, kind, sq, gone, st, u, v = draw(rng); i = np.arange(LN); c = i % 8
    st[:, 1::2] = st[:, 1::2, 0:1]
    edge = ((rng.integers(0, B, (N, 8, 1, LN)) << SH) - rng.integers(0, 2, (N, 8, 1, LN))) & (SQ - 1)
    k0 = np.where(c == 3, edge, sq[:, :, 0:1]); s0 = st[:, :, 0][:, :, None, None]; q = sq[:, :, 1:].copy()
    sm = np.take_along_axis(st, rng.integers(0, 16, (N, 8, 15 * LN)), 2).reshape(N, 8, 15, LN)
    q = np.where((c == 1) | (c == 6), k0, q); q = np.where(c == 2, k0 + s0, q)
    q = np.where(c == 4, k0 + s0 * rng.integers(0, 2, q.shape), q); q = np.where(c == 5, k0 - sm, q)
    sq = np.concatenate([k0, q & (SQ - 1)], axis=2)
    but = (c == 2) & ((i >> 3) % 2 == 1); sq[:, :, 15] = np.where(but, (sq[:, :, 15] + 1) & (SQ - 1), sq[:, :, 15])
    kind = np.where(c == 6, kind[:, :, 0:1], kind)
    gone = np.where(c == 0, True, np.where((c == 3) | (c == 7), gone, False))
    fe[:, 4] = -np.abs(fe[:, 4]); fe[:, 6] = np.abs(fe[:, 6])
    u[:, 0:2] = np.minimum(u[:, 0:2], 126); u[:, 0:2, :, 0] = 127
    u[:, 7, :, 8:] = u[:, 7, :, :8]; v[:, 7, :, 8:] = v[:, 7, :, :8]; v[:, 2, :, 8:] = v[:, 2, :, :8]
    return pack(fe, kind, sq, gone, st, u, v)
def setup_inputs_calm(rng):
    fe, kind, sq, gone, st, u, v = draw(rng); i = np.arange(LN)
    kind[:, :, 0] = 1; kind[:, :, 1:] = rng.integers(2, np.where(i % 2 == 0, 9, KN), (N, 8, 15, LN))
    sq = np.moveaxis(np.argsort(rng.random((N, 8, LN, SQ)), axis=-1)[..., :16], 3, 2)
    sq = (sq - sq[:, :, 0:1] + rng.integers(0, SQ, (1, 8, 1, LN)) + rng.integers(0, 3, (N, 8, 1, LN))) & (SQ - 1)
    gone[:, 4:] = False
    fe = rng.integers(-1, 2, (N, 8, 16, B, KN, SQ), dtype=np.int8); fe[:, :, :, :, :9] = 0; fe[:, 4:] += 8
    a = (np.arange(N)[:, None] + np.arange(8)) & 3; brim = (np.arange(8) >= 4)[None, :, None]; half = (np.arange(16) < 8)[None, None, :]
    fe[:, :, :, :, 1, :] = np.where(half, a[:, :, None] + np.where(brim, 6, 0), np.where(brim, 7, 2)).astype(np.int8)[..., None, None]
    t1 = rng.integers(0, 2, (N, 8, 1, 16)); t1[..., 1] = 1 - t1[..., 0]; t2 = rng.integers(0, 2, (N, 8, 1, 16)); t2[..., 1] = 1 - t2[..., 0]
    h = (np.arange(16) < 8)[:, None]
    u = np.where(h, 1 - t1, t1) * rng.integers(1, 16, (N, 8, 1, 1)); v = np.where(h, 1 - t2, t2) * rng.integers(1, 16, (N, 8, 1, 1))
    return pack(fe, kind, sq, gone, st, u, v)
def setup_inputs_spread(rng):
    fe, kind, sq, gone, st, u, v = draw(rng)
    lim = np.array([0, 1, 3, 7, 15], np.int8)[rng.integers(0, 5, (N, 8, 1, B, KN, SQ))]
    fe = np.clip(rng.integers(-15, 16, (N, 8, 16, B, KN, SQ), dtype=np.int8), -lim, lim)
    big = np.array([1, 15, 60, 127])
    lu = big[rng.integers(0, 4, (N, 8, 1, 16))]; lv = big[rng.integers(0, 4, (N, 8, 1, 16))]
    u = np.clip(rng.integers(-127, 128, u.shape), -lu, lu); v = np.clip(rng.integers(-127, 128, v.shape), -lv, lv)
    st = np.minimum(np.exp2(rng.random(st.shape) * (SQ.bit_length() - 1)).astype(np.int64), SQ - 1)
    kind = np.minimum(1 + ((KN - 1) * rng.random(kind.shape) ** 3).astype(np.int64), KN - 1)
    sq[:, ::2] = np.minimum((SQ * rng.random((N, 4, 16, LN)) ** 2).astype(np.int64), SQ - 1)
    gone = rng.random(gone.shape) < rng.random((N, 8, 1, LN))
    return pack(fe, kind, sq, gone, st, u, v)
def steepness(rng, neg):
    t = np.argsort(rng.random((N, 8, 16, 12)), axis=2) & 1
    w = np.concatenate([rng.integers(110, 116, (N, 8, 16, 4)), rng.integers(119, 127, (N, 8, 16, 1)) + t], axis=3)
    return w - np.where(neg, 237, 0)[None, :, None, None]
def setup_inputs_steep(rng):
    fe, kind, sq, gone, st, u, v = draw(rng); g = np.arange(8)
    fe = rng.integers(5, 11, (N, 8, 16, B, KN, SQ), dtype=np.int8); gone = rng.random(gone.shape) < 0.03
    st = 1 + np.argsort(rng.random((N, 8, SQ - 1)), axis=-1)[..., :16]
    u = steepness(rng, (g >> 1) % 2 == 1); v = steepness(rng, g % 2 == 1)
    u[:, 6:] = np.roll(u[:, 6:], -4, axis=3)
    return pack(fe, kind, sq, gone, st, u, v)
def check_inputs(d):
    bad = []
    for k, lo, hi in (("feat", -15, 15), ("pos", 0, KS - 1), ("step", 1, SQ - 1), ("u", -127, 127), ("v", -127, 127)):
        x = np.asarray(d[k]).astype(np.float32)
        if not (np.min(x) >= lo and np.max(x) <= hi): bad.append("range of " + k)
        elif not np.all(x == np.rint(x)): bad.append("whole numbers in " + k)
    p = np.asarray(d["pos"])
    if np.any((p > 0) & (p < SQ)): bad.append("piece numbers of kind 0 in pos")
    if np.any(p[:, ::16] < SQ): bad.append("an empty row 0 in pos")
    if np.any(np.asarray(d["feat"]).reshape(N, 128, B, KN, SQ)[:, :, :, 0].astype(np.float32) != 0): bad.append("columns of kind 0 in feat")
    return bad
def reference(feat, pos, step, u, v):
    fe = feat.astype(np.float32).astype(np.int32).reshape(N, 8, 16, W); st = step.astype(np.int64).reshape(N, 8, 16)
    ut = np.swapaxes(u.astype(np.float32).astype(np.int64).reshape(N, 8, 16, 16), 2, 3); vt = np.swapaxes(v.astype(np.float32).astype(np.int64).reshape(N, 8, 16, 16), 2, 3)
    cur = pos.astype(np.int64).reshape(N, 8, 16, LN)
    cl = np.zeros((N, 8, 16, LN, B), np.int64); ca = np.zeros((N, 8, 16, LN, B), np.int64); row = np.arange(16)[None, None, :, None]
    for t in range(RO):
        if t > 0: cur = np.roll(cur, 1, axis=0)
        b = (cur[:, :, 0] & (SQ - 1)) >> SH
        ix = np.broadcast_to(b[:, :, None, :, None], (N, 8, 16, LN, 1))
        o = np.take_along_axis(cl, ix, 4)[..., 0]; a = np.take_along_axis(ca, ix, 4)[..., 0]; ne = o != cur
        for k in range(16):
            w = np.take_along_axis(fe, (b * KS + o[:, :, k])[:, :, None, :], 3)
            a = np.where(ne[:, :, k][:, :, None, :], np.maximum(a - w, 0), a)
        for k in range(16):
            w = np.take_along_axis(fe, (b * KS + cur[:, :, k])[:, :, None, :], 3)
            a = np.where(ne[:, :, k][:, :, None, :], np.maximum(a + w, 0), a)
        np.put_along_axis(cl, ix, cur[..., None], 4); np.put_along_axis(ca, ix, a[..., None], 4)
        y = np.minimum(a, 127)
        k = np.argmax(np.where(cur > 0, np.matmul(ut, y), -2 ** 40), axis=2); m = np.argmax(np.matmul(vt, y), axis=2)
        old = np.take_along_axis(cur, k[:, :, None, :], 2)[:, :, 0]; s = old & (SQ - 1)
        new = (s + np.take_along_axis(st, m, 2)) & (SQ - 1)
        me = row == k[:, :, None, :]
        hit = (cur > 0) & (row > 0) & ((cur & (SQ - 1)) == new[:, :, None, :])
        cur = np.where(me, (old - s + new)[:, :, None, :], np.where(hit, 0, cur))
    return {"yl": cur.reshape(N, 128, LN).astype(np.float32), "ya": ca.reshape(N, 128, LN * B).astype(np.float32), "yc": cl.reshape(N, 128, LN * B).astype(np.float32)}

@@ -1,0 +1,568 @@
+from concourse.bass import DstId, RemoteDMATransfer
+from concourse.mybir import AluOpType as ALU, ActivationFunctionType as AF
+
+N, LN, PL = 6, 192, 5
+CH = [64, 64, 64]
+NC = len(CH)
+I0 = [sum(CH[:c]) for c in range(NC)]
+CFG = dict(
+    xv=[[22, 26, 8, 0], [24, 6, 12, 0], [10, 10, 12, 0], [10, 10, 4, 0], [18, 6, 0, 0]],
+    osq=True,
+    sub=[[0, 0, 0, 0]] * 5,
+    fold=True,
+    neg="AVAAAAAA",
+    bb="V", lf="V", of="V", sv="V", sg="V", r1e="V", wipe="V", yl="A", eqf=False, bc="rev")
+BIG = float(2 ** 24)
+MATS = ["I", "nI", "nBIG", "pHUGE", "nIw", "one", "none", "noneI", "kb", "dtie", "tie", "u16", "v16", "nu2k", "v2k"]
+BANKS = ["bOF", "bL", "bZO", "bZL", "bST", "bE1", "bE2", "bX"]
+
+SCRATCH = {
+    "tab": ("sbuf", [128, 16384], "bfloat16"),
+    "posi": ("sbuf", [128, LN], "int32"),
+    "sqi": ("sbuf", [128, LN], "int32"),
+    "kqi": ("sbuf", [128, LN], "int32"),
+    "ub": ("sbuf", [128, 16], "bfloat16"),
+    "vb": ("sbuf", [128, 16], "bfloat16"),
+    "stp": ("sbuf", [128, 8], "int32"),
+    "pc": ("sbuf", [128, 8], "int32"),
+    "rc": ("sbuf", [128, 8], "int32"),
+    "col": ("sbuf", [128, 16], "float32"),
+    "m16": ("sbuf", [128, 8], "float32"),
+    "d1": ("sbuf", [128, 128], "int32"),
+    "d2": ("sbuf", [128, 128], "int32"),
+    "d3": ("sbuf", [128, 128], "int32"),
+    "mat": ("sbuf", [128, 128 * len(MATS)], "bfloat16"),
+    "idf": ("sbuf", [128, 128], "float32"),
+    "idm": ("sbuf", [128, 128], "float32"),
+    "base": ("sbuf", [128, 144], "bfloat16"),
+    "c128": ("sbuf", [128, 8], "bfloat16"),
+    "ones": ("sbuf", [128, 64], "bfloat16"),
+    "rst": ("sbuf", [128, 128], "float32"),
+    "bci": ("sbuf", [128, 8], "int32"),
+    "bco": ("sbuf", [128, 8], "uint16"),
+    "ca": ("sbuf", [128, 8 * LN], "float32"),
+    "cc": ("sbuf", [128, 8 * LN], "float32"),
+    "lb": ("sbuf", [128, PL * 3 * LN], "bfloat16"),
+    "s2": ("sbuf", [128, PL * 2 * LN], "bfloat16"),
+    "kq": ("sbuf", [128, PL * LN], "bfloat16"),
+    "ylf": ("sbuf", [128, LN], "float32"),
+    "ha": ("sbuf", [128, 64 * 16], "bfloat16"),
+    "hb": ("sbuf", [128, 64 * 32], "float16"),
+}
+for _b in BANKS:
+    SCRATCH[_b] = ("psum", [128, 512], "float32")
+for _c in range(NC):
+    SCRATCH.update({
+        "gb%d" % _c: ("sbuf", [128, 64 * 32], "bfloat16"),
+        "rb%d" % _c: ("sbuf", [128, 64 * 32], "float16"),
+        "a1%d" % _c: ("sbuf", [128, 64], "float16"),
+        "bb%d" % _c: ("sbuf", [128, 64], "bfloat16"),
+        "off%d" % _c: ("sbuf", [128, 8], "uint16"),
+        "idx%d" % _c: ("sbuf", [128, 128], "uint16"),
+        "lf%d" % _c: ("sbuf", [128, 64], "float32"),
+        "of%d" % _c: ("sbuf", [128, 64], "float32"),
+        "eq%d" % _c: ("sbuf", [128, 64], "bfloat16"),
+        "yp%d" % _c: ("sbuf", [128, 192], "bfloat16"),
+        "mx%d" % _c: ("sbuf", [128, 128], "float32"),
+        "mf%d" % _c: ("sbuf", [128, 128], "float32"),
+        "sv%d" % _c: ("sbuf", [128, 64], "bfloat16"),
+        "sg%d" % _c: ("sbuf", [128, 64], "bfloat16"),
+    })
+
+SEMAPHORES = (["V", "A", "P", "E", "lpos", "lu", "lv", "lstp", "st", "sent"] + ["ltab%d" % h for h in range(4)]
+              + ["kq%d" % t for t in range(1, PL)]
+              + ["ar%d_%d" % (t, c) for t in range(1, PL) for c in range(NC)])
+
+EST = dict(cyc=0.00104, fix=0.0, r=1.56, sc=3.8, pe=0.0005, hop=0.1, same=0.06, remote=3.0, issue=0.5, load0=3.5,
+           load1=5.0, load2=6.5, load3=8.0, small=2.2, slack=0.12, lag=3.5)
+
+
+def popcount(m):
+    return bin(m).count("1")
+
+
+def cut(a, b, n):
+    e = [a + 2 * ((b - a) // 2 * j // n) for j in range(n)] + [b]
+    return [(e[j], e[j + 1]) for j in range(n) if e[j + 1] > e[j]]
+
+
+def build(g, core, T, topo):
+    ops, cur = [], [None]
+    rank = T.rank_of(core)
+    cores = T.cores
+    nxt, prv = cores[(rank + 1) % N], cores[(rank - 1) % N]
+    V, A, PE = g.vector, g.scalar, g.tensor
+    sgA = CFG["sg"] == "A"
+
+    def op(eng, fn, rd, wr, cost, sem=None, inc=1, bank=(), lat=None, name=""):
+        ops.append(dict(eng=eng, fn=fn, rd=list(rd), wr=list(wr), cost=cost, sem=sem or eng, inc=inc,
+                        bank=list(bank), lat=lat, name=name, chunk=cur[0]))
+
+    def ew(n):
+        return ("ew", n)
+
+    def mat(name):
+        k = MATS.index(name)
+        return T.mat[:, 128 * k:128 * (k + 1)]
+
+    def matc(name, a, b):
+        k = MATS.index(name)
+        return T.mat[:, 128 * k + a:128 * k + b]
+
+    def mm(bank, parts, name):
+        for p, (terms, rd) in enumerate(parts):
+            def fn(p=p, terms=terms):
+                last = None
+                for j, (o, l, r, _) in enumerate(terms):
+                    last = PE.matmul(o, l, r, p == 0 and j == 0, p == len(parts) - 1 and j == len(terms) - 1)
+                return last
+            op("E", fn, rd, [bank], ("pe", sum(x[3] for x in terms)), bank=[bank], name=name + str(p))
+
+    def ts(out, in0, s1, s2, o0, o1, rd, wr, n, bank=(), name=""):
+        if o1 is None:
+            op("V", lambda: V.tensor_scalar(out, in0, s1, None, o0), rd, wr, ew(n), bank=bank, name=name)
+        else:
+            op("V", lambda: V.tensor_scalar(out, in0, s1, s2, o0, o1), rd, wr, ew(n), bank=bank, name=name)
+
+    def act(out, in_, fn, rd, wr, cost, bank=(), name="", **kw):
+        op("A", lambda: A.activation(out, in_, fn, **kw), rd, wr, cost, bank=bank, name=name)
+
+    def ms(ap, val, wr, n, name=""):
+        op("V", lambda: V.memset(ap, val), [], wr, ew(n), name=name)
+
+    def fill(ap, pat, base, wr, n):
+        op("P", lambda: g.iota(ap, pat, base, 0, allow_small_or_imprecise_dtypes=True), [], wr, ("pool", n))
+
+    for h in range(4):
+        op("S", lambda h=h: g.sync.dma_start(T.tab[:, 2048 * h:2048 * (h + 1)], T.feat[:, 2048 * h:2048 * (h + 1)]),
+           [], ["tab%d" % h], ("dma",), "ltab%d" % h, 16, lat="load%d" % h)
+    op("A", lambda: A.dma_start(T.posi[:], T.pos[:]), [], ["posi"], ("dma",), "lpos", 16, lat="small")
+    op("A", lambda: A.dma_start(T.ub[:], T.u[:]), [], ["ub"], ("dma",), "lu", 16, lat="small")
+    op("A", lambda: A.dma_start(T.vb[:], T.v[:]), [], ["vb"], ("dma",), "lv", 16, lat="small")
+    op("A", lambda: A.dma_start(T.stp[:, 0:1], T.step[:]), [], ["stp"], ("dma",), "lstp", 16, lat="small")
+    for h in range(8):
+        src, dst = T.tab[:, 1024 * h:1024 * (h + 1)], T.tab[:, 8192 + 1024 * h:8192 + 1024 * (h + 1)]
+        if CFG["neg"][h] == "V":
+            ts(dst, src, -1.0, None, ALU.mult, None, ["tab%d" % (h // 2)], ["neg%d" % h], 512, name="neg")
+        else:
+            act(dst, src, AF.Identity, ["tab%d" % (h // 2)], ["neg%d" % h], ew(1024), name="neg", scale=-1.0)
+    tabk = ["tab%d" % h for h in range(4)]
+    negk = ["neg%d" % h for h in range(8)]
+
+    op("P", lambda: g.iota(T.d1[:], [[-1, 128]], 0, 1), [], ["d1"], ("pool", 128))
+    op("P", lambda: g.iota(T.d2[:], [[-16, 8], [0, 16]], 0, 1), [], ["d2"], ("pool", 128))
+    op("P", lambda: g.iota(T.pc[:, 0:1], [[0, 1]], 0, 1), [], ["pc"], ("pool", 1))
+    fill(T.c128[:, 0:4], [[128, 4]], 0, ["c128"], 4)
+    fill(mat("tie"), [[0, 8], [-1, 16]], 15, ["tie"], 128)
+    fill(T.ones[:], [[0, 64]], 1, ["ones"], 64)
+    fill(T.base[:, 0:16], [[0, 16]], 0, ["base0"], 16)
+    fill(T.ha[:], [[0, 1024]], 0, ["ha0", "ha1"], 1024)
+    for c in range(NC):
+        a, b = 8 * I0[c], 8 * (I0[c] + CH[c])
+        fill(T["yp%d" % c][:], [[0, 192]], 0, ["yp%d" % c], 192)
+        fill(T.cc[:, a:b], [[0, b - a]], 0, ["cc%d" % c], b - a)
+        fill(T.ca[:, a:b], [[0, b - a]], 0, ["ca%d" % c], b - a)
+
+    c_r8, c_king, c_hit, c_step, c_tie, c_pm, c_t2 = (T.col[:, j:j + 1] for j in range(7))
+    ts(mat("I"), T.d1[:], 0.0, None, ALU.is_equal, None, ["d1"], ["I"], 128)
+    ts(T.idf[:], T.d1[:], 0.0, None, ALU.is_equal, None, ["d1"], ["idf"], 128)
+    ts(c_pm, T.pc[:, 0:1], 64.0, -256.0, ALU.is_ge, ALU.mult, ["pc"], ["c_pm0"], 64)
+    ts(c_t2, c_pm, 128.0, None, ALU.add, None, ["c_pm0"], ["c_pm"], 64)
+    ts(T.idm[:], T.idf[:], c_t2, None, ALU.mult, None, ["idf", "c_pm"], ["idm"], 128)
+    for nm, s in (("nI", -1.0), ("nBIG", -BIG), ("pHUGE", 128 * BIG), ("nIw", -32.0 if sgA else -64.0)):
+        ts(mat(nm), mat("I"), s, None, ALU.mult, None, ["I"], [nm], 64)
+    ts(mat("kb"), T.d2[:], 0.0, 1024.0, ALU.is_equal, ALU.mult, ["d2"], ["kb"], 128)
+    ts(T.d3[:], T.d2[:], 4, None, ALU.arith_shift_right, None, ["d2"], ["d3"], 128)
+    ts(mat("one"), T.d3[:], 0.0, None, ALU.is_equal, None, ["d3"], ["one"], 128)
+    ts(mat("none"), mat("one"), -1.0, None, ALU.mult, None, ["one"], ["none"], 64)
+    op("V", lambda: V.tensor_tensor(mat("noneI"), mat("none"), mat("I"), ALU.subtract), ["none", "I"], ["noneI"],
+       ew(256))
+    ts(T.m16[:], mat("one")[:, 0::16], 16.0, None, ALU.mult, None, ["one"], ["m16"], 64)
+    ts(T.rc[:, 0:1], T.pc[:, 0:1], 15, None, ALU.bitwise_and, None, ["pc"], ["rc"], 64)
+    ts(c_r8, T.rc[:, 0:1], 8.0, -8.4375 if CFG["osq"] else -192.0, ALU.mult, ALU.add, ["rc"], ["c_r8"], 64)
+    ts(c_king, T.rc[:, 0:1], 0.0, None, ALU.is_equal, None, ["rc"], ["c_king"], 64)
+    ts(c_hit, c_king, -1032.0, 32.0 if sgA else 0.0, ALU.mult, ALU.add, ["c_king"], ["c_hit"], 64)
+    ts(c_tie, T.rc[:, 0:1], 128.0, -1920.0, ALU.mult, ALU.add, ["rc"], ["c_tie"], 64)
+    ts(c_step, T.stp[:, 0:1], c_tie, None, ALU.subtract, None, ["stp", "c_tie"], ["c_step"], 64)
+    ts(T.base[:, 16:144], mat("I"), c_king, 0.125 if CFG["osq"] else 1.0, ALU.mult, ALU.mult, ["I", "c_king"],
+       ["base"], 64)
+    ts(mat("dtie"), mat("I"), c_tie, None, ALU.mult, None, ["I", "c_tie"], ["dtie"], 64)
+    if CFG["bc"] != "rev":
+        op("P", lambda: g.iota(T.bci[:], [[16, 8]], 15, 0), [], ["bci"], ("pool", 8))
+        op("V", lambda: V.tensor_copy(T.bco[:], T.bci[:]), ["bci"], ["bco"], ew(64))
+    ms(T.rst[:], 0.0, ["rst"], 128)
+    ms(T.rst[:, 0::16], -float(2 ** 26), ["rst"], 64)
+    ms(T.hb[:], 0.0, ["hb0", "hb1"], 1024)
+    for gq in range(8):
+        for nm, src, key in (("u16", T.ub, "ub"), ("v16", T.vb, "vb")):
+            act(matc(nm, 16 * gq, 16 * gq + 16), src[:], AF.Identity, [key, "m16"], ["%s_%d" % (nm, gq)], ew(64),
+                scale=T.m16[:, gq:gq + 1])
+    uk, vk = (["%s_%d" % (nm, gq) for gq in range(8)] for nm in ("u16", "v16"))
+    ts(mat("nu2k"), mat("u16"), -128.0, None, ALU.mult, None, uk, ["nu2k"], 64)
+    ts(mat("v2k"), mat("v16"), 128.0, None, ALU.mult, None, vk, ["v2k"], 64)
+
+    def lbv(t, c):
+        w, b = CH[c], 3 * (t * LN + I0[c])
+        x, y, z = T.lb[:, b:b + w], T.lb[:, b + w:b + 2 * w], T.lb[:, b + 2 * w:b + 3 * w]
+        lo, hi = T.lb[:, b:b + 2 * w], T.lb[:, b + w:b + 3 * w]
+        return (z, y, x, hi, lo) if t % 2 == 0 else (x, y, z, lo, hi)
+
+    def s2v(t, c):
+        w, b = CH[c], 2 * (t * LN + I0[c])
+        x, y = T.s2[:, b:b + w], T.s2[:, b + w:b + 2 * w]
+        return (x, y, T.s2[:, b:b + 2 * w]) if t % 2 == 0 else (y, x, T.s2[:, b:b + 2 * w])
+
+    ts(T.sqi[:], T.posi[:], 63, None, ALU.bitwise_and, None, ["posi"], ["sqi"], LN)
+    ts(T.kqi[:], T.posi[:], 960, None, ALU.bitwise_and, None, ["posi"], ["kqi"], LN)
+    ts(T.kq[:, 0:LN], T.kqi[:], -64.0, None, ALU.add, None, ["kqi"], ["kq0"], LN)
+    for c in range(NC):
+        sq, dead = lbv(0, c)[0:2]
+        a, b = I0[c], I0[c] + CH[c]
+        ts(sq, T.sqi[:, a:b], 64.0, None, ALU.add, None, ["sqi"], ["sq0_%d" % c], 64)
+        ts(dead, T.posi[:, a:b], 64.0, None, ALU.is_lt, None, ["posi"], ["dead0_%d" % c], 64)
+
+    def kq_masks(src):
+        r = T.rank_of(src)
+        dst = [cores[(r + t) % N] for t in range(1, PL)]
+        far = [d for d in dst if topo.chip(d) != topo.chip(src)]
+        narrow = topo.mask(src, far[0]) if far else 0
+        out = {}
+        for d in dst:
+            m = topo.mask(src, d)
+            out[d] = m if m == narrow else m & ~narrow
+        return out
+
+    def send_kq():
+        mk = kq_masks(core)
+        for t in range(1, PL):
+            d = cores[(rank + t) % N]
+            rid, pid = topo.addr(d)[0:2]
+            g.remote_dma(T.kq[:, t * LN:(t + 1) * LN], T.kq[:, 0:LN], T.sem["kq%d" % t], T.sem.sent, pid, rid, mk[d])
+        return None
+    op("P", send_kq, ["kq0"], ["kqsent"], ("remote", 4), "sent", sum(popcount(m) for m in kq_masks(core).values()))
+    for t in range(1, PL):
+        src = cores[(rank - t) % N]
+        op("X", None, ["kqsent"], ["kq%d" % t], ("none",), "kq%d" % t, popcount(kq_masks(src)[core]), lat="remote")
+
+    m_out, m_in = topo.mask(core, nxt), topo.mask(prv, core)
+    rid_n, pid_n = topo.addr(nxt)[0:2]
+
+    def ply(t, c):
+        w, i0 = CH[c], I0[c]
+        cur[0] = c
+        k = w // 16
+        B = lambda s: T["%s%d" % (s, c)]
+        K = lambda s: "%s%d" % (s, c)
+        KT = lambda s: "%s%d_%d" % (s, t, c)
+        sq, dead, nsq, _, sent = lbv(t, c)
+        r1e, hit, src2 = s2v(t, c)
+        kq = T.kq[:, t * LN + i0:t * LN + i0 + w]
+        kqk = "kq%d" % t
+        bb, off, idx = B("bb")[:, 0:w], B("off")[:, 0:k], B("idx")
+        lf, of, eq = B("lf")[:, 0:w], B("of")[:, 0:w], B("eq")[:, 0:w]
+        sv, sg, y = B("sv")[:, 0:w], B("sg")[:, 0:w], B("yp")[:, 64:64 + w]
+        ca, cc = T.ca[:, 8 * i0:8 * (i0 + w)], T.cc[:, 8 * i0:8 * (i0 + w)]
+        ones = T.ones[:, 0:w]
+        tag = "%d.%d " % (t, c)
+        term = lambda o, m, r: (o, mat(m), r, 64)
+
+        if CFG["bb"] == "V":
+            ts(bb, sq, 0.125, 183.5625, ALU.mult, ALU.add, [KT("sq")], [K("bb")], 64, name=tag + "bb")
+        else:
+            act(bb, sq, AF.Identity, [KT("sq")], [K("bb")], ew(64), name=tag + "bb", scale=0.125, bias=183.5625)
+        po = T.bOF[:, 0:k]
+        mm("bOF", [([(po, mat("I"), T.c128[:, 0:k], 64)], ["I", "c128"]),
+                   ([(po, T.base[:, 16 - r:144 - r], (sq if CFG["osq"] else bb)[:, r:w:16], 64) for r in range(16)],
+                    ["base", "base0", KT("sq") if CFG["osq"] else K("bb")])], tag + "mm_off")
+        ts(off, po, c_r8, None, ALU.add, None, ["bOF", "c_r8"], [K("off")], 64, ["bOF"], tag + "off")
+        lsum = lambda o: [term(o, "I", kq), term(o, "I", sq), term(o, "nBIG", dead)]
+        lk = ["I", "nBIG", KT("sq"), KT("dead"), kqk]
+        pl, zo, zl = T.bL[:, 0:w], T.bZO[:, 0:w], T.bZL[:, 0:w]
+        mm("bL", [(lsum(pl), lk)], tag + "mm_L")
+        if CFG["lf"] == "V":
+            ts(lf, pl, 0.0, None, ALU.max, None, ["bL"], [K("lf")], 64, ["bL"], tag + "lf")
+        else:
+            act(lf, pl, AF.Relu, ["bL"], [K("lf")], ew(64), ["bL"], tag + "lf")
+        zpre = [(lsum(zl), lk), ([term(zl, "kb", bb)], ["kb", K("bb")])]
+        if t > 0:
+            if CFG["of"] == "V":
+                op("V", lambda: V.tensor_copy(of, cc.indirect(off)), [K("cc"), K("off")], [K("of")], ("gV", w),
+                   name=tag + "of")
+            else:
+                act(of, cc.indirect(off), AF.Identity, [K("cc"), K("off")], [K("of")], ("gA", w), name=tag + "of")
+            if CFG["eqf"]:
+                op("V", lambda: V.tensor_tensor(eq, cc.indirect(off), lf, ALU.is_equal),
+                   [K("cc"), K("off"), K("lf")], [K("eq")], ("gV", w), name=tag + "eq")
+            else:
+                op("V", lambda: V.tensor_tensor(eq, of, pl, ALU.is_equal), [K("of"), "bL"], [K("eq")], ew(64),
+                   bank=["bL"], name=tag + "eq")
+            mm("bZO", [([term(zo, "kb", bb)], ["kb", K("bb")]), ([(zo, T.idf[:], of, 256)], ["idf", K("of")]),
+                       ([term(zo, "nBIG", eq)], ["nBIG", K("eq")])], tag + "mm_ZO")
+            mm("bZL", zpre + [([term(zl, "nBIG", eq)], ["nBIG", K("eq")])], tag + "mm_ZL")
+            ts(idx[:, 1:2 * w:2], zl, -196608.0, 0.0, ALU.add, ALU.max, ["bZL"], [K("idy")], 64, ["bZL"],
+               tag + "idxL")
+            ts(idx[:, 0:2 * w:2], zo, 8192.0 - 196608.0, 0.0, ALU.add, ALU.max, ["bZO"], [K("idx")], 64, ["bZO"],
+               tag + "idxO")
+            m, H, hk, xv, win, wk = 2, T.hb, "hb", CFG["xv"][t][c], T.tab[:], tabk + negk + [K("idx"), K("idy")]
+        else:
+            mm("bZL", zpre, tag + "mm_ZL")
+            ts(idx[:, 0:w], zl, -196608.0, 0.0, ALU.add, ALU.max, ["bZL"], [K("idx"), K("idy")], w, ["bZL"],
+               tag + "idx")
+            m, H, hk, xv, win, wk = 1, T.ha, "ha", CFG["xv"][0][c], T.tab[:, 0:8192], tabk + [K("idx"), K("idy")]
+        xa, sl = w - xv, 16 * m
+        G, R = B("gb"), B("rb")
+        rk = [K("r0_"), K("r1_")]
+        two = t > 0 and w > 32 and CFG["sub"][t][c]
+        for j, (a, b) in enumerate([(0, 32), (32, w)] if two else [(0, w)]):
+            hs = [j] if two else [0, 1]
+            ka, kv = ([K("g%d%s_" % (h, q)) for h in hs] for q in "AV")
+            x = max(a, min(b, xa))
+            if x > a:
+                act(G[:, sl * a:sl * x], win.indirect(idx[:, m * a:m * x]), AF.Identity, wk,
+                    ka, ("gA", sl * (x - a)), name=tag + "gA")
+            if b > x:
+                op("V", lambda x=x, b=b: V.tensor_copy(G[:, sl * x:sl * b], win.indirect(idx[:, m * x:m * b])),
+                   wk, kv, ("gV", sl * (b - x)), name=tag + "gV")
+        for j, (a, b) in enumerate([(0, 32), (32, w)] if two else [(0, w)]):
+            hs = [j] if two else [0, 1]
+            gk = [K("g%d%s_" % (h, q)) for h in hs for q in "AV"]
+            hh = [hk + str(h) for h in hs]
+            g0, h0 = G[:, sl * a:sl * b:sl], H[:, sl * a:sl * b:sl]
+            if t > 0:
+                a1, ak = B("a1")[:, a:b], [K("a%d_" % h) for h in hs]
+                op("V", lambda a1=a1, g0=g0, a=a, b=b: V.tensor_tensor(
+                    a1, ca.indirect(B("off")[:, a // 16:b // 16]), g0, ALU.add), [K("ca"), K("off")] + gk, ak,
+                   ("gV", b - a), name=tag + "a1")
+                ts(h0, a1, 0.0, None, ALU.max, None, ak, hh, 64, name=tag + "h0")
+            else:
+                ts(h0, g0, 0.0, None, ALU.max, None, gk, hh, 64, name=tag + "h0")
+            ms(g0, -1024.0, gk, 64, tag + "wipe")
+            op("V", lambda a=a, b=b: V.tensor_tensor_scan(R[:, sl * a:sl * b], G[:, sl * a:sl * b],
+                                                          H[:, sl * a:sl * b], 0.0, ALU.add, ALU.max),
+               gk + hh, [rk[h] for h in hs], ew((b - a) * sl // 2), name=tag + "scan")
+        acc = R[:, sl - 1:sl * w:sl]
+        ts(y, acc, 127.0, None, ALU.min, None, rk, [K("yp")], 64, name=tag + "y")
+        op("V", lambda: V.tensor_copy(cc.indirect(off), lf), [K("lf"), K("off")], [K("cc")], ("sV", w),
+           name=tag + "scL")
+        op("V", lambda: V.tensor_copy(ca.indirect(off), acc), rk + [K("off")], [K("ca")], ("sV", w),
+           name=tag + "scA")
+        if t == PL - 1:
+            op("S", lambda: g.sync.dma_start(T.yc[:, 8 * i0:8 * (i0 + w)], cc), [K("cc")], [], ("dma",), "st", 16,
+               lat="small")
+            op("S", lambda: g.sync.dma_start(T.ya[:, 8 * i0:8 * (i0 + w)], ca), [K("ca")], [], ("dma",), "st", 16,
+               lat="small")
+        st, mx, mf = T.bST[:, 0:128], B("mx"), B("mf")
+        mm("bST", [([(st, mat("I"), mat("tie"), 128), (T.bST[0:w, 0:128], dead, mat("nBIG"), 128)],
+                    ["I", "tie", "nBIG", KT("dead")]),
+                   ([(st, B("yp")[:, 64:192], mat("u16"), 128), (st, B("yp")[:, 0:128], mat("v16"), 128)],
+                    [K("yp")] + uk + vk)], tag + "mm_S")
+        op("V", lambda: V.tensor_tensor_scan(mx[:], T.rst[:], st, 0.0, ALU.add, ALU.max), ["rst", "bST"],
+           [K("mx")], ew(128), bank=["bST"], name=tag + "max")
+        if CFG["bc"] == "rev":
+            op("V", lambda: V.tensor_tensor_scan(mf[:, ::-1], T.rst[:], mx[:, ::-1], 0.0, ALU.add, ALU.max),
+               ["rst", K("mx")], [K("mf")], ew(128), name=tag + "mf")
+        elif CFG["bc"] == "gV":
+            op("V", lambda: V.tensor_copy(mf[:], mx[:].indirect(T.bco[:])), ["bco", K("mx")], [K("mf")],
+               ("gV", 128), name=tag + "mf")
+        else:
+            act(mf[:], mx[:].indirect(T.bco[:]), AF.Identity, ["bco", K("mx")], [K("mf")], ("gA", 128),
+                name=tag + "mf")
+        e1, e2, ex = T.bE1[:, 0:w], T.bE2[:, 0:w], T.bX[:, 0:w]
+        mm("bE2", [([term(e2, "v2k", y)], ["v2k", K("yp")]),
+                   ([(e2, mf[:], T.idm[:, 64:64 + w], 256)], ["idm", K("mf")])], tag + "mm_E2")
+        mm("bE1", [([term(e1, "dtie", ones), term(e1, "pHUGE", dead)], ["dtie", "ones", "pHUGE", KT("dead")]),
+                   ([term(e1, "nu2k", y)], ["nu2k", K("yp")]),
+                   ([(e1, mf[:], T.idm[:, 0:w], 256)], ["idm", K("mf")])], tag + "mm_E1")
+        if CFG["sv"] == "V":
+            ts(sv, e2, c_step, 0.0, ALU.add, ALU.max, ["bE2", "c_step"], [K("sv")], 64, ["bE2"], tag + "sv")
+        else:
+            act(sv, e2, AF.Relu, ["bE2", "c_step"], [K("sv")], ew(64), ["bE2"], tag + "sv", bias=c_step)
+        op("V", lambda: V.tensor_tensor(nsq, e1, sq, ALU.min), ["bE1", KT("sq")], [KT("nsq")], ew(64),
+           bank=["bE1"], name=tag + "nsq")
+        mm("bX", [([term(ex, "one", sq)], ["one", KT("sq")]), ([term(ex, "one", sv)], [K("sv")]),
+                  ([term(ex, "none", nsq)], ["none", KT("nsq")])], tag + "mm_x")
+        if sgA:
+            act(sg, ex, AF.Sign, ["bX"], [K("sg")], ew(64), ["bX"], tag + "sg", bias=-127.5)
+        else:
+            ts(sg, ex, 128.0, None, ALU.is_ge, None, ["bX"], [K("sg")], 64, ["bX"], tag + "sg")
+        pk = ["I", "nI", "one", "noneI", "nIw", "ones", KT("sq"), KT("nsq"), K("sv")]
+        mm("bE1", [([term(e1, "one", sq), term(e1, "noneI", nsq), term(e1, "one", sv)], pk),
+                   ([term(e1, "nIw", sg)], [K("sg")])], tag + "mm_R2")
+        mm("bE2", [([term(e2, "I", sq), term(e2, "nI", nsq), term(e2, "one", sv)]
+                    + ([term(e2, "nIw", ones)] if sgA else []), pk),
+                   ([term(e2, "nIw", sg)], [K("sg")])], tag + "mm_R1")
+        plain = t < PL - 1 and not CFG["fold"]
+        if plain:
+            ts(eq, e1, c_hit, None, ALU.is_equal, None, ["bE1", "c_hit"], [K("eq")], 64, ["bE1"], tag + "hit")
+            op("V", lambda: V.tensor_tensor(hit, eq, dead, ALU.max), [K("eq"), KT("dead")], [KT("hit")], ew(128),
+               name=tag + "gone")
+        else:
+            ts(hit, e1, c_hit, None, ALU.is_equal, None, ["bE1", "c_hit"], [KT("hit")], 64, ["bE1"], tag + "hit")
+        if CFG["r1e"] == "V" or t == PL - 1 or plain:
+            op("V", lambda: V.tensor_tensor(r1e, e2, nsq, ALU.max), ["bE2", KT("nsq")], [KT("r1e")], ew(64),
+               bank=["bE2"], name=tag + "r1e")
+        else:
+            act(r1e, e2, AF.Identity, ["bE2"], [KT("r1e")], ew(64), ["bE2"], tag + "r1e")
+        if t < PL - 1:
+            land = lbv(t + 1, c)[3]
+            ar = "ar%d_%d" % (t + 1, c)
+
+            def hop():
+                if plain:
+                    g.remote_dma(land, src2, T.sem[ar], T.sem.sent, pid_n, rid_n, m_out)
+                    return None
+                g.remote_dma_fused([RemoteDMATransfer(dst_ids=[DstId(rid=rid_n, pnc=pid_n)], dma_engine_mask=m_out,
+                                                      remote_sem=T.sem[ar], srcs=[sent, src2], dsts=[land],
+                                                      alu_op=2)], local_sem=T.sem.sent)
+                return None
+            op("P", hop, [KT("nsq"), KT("dead"), KT("r1e"), KT("hit")], [KT("hop")], ("remote", 1), "sent",
+               popcount(m_out), name=tag + "hop")
+            op("X", None, [KT("hop")], ["sq%d_%d" % (t + 1, c), "dead%d_%d" % (t + 1, c)], ("none",), ar,
+               popcount(m_in), lat="remote")
+        else:
+            mm("bX", [([term(ex, "I", kq), term(ex, "nBIG", dead)], ["I", "nBIG", kqk, KT("dead")]),
+                      ([term(ex, "nBIG", hit), term(ex, "I", r1e)], [KT("hit"), KT("r1e")])], tag + "mm_Y")
+            yo = T.ylf[:, i0:i0 + w]
+            if CFG["yl"] == "V":
+                ts(yo, ex, 0.0, None, ALU.max, None, ["bX"], [K("ylf")], 64, ["bX"], tag + "yl")
+            else:
+                act(yo, ex, AF.Relu, ["bX"], [K("ylf")], ew(64), ["bX"], tag + "yl")
+            op("S", lambda: g.sync.dma_start(T.yl[:, i0:i0 + w], yo), [K("ylf")], [], ("dma",), "st", 16,
+               lat="small")
+
+    for t in range(PL):
+        for c in range(NC):
+            ply(t, c)
+    return ops
+
+
+def find_deps(ops):
+    lastw, readers, lastb = {}, {}, {}
+    deps = []
+    for j, o in enumerate(ops):
+        d = set()
+        for key in o["rd"]:
+            if key in lastw:
+                d.add(lastw[key])
+        for key in o["wr"]:
+            if key in lastw:
+                d.add(lastw[key])
+            d.update(readers.get(key, []))
+        for key in o["bank"]:
+            d.update(x for x in lastb.get(key, []) if ops[x]["eng"] != o["eng"])
+        d.discard(j)
+        deps.append(sorted(d))
+        for key in o["rd"]:
+            readers.setdefault(key, []).append(j)
+        for key in o["wr"]:
+            lastw[key] = j
+            readers[key] = []
+        for key in o["bank"]:
+            lastb[key] = [x for x in lastb.get(key, []) if ops[x]["eng"] == o["eng"]] + [j]
+    return deps
+
+
+def busy(o, e):
+    c = o["cost"]
+    if c[0] == "ew":
+        return e["fix"] + max(64, c[1]) * e["cyc"]
+    if c[0] == "gV":
+        return 0.05 + c[1] * e["r"] * e["cyc"]
+    if c[0] == "gA":
+        return 0.065 + c[1] * e["r"] * e["cyc"]
+    if c[0] == "sV":
+        return 0.05 + c[1] * e["sc"] * e["cyc"]
+    if c[0] == "pe":
+        return c[1] * e["pe"]
+    if c[0] == "pool":
+        return 0.13 + 2 * c[1] * e["cyc"]
+    if c[0] == "remote":
+        return c[1] * e["issue"]
+    if c[0] == "dma":
+        return 0.06
+    return 0.0
+
+
+def gap(a, b, e):
+    if a["lat"]:
+        return e[a["lat"]]
+    if b["eng"] == "X" or (a["eng"] == "E" and b["eng"] == "E"):
+        return 0.0
+    return e["same"] if a["eng"] == b["eng"] else e["hop"]
+
+
+def arrange(ops, deps, e, bump=None):
+    n = len(ops)
+    succ = [[] for _ in range(n)]
+    for j in range(n):
+        for d in deps[j]:
+            succ[d].append(j)
+    dur = [busy(o, e) for o in ops]
+    prio = [0.0] * n
+    for j in range(n - 1, -1, -1):
+        tail = e[ops[j]["lat"]] if ops[j]["lat"] else 0.0
+        if not succ[j] and ops[j]["chunk"] is not None:
+            tail += e["lag"] * (NC - 1 - ops[j]["chunk"])
+        prio[j] = dur[j] + max([tail] + [gap(ops[j], ops[s], e) + prio[s] for s in succ[j]])
+    if bump:
+        prio = [p + bump[j] for j, p in enumerate(prio)]
+    left = [len(d) for d in deps]
+    rdy = {}
+    for j in range(n):
+        if not left[j]:
+            rdy.setdefault(ops[j]["eng"], {})[j] = 0.0
+    free, end, order = {}, [0.0] * n, []
+    while len(order) < n:
+        first = {q: max(min(r.values()), free.get(q, 0.0)) for q, r in rdy.items() if r}
+        eng = min(first, key=lambda q: first[q])
+        lim = first[eng] + e["slack"]
+        j = max((x for x, v in rdy[eng].items() if v <= lim), key=lambda x: prio[x])
+        end[j] = max(rdy[eng][j], free.get(eng, 0.0)) + dur[j]
+        if eng != "X":
+            free[eng] = end[j]
+        order.append(j)
+        del rdy[eng][j]
+        for s in succ[j]:
+            left[s] -= 1
+            if not left[s]:
+                rdy.setdefault(ops[s]["eng"], {})[s] = max(end[d] + gap(ops[d], ops[s], e) for d in deps[s])
+    return order
+
+
+ORDER = {}
+
+
+def rank_program(g, core, T, topo):
+    if T.rank_of(core) is None:
+        return
+    ops = build(g, core, T, topo)
+    deps = find_deps(ops)
+    if "o" not in ORDER:
+        ORDER["o"] = arrange(ops, deps, EST)
+    place = {j: p for p, j in enumerate(ORDER["o"])}
+    queue = {"V": g.vector, "A": g.scalar, "E": g.tensor, "P": g, "S": g.sync}
+    count, known, done = {}, {q: {} for q in queue}, {}
+    for j in ORDER["o"]:
+        o = ops[j]
+        count[o["sem"]] = count.get(o["sem"], 0) + o["inc"]
+        if o["eng"] == "X":
+            done[j] = (o["sem"], count[o["sem"]], {})
+            continue
+        kn = known[o["eng"]]
+        for d in sorted(deps[j], key=lambda x: -place[x]):
+            if o["eng"] == "E" and ops[d]["eng"] == "E":
+                continue
+            s, val, clock = done[d]
+            if kn.get(s, 0) < val:
+                queue[o["eng"]].wait_ge(T.sem[s], val)
+                kn[s] = val
+            for s2, v2 in clock.items():
+                if kn.get(s2, 0) < v2:
+                    kn[s2] = v2
+        ins = o["fn"]()
+        if ins is not None:
+            ins.then_inc(T.sem[o["sem"]], o["inc"])
+        done[j] = (o["sem"], count[o["sem"]], dict(kn))
+    for s, val in count.items():
+        if max(kn.get(s, 0) for kn in known.values()) < val:
+            g.wait_ge(T.sem[s], val)

@@ -6,12 +6,12 @@ CH = [64, 64, 64]
 NC = len(CH)
 I0 = [sum(CH[:c]) for c in range(NC)]
 CFG = dict(
-    xv=[[22, 26, 8, 0], [24, 6, 12, 0], [10, 10, 12, 0], [10, 10, 4, 0], [18, 6, 0, 0]],
+    xv=[[22, 28, 0, 0], [18, 0, 10, 0], [16, 4, 4, 0], [10, 16, 8, 0], [18, 0, 2, 0]],
     osq=True,
-    sub=[[0, 0, 0, 0]] * 5,
+    sub=[[0, 0, 0, 0], [0, 1, 0, 0]] + [[0, 0, 0, 0]] * 3,
     fold=True,
     neg="AVAAAAAA",
-    bb="V", lf="V", of="V", sv="V", sg="V", r1e="V", wipe="V", yl="A", eqf=False, bc="rev")
+    bb="V", lf="V", of="V", sv="V", sg="V", r1e="V", wipe="V", yl="V", eqf=False, bc="rev")
 BIG = float(2 ** 24)
 MATS = ["I", "nI", "nBIG", "pHUGE", "nIw", "one", "none", "noneI", "kb", "dtie", "tie", "u16", "v16", "nu2k", "v2k"]
 BANKS = ["bOF", "bL", "bZO", "bZL", "bST", "bE1", "bE2", "bX"]
@@ -73,8 +73,8 @@ SEMAPHORES = (["V", "A", "P", "E", "lpos", "lu", "lv", "lstp", "st", "sent"] + [
               + ["kq%d" % t for t in range(1, PL)]
               + ["ar%d_%d" % (t, c) for t in range(1, PL) for c in range(NC)])
 
-EST = dict(cyc=0.00104, fix=0.0, r=1.56, sc=3.8, pe=0.0005, hop=0.1, same=0.06, remote=3.0, issue=0.5, load0=3.5,
-           load1=5.0, load2=6.5, load3=8.0, small=2.2, slack=0.12, lag=3.5)
+EST = dict(cyc=0.00093, fix=0.03307, r=1.56, sc=4.21722, pe=0.00052, hop=0.22, same=0.1361, remote=3.79521,
+           issue=0.51552, load0=3.5, load1=5.0, load2=6.5, load3=8.0, small=2.2, slack=0.13026, lag=3.5)
 
 
 def popcount(m):

@@ -6,14 +6,15 @@ CH = [64, 64, 64]
 NC = len(CH)
 I0 = [sum(CH[:c]) for c in range(NC)]
 CFG = dict(
-    xv=[[22, 28, 0, 0], [18, 0, 10, 0], [16, 4, 4, 0], [10, 16, 8, 0], [18, 0, 2, 0]],
+    xv=[[28, 30, 4, 0], [20, 6, 6, 0], [18, 14, 12, 0], [16, 12, 20, 0], [22, 14, 16, 0]],
     osq=True,
-    sub=[[0, 0, 0, 0], [0, 1, 0, 0]] + [[0, 0, 0, 0]] * 3,
-    fold=True,
+    sub=[[0, 0, 0, 0]] * 5,
+    fold=True, nosg=True,
     neg="AVAAAAAA",
-    bb="V", lf="V", of="V", sv="V", sg="V", r1e="V", wipe="V", yl="V", eqf=False, bc="rev")
+    bb="V", lf="V", of="V", sv="V", sg="V", r1e="V", wipe="V", yl="A", eqf=True, bc="rev")
 BIG = float(2 ** 24)
-MATS = ["I", "nI", "nBIG", "pHUGE", "nIw", "one", "none", "noneI", "kb", "dtie", "tie", "u16", "v16", "nu2k", "v2k"]
+MATS = ["I", "nI", "nBIG", "pHUGE", "nIw", "one", "none", "noneI", "kb", "dtie", "tie", "u16", "v16", "nu2k", "v2k",
+        "oneI", "m2", "nm2"]
 BANKS = ["bOF", "bL", "bZO", "bZL", "bST", "bE1", "bE2", "bX"]
 
 SCRATCH = {
@@ -44,6 +45,7 @@ SCRATCH = {
     "cc": ("sbuf", [128, 8 * LN], "float32"),
     "lb": ("sbuf", [128, PL * 3 * LN], "bfloat16"),
     "s2": ("sbuf", [128, PL * 2 * LN], "bfloat16"),
+    "s3": ("sbuf", [128, PL * 2 * LN], "bfloat16"),
     "kq": ("sbuf", [128, PL * LN], "bfloat16"),
     "ylf": ("sbuf", [128, LN], "float32"),
     "ha": ("sbuf", [128, 64 * 16], "bfloat16"),
@@ -73,8 +75,8 @@ SEMAPHORES = (["V", "A", "P", "E", "lpos", "lu", "lv", "lstp", "st", "sent"] + [
               + ["kq%d" % t for t in range(1, PL)]
               + ["ar%d_%d" % (t, c) for t in range(1, PL) for c in range(NC)])
 
-EST = dict(cyc=0.00093, fix=0.03307, r=1.56, sc=4.21722, pe=0.00052, hop=0.22, same=0.1361, remote=3.79521,
-           issue=0.51552, load0=3.5, load1=5.0, load2=6.5, load3=8.0, small=2.2, slack=0.13026, lag=3.5)
+EST = dict(cyc=0.00087, fix=0.02, r=1.3, sc=2.82577, pe=0.00061, hop=0.20057, same=0.2, remote=2.3, issue=0.50005,
+           load0=3.25, load1=4.5, load2=5.75, load3=7, small=2.2, slack=0.15, lag=2.61371)
 
 
 def popcount(m):
@@ -163,7 +165,7 @@ def build(g, core, T, topo):
         fill(T.cc[:, a:b], [[0, b - a]], 0, ["cc%d" % c], b - a)
         fill(T.ca[:, a:b], [[0, b - a]], 0, ["ca%d" % c], b - a)
 
-    c_r8, c_king, c_hit, c_step, c_tie, c_pm, c_t2 = (T.col[:, j:j + 1] for j in range(7))
+    c_r8, c_king, c_hit, c_step, c_tie, c_pm, c_t2, c_h2 = (T.col[:, j:j + 1] for j in range(8))
     ts(mat("I"), T.d1[:], 0.0, None, ALU.is_equal, None, ["d1"], ["I"], 128)
     ts(T.idf[:], T.d1[:], 0.0, None, ALU.is_equal, None, ["d1"], ["idf"], 128)
     ts(c_pm, T.pc[:, 0:1], 64.0, -256.0, ALU.is_ge, ALU.mult, ["pc"], ["c_pm0"], 64)
@@ -175,12 +177,18 @@ def build(g, core, T, topo):
     ts(T.d3[:], T.d2[:], 4, None, ALU.arith_shift_right, None, ["d2"], ["d3"], 128)
     ts(mat("one"), T.d3[:], 0.0, None, ALU.is_equal, None, ["d3"], ["one"], 128)
     ts(mat("none"), mat("one"), -1.0, None, ALU.mult, None, ["one"], ["none"], 64)
-    op("V", lambda: V.tensor_tensor(mat("noneI"), mat("none"), mat("I"), ALU.subtract), ["none", "I"], ["noneI"],
-       ew(256))
-    ts(T.m16[:], mat("one")[:, 0::16], 16.0, None, ALU.mult, None, ["one"], ["m16"], 64)
+    op("V", lambda: V.tensor_tensor(mat("noneI"), mat("none"), mat("I"), ALU.add if CFG["nosg"] else ALU.subtract),
+       ["none", "I"], ["noneI"], ew(256))
     ts(T.rc[:, 0:1], T.pc[:, 0:1], 15, None, ALU.bitwise_and, None, ["pc"], ["rc"], 64)
-    ts(c_r8, T.rc[:, 0:1], 8.0, -8.4375 if CFG["osq"] else -192.0, ALU.mult, ALU.add, ["rc"], ["c_r8"], 64)
     ts(c_king, T.rc[:, 0:1], 0.0, None, ALU.is_equal, None, ["rc"], ["c_king"], 64)
+    if CFG["nosg"]:
+        ts(mat("oneI"), mat("noneI"), -1.0, None, ALU.mult, None, ["noneI"], ["oneI"], 64)
+        op("V", lambda: V.tensor_tensor(mat("nm2"), mat("oneI"), mat("I"), ALU.subtract), ["oneI", "I"], ["nm2"],
+           ew(256))
+        ts(mat("m2"), mat("nm2"), -1.0, None, ALU.mult, None, ["nm2"], ["m2"], 64)
+        ts(c_h2, c_king, -1096.0, 64.0, ALU.mult, ALU.add, ["c_king"], ["c_h2"], 64)
+    ts(T.m16[:], mat("one")[:, 0::16], 16.0, None, ALU.mult, None, ["one"], ["m16"], 64)
+    ts(c_r8, T.rc[:, 0:1], 8.0, -8.4375 if CFG["osq"] else -192.0, ALU.mult, ALU.add, ["rc"], ["c_r8"], 64)
     ts(c_hit, c_king, -1032.0, 32.0 if sgA else 0.0, ALU.mult, ALU.add, ["c_king"], ["c_hit"], 64)
     ts(c_tie, T.rc[:, 0:1], 128.0, -1920.0, ALU.mult, ALU.add, ["rc"], ["c_tie"], 64)
     ts(c_step, T.stp[:, 0:1], c_tie, None, ALU.subtract, None, ["stp", "c_tie"], ["c_step"], 64)
@@ -207,10 +215,10 @@ def build(g, core, T, topo):
         lo, hi = T.lb[:, b:b + 2 * w], T.lb[:, b + w:b + 3 * w]
         return (z, y, x, hi, lo) if t % 2 == 0 else (x, y, z, lo, hi)
 
-    def s2v(t, c):
+    def s2v(t, c, buf=T.s2):
         w, b = CH[c], 2 * (t * LN + I0[c])
-        x, y = T.s2[:, b:b + w], T.s2[:, b + w:b + 2 * w]
-        return (x, y, T.s2[:, b:b + 2 * w]) if t % 2 == 0 else (y, x, T.s2[:, b:b + 2 * w])
+        x, y = buf[:, b:b + w], buf[:, b + w:b + 2 * w]
+        return (x, y, buf[:, b:b + 2 * w]) if t % 2 == 0 else (y, x, buf[:, b:b + 2 * w])
 
     ts(T.sqi[:], T.posi[:], 63, None, ALU.bitwise_and, None, ["posi"], ["sqi"], LN)
     ts(T.kqi[:], T.posi[:], 960, None, ALU.bitwise_and, None, ["posi"], ["kqi"], LN)
@@ -379,6 +387,43 @@ def build(g, core, T, topo):
             act(sv, e2, AF.Relu, ["bE2", "c_step"], [K("sv")], ew(64), ["bE2"], tag + "sv", bias=c_step)
         op("V", lambda: V.tensor_tensor(nsq, e1, sq, ALU.min), ["bE1", KT("sq")], [KT("nsq")], ew(64),
            bank=["bE1"], name=tag + "nsq")
+        if CFG["nosg"]:
+            x3, y3, src3 = s2v(t, c, T.s3)
+            mm("bX", [([term(ex, "oneI", sq)], ["oneI", KT("sq")]), ([term(ex, "one", sv)], ["one", K("sv")]),
+                      ([term(ex, "none", nsq)], ["none", KT("nsq")])], tag + "mm_x")
+            mm("bE2", [([term(e2, "m2", sq), term(e2, "one", sv)], ["m2", "one", KT("sq"), K("sv")]),
+                       ([term(e2, "nm2", nsq)], ["nm2", KT("nsq")])], tag + "mm_z")
+            ts(hit, ex, c_hit, None, ALU.is_equal, None, ["bX", "c_hit"], [KT("hit")], 64, ["bX"], tag + "h1")
+            ts(y3, ex, c_h2, None, ALU.is_equal, None, ["bX", "c_h2"], [KT("hit2")], 64, ["bX"], tag + "h2")
+            ts(r1e, e2, 0.0, None, ALU.max, None, ["bE2"], [KT("r1e")], 64, ["bE2"], tag + "up")
+            ts(x3, e2, 128.0, -64.0, ALU.is_ge, ALU.mult, ["bE2"], [KT("wrap")], 64, ["bE2"], tag + "wrap")
+            four = [KT("hit"), KT("hit2"), KT("r1e"), KT("wrap")]
+            if t < PL - 1:
+                land = lbv(t + 1, c)[3]
+                ar = "ar%d_%d" % (t + 1, c)
+
+                def hop3():
+                    g.remote_dma_fused([RemoteDMATransfer(
+                        dst_ids=[DstId(rid=rid_n, pnc=pid_n)], dma_engine_mask=m_out, remote_sem=T.sem[ar],
+                        srcs=[sent, src2, src3], dsts=[land], alu_op=1)], local_sem=T.sem.sent)
+                    return None
+                op("P", hop3, [KT("nsq"), KT("dead")] + four, [KT("hop")], ("remote", 1), "sent", popcount(m_out),
+                   name=tag + "hop")
+                op("X", None, [KT("hop")], ["sq%d_%d" % (t + 1, c), "dead%d_%d" % (t + 1, c)], ("none",), ar,
+                   popcount(m_in), lat="remote")
+            else:
+                mm("bE1", [([term(e1, "I", kq), term(e1, "nBIG", dead), term(e1, "I", nsq)],
+                            ["I", "nBIG", kqk, KT("dead"), KT("nsq")]),
+                           ([term(e1, "nBIG", hit), term(e1, "nBIG", y3), term(e1, "I", r1e), term(e1, "I", x3)],
+                            four)], tag + "mm_Y")
+                yo = T.ylf[:, i0:i0 + w]
+                if CFG["yl"] == "V":
+                    ts(yo, e1, 0.0, None, ALU.max, None, ["bE1"], [K("ylf")], 64, ["bE1"], tag + "yl")
+                else:
+                    act(yo, e1, AF.Relu, ["bE1"], [K("ylf")], ew(64), ["bE1"], tag + "yl")
+                op("S", lambda: g.sync.dma_start(T.yl[:, i0:i0 + w], yo), [K("ylf")], [], ("dma",), "st", 16,
+                   lat="small")
+            return
         mm("bX", [([term(ex, "one", sq)], ["one", KT("sq")]), ([term(ex, "one", sv)], [K("sv")]),
                   ([term(ex, "none", nsq)], ["none", KT("nsq")])], tag + "mm_x")
         if sgA:

@@ -1,21 +1,22 @@
+import math
+import numpy as np
 from concourse.bass import DstId, RemoteDMATransfer
 from concourse.mybir import AluOpType as ALU, ActivationFunctionType as AF
 
 N, LN, PL = 6, 192, 5
-CH = [64, 64, 64]
-NC = len(CH)
-I0 = [sum(CH[:c]) for c in range(NC)]
 CFG = dict(
-    xv=[[28, 30, 4, 0], [20, 6, 6, 0], [18, 14, 12, 0], [16, 12, 20, 0], [22, 14, 16, 0]],
-    osq=True,
-    sub=[[0, 0, 0, 0]] * 5,
-    fold=True, nosg=True,
+    ch=[64, 64, 64],
+    cut=[["A36V28.", "A34V30.", "A60V4."]] + [["A32.A16V16."] * 3] * 4,
     neg="AVAAAAAA",
-    bb="V", lf="V", of="V", sv="V", sg="V", r1e="V", wipe="V", yl="A", eqf=True, bc="rev")
+    loads=4,
+    off="SSSSS",
+    bb="AAAAA", lf="AAAAA", of="VVVVV", sv="AAAAA", mv="VVVVV", up="AAAAA", wr="AAAAA", yl="A", wipe="V",
+    banks=dict(off="b0", L="b1", ZO="b2", ZL="b3", ST="b4", E1="b5", E2="b6", X="b7", U="b6", W="b5", Y="b7"))
+CH = CFG["ch"]
 BIG = float(2 ** 24)
-MATS = ["I", "nI", "nBIG", "pHUGE", "nIw", "one", "none", "noneI", "kb", "dtie", "tie", "u16", "v16", "nu2k", "v2k",
-        "oneI", "m2", "nm2"]
-BANKS = ["bOF", "bL", "bZO", "bZL", "bST", "bE1", "bE2", "bX"]
+MATS = ["I", "I32", "nBIG", "nHUGE", "one", "none", "oneI", "twoI", "nI32", "kb", "k4", "dtie", "tie", "u16", "v16",
+        "u4k", "v2k"]
+MAXC = 4
 
 SCRATCH = {
     "tab": ("sbuf", [128, 16384], "bfloat16"),
@@ -32,6 +33,11 @@ SCRATCH = {
     "d1": ("sbuf", [128, 128], "int32"),
     "d2": ("sbuf", [128, 128], "int32"),
     "d3": ("sbuf", [128, 128], "int32"),
+    "d4": ("sbuf", [128, 64], "int32"),
+    "d5": ("sbuf", [128, 64], "int32"),
+    "d6": ("sbuf", [128, 64], "float32"),
+    "dgm": ("sbuf", [128, 64], "bfloat16"),
+    "x8": ("sbuf", [128, 64], "bfloat16"),
     "mat": ("sbuf", [128, 128 * len(MATS)], "bfloat16"),
     "idf": ("sbuf", [128, 128], "float32"),
     "idm": ("sbuf", [128, 128], "float32"),
@@ -39,66 +45,80 @@ SCRATCH = {
     "c128": ("sbuf", [128, 8], "bfloat16"),
     "ones": ("sbuf", [128, 64], "bfloat16"),
     "rst": ("sbuf", [128, 128], "float32"),
-    "bci": ("sbuf", [128, 8], "int32"),
-    "bco": ("sbuf", [128, 8], "uint16"),
+    "ramp": ("sbuf", [128, 32], "int32"),
     "ca": ("sbuf", [128, 8 * LN], "float32"),
     "cc": ("sbuf", [128, 8 * LN], "float32"),
-    "lb": ("sbuf", [128, PL * 3 * LN], "bfloat16"),
+    "lb": ("sbuf", [128, PL * 2 * LN], "bfloat16"),
     "s2": ("sbuf", [128, PL * 2 * LN], "bfloat16"),
     "s3": ("sbuf", [128, PL * 2 * LN], "bfloat16"),
     "kq": ("sbuf", [128, PL * LN], "bfloat16"),
     "ylf": ("sbuf", [128, LN], "float32"),
     "ha": ("sbuf", [128, 64 * 16], "bfloat16"),
-    "hb": ("sbuf", [128, 64 * 32], "float16"),
+    "hb": ("sbuf", [128, LN * 32], "float16"),
+    "gb": ("sbuf", [128, LN * 32], "bfloat16"),
+    "rb": ("sbuf", [128, LN * 32], "float16"),
 }
-for _b in BANKS:
-    SCRATCH[_b] = ("psum", [128, 512], "float32")
-for _c in range(NC):
+for _b in range(8):
+    SCRATCH["b%d" % _b] = ("psum", [128, 512], "float32")
+for _c in range(MAXC):
     SCRATCH.update({
-        "gb%d" % _c: ("sbuf", [128, 64 * 32], "bfloat16"),
-        "rb%d" % _c: ("sbuf", [128, 64 * 32], "float16"),
-        "a1%d" % _c: ("sbuf", [128, 64], "float16"),
+        "acc%d" % _c: ("sbuf", [128, 64], "float16"),
         "bb%d" % _c: ("sbuf", [128, 64], "bfloat16"),
+        "dsc%d" % _c: ("sbuf", [128, 64], "float32"),
         "off%d" % _c: ("sbuf", [128, 8], "uint16"),
         "idx%d" % _c: ("sbuf", [128, 128], "uint16"),
         "lf%d" % _c: ("sbuf", [128, 64], "float32"),
         "of%d" % _c: ("sbuf", [128, 64], "float32"),
+        "oh%d" % _c: ("sbuf", [128, 64], "float16"),
         "eq%d" % _c: ("sbuf", [128, 64], "bfloat16"),
         "yp%d" % _c: ("sbuf", [128, 192], "bfloat16"),
         "mx%d" % _c: ("sbuf", [128, 128], "float32"),
         "mf%d" % _c: ("sbuf", [128, 128], "float32"),
         "sv%d" % _c: ("sbuf", [128, 64], "bfloat16"),
-        "sg%d" % _c: ("sbuf", [128, 64], "bfloat16"),
+        "mv%d" % _c: ("sbuf", [128, 64], "bfloat16"),
     })
 
 SEMAPHORES = (["V", "A", "P", "E", "lpos", "lu", "lv", "lstp", "st", "sent"] + ["ltab%d" % h for h in range(4)]
-              + ["kq%d" % t for t in range(1, PL)]
-              + ["ar%d_%d" % (t, c) for t in range(1, PL) for c in range(NC)])
+              + ["hcp%d" % c for c in range(MAXC)] + ["kq%d" % t for t in range(1, PL)]
+              + ["ar%d_%d" % (t, c) for t in range(1, PL) for c in range(MAXC)])
 
-EST = dict(cyc=0.00087, fix=0.02, r=1.3, sc=2.82577, pe=0.00061, hop=0.20057, same=0.2, remote=2.3, issue=0.50005,
-           load0=3.25, load1=4.5, load2=5.75, load3=7, small=2.2, slack=0.15, lag=2.61371)
+EST = dict(cyc=0.00087, fix=0.02, fixa=0.03, r=1.3, sc=2.8, pe=0.00061, hop=0.2, same=0.2, remote=2.3, issue=0.5,
+           load0=2.0, load=5.0, small=2.2, copy=3.2, slack=0.15, lag=2.6)
+SLOW = dict(r=1.6, cyc=0.00095, hop=0.24, same=0.24, remote=2.7, sc=3.5, pe=0.0007, fixa=0.05)
+STEPS = 100000
 
 
 def popcount(m):
     return bin(m).count("1")
 
 
-def cut(a, b, n):
-    e = [a + 2 * ((b - a) // 2 * j // n) for j in range(n)] + [b]
-    return [(e[j], e[j + 1]) for j in range(n) if e[j + 1] > e[j]]
+def pieces(text):
+    out, a, j = [], 0, 0
+    while j < len(text):
+        e, k = text[j], j + 1
+        while k < len(text) and text[k].isdigit():
+            k += 1
+        b = a + int(text[j + 1:k])
+        dot = k < len(text) and text[k] == "."
+        out.append((e, a, b, dot))
+        a, j = b, k + dot
+    return out
 
 
 def build(g, core, T, topo):
     ops, cur = [], [None]
+    CH = CFG["ch"]
+    NC = len(CH)
+    I0 = [sum(CH[:c]) for c in range(NC)]
     rank = T.rank_of(core)
     cores = T.cores
     nxt, prv = cores[(rank + 1) % N], cores[(rank - 1) % N]
     V, A, PE = g.vector, g.scalar, g.tensor
-    sgA = CFG["sg"] == "A"
+    BK = CFG["banks"]
 
     def op(eng, fn, rd, wr, cost, sem=None, inc=1, bank=(), lat=None, name=""):
         ops.append(dict(eng=eng, fn=fn, rd=list(rd), wr=list(wr), cost=cost, sem=sem or eng, inc=inc,
-                        bank=list(bank), lat=lat, name=name, chunk=cur[0]))
+                        bank=list(bank), lat=lat, name=name or (wr[0] if wr else ""), chunk=cur[0]))
 
     def ew(n):
         return ("ew", n)
@@ -121,13 +141,20 @@ def build(g, core, T, topo):
             op("E", fn, rd, [bank], ("pe", sum(x[3] for x in terms)), bank=[bank], name=name + str(p))
 
     def ts(out, in0, s1, s2, o0, o1, rd, wr, n, bank=(), name=""):
+        cost = n if isinstance(n, tuple) else ew(n)
         if o1 is None:
-            op("V", lambda: V.tensor_scalar(out, in0, s1, None, o0), rd, wr, ew(n), bank=bank, name=name)
+            op("V", lambda: V.tensor_scalar(out, in0, s1, None, o0), rd, wr, cost, bank=bank, name=name)
         else:
-            op("V", lambda: V.tensor_scalar(out, in0, s1, s2, o0, o1), rd, wr, ew(n), bank=bank, name=name)
+            op("V", lambda: V.tensor_scalar(out, in0, s1, s2, o0, o1), rd, wr, cost, bank=bank, name=name)
 
     def act(out, in_, fn, rd, wr, cost, bank=(), name="", **kw):
         op("A", lambda: A.activation(out, in_, fn, **kw), rd, wr, cost, bank=bank, name=name)
+
+    def relu(eng, out, in_, bias, rd, wr, n, bank=(), name=""):
+        if eng == "V":
+            ts(out, in_, bias, 0.0, ALU.add, ALU.max, rd, wr, n, bank, name)
+        else:
+            act(out, in_, AF.Relu, rd, wr, ew(n), bank, name, bias=bias)
 
     def ms(ap, val, wr, n, name=""):
         op("V", lambda: V.memset(ap, val), [], wr, ew(n), name=name)
@@ -135,98 +162,101 @@ def build(g, core, T, topo):
     def fill(ap, pat, base, wr, n):
         op("P", lambda: g.iota(ap, pat, base, 0, allow_small_or_imprecise_dtypes=True), [], wr, ("pool", n))
 
-    for h in range(4):
-        op("S", lambda h=h: g.sync.dma_start(T.tab[:, 2048 * h:2048 * (h + 1)], T.feat[:, 2048 * h:2048 * (h + 1)]),
-           [], ["tab%d" % h], ("dma",), "ltab%d" % h, 16, lat="load%d" % h)
+    nl = CFG["loads"]
+    lw = 8192 // nl
+    for h in range(nl):
+        op("S", lambda h=h: g.sync.dma_start(T.tab[:, 8192 + lw * h:8192 + lw * (h + 1)],
+                                             T.feat[:, lw * h:lw * (h + 1)]),
+           [], ["tab%d" % h], ("dma",), "ltab%d" % h, 16, lat=("load", (h + 1) / nl))
     op("A", lambda: A.dma_start(T.posi[:], T.pos[:]), [], ["posi"], ("dma",), "lpos", 16, lat="small")
     op("A", lambda: A.dma_start(T.ub[:], T.u[:]), [], ["ub"], ("dma",), "lu", 16, lat="small")
     op("A", lambda: A.dma_start(T.vb[:], T.v[:]), [], ["vb"], ("dma",), "lv", 16, lat="small")
     op("A", lambda: A.dma_start(T.stp[:, 0:1], T.step[:]), [], ["stp"], ("dma",), "lstp", 16, lat="small")
     for h in range(8):
-        src, dst = T.tab[:, 1024 * h:1024 * (h + 1)], T.tab[:, 8192 + 1024 * h:8192 + 1024 * (h + 1)]
+        src, dst = T.tab[:, 8192 + 1024 * h:8192 + 1024 * (h + 1)], T.tab[:, 1024 * h:1024 * (h + 1)]
+        rd = ["tab%d" % (h * nl // 8)]
         if CFG["neg"][h] == "V":
-            ts(dst, src, -1.0, None, ALU.mult, None, ["tab%d" % (h // 2)], ["neg%d" % h], 512, name="neg")
+            ts(dst, src, -1.0, -32.0, ALU.mult, ALU.add, rd, ["neg%d" % h], 512)
         else:
-            act(dst, src, AF.Identity, ["tab%d" % (h // 2)], ["neg%d" % h], ew(1024), name="neg", scale=-1.0)
-    tabk = ["tab%d" % h for h in range(4)]
+            act(dst, src, AF.Identity, rd, ["neg%d" % h], ew(1024), scale=-1.0, bias=-32.0)
+    tabk = ["tab%d" % h for h in range(nl)]
     negk = ["neg%d" % h for h in range(8)]
 
     op("P", lambda: g.iota(T.d1[:], [[-1, 128]], 0, 1), [], ["d1"], ("pool", 128))
     op("P", lambda: g.iota(T.d2[:], [[-16, 8], [0, 16]], 0, 1), [], ["d2"], ("pool", 128))
     op("P", lambda: g.iota(T.pc[:, 0:1], [[0, 1]], 0, 1), [], ["pc"], ("pool", 1))
-    fill(T.c128[:, 0:4], [[128, 4]], 0, ["c128"], 4)
+    op("P", lambda: g.iota(T.ramp[:], [[-32, 32]], 512, 0), [], ["ramp"], ("pool", 32))
     fill(mat("tie"), [[0, 8], [-1, 16]], 15, ["tie"], 128)
     fill(T.ones[:], [[0, 64]], 1, ["ones"], 64)
-    fill(T.base[:, 0:16], [[0, 16]], 0, ["base0"], 16)
-    fill(T.ha[:], [[0, 1024]], 0, ["ha0", "ha1"], 1024)
+    ms(T.ha[:], 0.0, ["ha"], 512)
     for c in range(NC):
         a, b = 8 * I0[c], 8 * (I0[c] + CH[c])
-        fill(T["yp%d" % c][:], [[0, 192]], 0, ["yp%d" % c], 192)
+        ms(T["yp%d" % c][:], 0.0, ["yp%d" % c], 96)
         fill(T.cc[:, a:b], [[0, b - a]], 0, ["cc%d" % c], b - a)
         fill(T.ca[:, a:b], [[0, b - a]], 0, ["ca%d" % c], b - a)
+    ts(T.hb[:, 0:32], T.ramp[:], 0.0, None, ALU.max, None, ["ramp"], ["hb0"], 64)
+    n = 32
+    while n < 32 * CH[0]:
+        m = min(n, 32 * CH[0] - n)
+        op("V", lambda n=n, m=m: V.tensor_copy(T.hb[:, n:n + m], T.hb[:, 0:m]), ["hb0"], ["hb0"], ew(m // 2))
+        n += m
+    for c in range(1, NC):
+        op("S", lambda c=c: g.sync.dma_start(T.hb[:, 32 * I0[c]:32 * (I0[c] + CH[c])], T.hb[:, 0:32 * CH[c]]),
+           ["hb0", tabk[-1]], ["hb%d" % c], ("dma",), "hcp%d" % c, 16, lat="copy")
 
     c_r8, c_king, c_hit, c_step, c_tie, c_pm, c_t2, c_h2 = (T.col[:, j:j + 1] for j in range(8))
     ts(mat("I"), T.d1[:], 0.0, None, ALU.is_equal, None, ["d1"], ["I"], 128)
     ts(T.idf[:], T.d1[:], 0.0, None, ALU.is_equal, None, ["d1"], ["idf"], 128)
-    ts(c_pm, T.pc[:, 0:1], 64.0, -256.0, ALU.is_ge, ALU.mult, ["pc"], ["c_pm0"], 64)
-    ts(c_t2, c_pm, 128.0, None, ALU.add, None, ["c_pm0"], ["c_pm"], 64)
+    ts(c_pm, T.pc[:, 0:1], 64.0, 128.0, ALU.is_ge, ALU.mult, ["pc"], ["c_pm0"], 64)
+    ts(c_t2, c_pm, -256.0, None, ALU.add, None, ["c_pm0"], ["c_pm"], 64)
     ts(T.idm[:], T.idf[:], c_t2, None, ALU.mult, None, ["idf", "c_pm"], ["idm"], 128)
-    for nm, s in (("nI", -1.0), ("nBIG", -BIG), ("pHUGE", 128 * BIG), ("nIw", -32.0 if sgA else -64.0)):
+    for nm, s in (("I32", 32.0), ("nI32", -32.0), ("nBIG", -BIG), ("nHUGE", -256 * BIG)):
         ts(mat(nm), mat("I"), s, None, ALU.mult, None, ["I"], [nm], 64)
     ts(mat("kb"), T.d2[:], 0.0, 1024.0, ALU.is_equal, ALU.mult, ["d2"], ["kb"], 128)
     ts(T.d3[:], T.d2[:], 4, None, ALU.arith_shift_right, None, ["d2"], ["d3"], 128)
     ts(mat("one"), T.d3[:], 0.0, None, ALU.is_equal, None, ["d3"], ["one"], 128)
-    ts(mat("none"), mat("one"), -1.0, None, ALU.mult, None, ["one"], ["none"], 64)
-    op("V", lambda: V.tensor_tensor(mat("noneI"), mat("none"), mat("I"), ALU.add if CFG["nosg"] else ALU.subtract),
-       ["none", "I"], ["noneI"], ew(256))
+    ts(mat("twoI"), mat("I"), 2.0, None, ALU.mult, None, ["I"], ["twoI"], 64)
     ts(T.rc[:, 0:1], T.pc[:, 0:1], 15, None, ALU.bitwise_and, None, ["pc"], ["rc"], 64)
     ts(c_king, T.rc[:, 0:1], 0.0, None, ALU.is_equal, None, ["rc"], ["c_king"], 64)
-    if CFG["nosg"]:
-        ts(mat("oneI"), mat("noneI"), -1.0, None, ALU.mult, None, ["noneI"], ["oneI"], 64)
-        op("V", lambda: V.tensor_tensor(mat("nm2"), mat("oneI"), mat("I"), ALU.subtract), ["oneI", "I"], ["nm2"],
-           ew(256))
-        ts(mat("m2"), mat("nm2"), -1.0, None, ALU.mult, None, ["nm2"], ["m2"], 64)
-        ts(c_h2, c_king, -1096.0, 64.0, ALU.mult, ALU.add, ["c_king"], ["c_h2"], 64)
+    ts(c_hit, c_king, -1024.0, None, ALU.mult, None, ["c_king"], ["c_hit"], 64)
+    ts(c_h2, c_king, -1096.0, 64.0, ALU.mult, ALU.add, ["c_king"], ["c_h2"], 64)
     ts(T.m16[:], mat("one")[:, 0::16], 16.0, None, ALU.mult, None, ["one"], ["m16"], 64)
-    ts(c_r8, T.rc[:, 0:1], 8.0, -8.4375 if CFG["osq"] else -192.0, ALU.mult, ALU.add, ["rc"], ["c_r8"], 64)
-    ts(c_hit, c_king, -1032.0, 32.0 if sgA else 0.0, ALU.mult, ALU.add, ["c_king"], ["c_hit"], 64)
-    ts(c_tie, T.rc[:, 0:1], 128.0, -1920.0, ALU.mult, ALU.add, ["rc"], ["c_tie"], 64)
-    ts(c_step, T.stp[:, 0:1], c_tie, None, ALU.subtract, None, ["stp", "c_tie"], ["c_step"], 64)
-    ts(T.base[:, 16:144], mat("I"), c_king, 0.125 if CFG["osq"] else 1.0, ALU.mult, ALU.mult, ["I", "c_king"],
-       ["base"], 64)
-    ts(mat("dtie"), mat("I"), c_tie, None, ALU.mult, None, ["I", "c_tie"], ["dtie"], 64)
-    if CFG["bc"] != "rev":
-        op("P", lambda: g.iota(T.bci[:], [[16, 8]], 15, 0), [], ["bci"], ("pool", 8))
-        op("V", lambda: V.tensor_copy(T.bco[:], T.bci[:]), ["bci"], ["bco"], ew(64))
+    ts(c_tie, T.rc[:, 0:1], -128.0, 1920.0, ALU.mult, ALU.add, ["rc"], ["c_tie"], 64)
+    ts(c_step, T.stp[:, 0:1], c_tie, None, ALU.add, None, ["stp", "c_tie"], ["c_step"], 64)
+    ts(mat("dtie"), mat("I"), c_tie, 2.0, ALU.mult, ALU.mult, ["I", "c_tie"], ["dtie"], 64)
+    if "E" in CFG["off"]:
+        fill(T.c128[:, 0:4], [[128, 4]], 0, ["c128"], 4)
+        fill(T.base[:, 0:16], [[0, 16]], 0, ["base0"], 16)
+        ts(c_r8, T.rc[:, 0:1], 8.0, None, ALU.mult, None, ["rc"], ["c_r8"], 64)
+        ts(T.base[:, 16:144], mat("I"), c_king, 4.0, ALU.mult, ALU.mult, ["I", "c_king"], ["base"], 64)
+    if "S" in CFG["off"]:
+        op("P", lambda: g.iota(T.d4[:], [[-1, 64]], 64, 1), [], ["d4"], ("pool", 64))
+        fill(T.x8[:], [[8, 64]], 0, ["x8"], 64)
+        ts(T.d5[:], T.d4[:], 15, None, ALU.bitwise_and, None, ["d4"], ["d5"], 64)
+        ts(T.d6[:], T.d5[:], 0.0, -4096.0, ALU.not_equal, ALU.mult, ["d5"], ["d6"], 64)
+        op("V", lambda: V.tensor_tensor(T.dgm[:], T.d6[:], T.x8[:], ALU.add), ["d6", "x8"], ["dgm"], ew(128))
+        ts(mat("k4"), mat("kb"), 1.0 / 256, None, ALU.mult, None, ["kb"], ["k4"], 64)
     ms(T.rst[:], 0.0, ["rst"], 128)
     ms(T.rst[:, 0::16], -float(2 ** 26), ["rst"], 64)
-    ms(T.hb[:], 0.0, ["hb0", "hb1"], 1024)
     for gq in range(8):
         for nm, src, key in (("u16", T.ub, "ub"), ("v16", T.vb, "vb")):
             act(matc(nm, 16 * gq, 16 * gq + 16), src[:], AF.Identity, [key, "m16"], ["%s_%d" % (nm, gq)], ew(64),
                 scale=T.m16[:, gq:gq + 1])
     uk, vk = (["%s_%d" % (nm, gq) for gq in range(8)] for nm in ("u16", "v16"))
-    ts(mat("nu2k"), mat("u16"), -128.0, None, ALU.mult, None, uk, ["nu2k"], 64)
+    ts(mat("u4k"), mat("u16"), 256.0, None, ALU.mult, None, uk, ["u4k"], 64)
     ts(mat("v2k"), mat("v16"), 128.0, None, ALU.mult, None, vk, ["v2k"], 64)
 
-    def lbv(t, c):
-        w, b = CH[c], 3 * (t * LN + I0[c])
-        x, y, z = T.lb[:, b:b + w], T.lb[:, b + w:b + 2 * w], T.lb[:, b + 2 * w:b + 3 * w]
-        lo, hi = T.lb[:, b:b + 2 * w], T.lb[:, b + w:b + 3 * w]
-        return (z, y, x, hi, lo) if t % 2 == 0 else (x, y, z, lo, hi)
-
-    def s2v(t, c, buf=T.s2):
+    def halves(buf, t, c):
         w, b = CH[c], 2 * (t * LN + I0[c])
-        x, y = buf[:, b:b + w], buf[:, b + w:b + 2 * w]
-        return (x, y, buf[:, b:b + 2 * w]) if t % 2 == 0 else (y, x, buf[:, b:b + 2 * w])
+        return buf[:, b:b + w], buf[:, b + w:b + 2 * w], buf[:, b:b + 2 * w]
 
     ts(T.sqi[:], T.posi[:], 63, None, ALU.bitwise_and, None, ["posi"], ["sqi"], LN)
     ts(T.kqi[:], T.posi[:], 960, None, ALU.bitwise_and, None, ["posi"], ["kqi"], LN)
-    ts(T.kq[:, 0:LN], T.kqi[:], -64.0, None, ALU.add, None, ["kqi"], ["kq0"], LN)
+    op("V", lambda: V.tensor_copy(T.kq[:, 0:LN], T.kqi[:]), ["kqi"], ["kq0"], ew(LN))
     for c in range(NC):
-        sq, dead = lbv(0, c)[0:2]
+        q, dead = halves(T.lb, 0, c)[0:2]
         a, b = I0[c], I0[c] + CH[c]
-        ts(sq, T.sqi[:, a:b], 64.0, None, ALU.add, None, ["sqi"], ["sq0_%d" % c], 64)
+        ts(q, T.sqi[:, a:b], 64.0, 1.0 / 32, ALU.add, ALU.mult, ["sqi"], ["sq0_%d" % c], 64)
         ts(dead, T.posi[:, a:b], 64.0, None, ALU.is_lt, None, ["posi"], ["dead0_%d" % c], 64)
 
     def kq_masks(src):
@@ -262,216 +292,175 @@ def build(g, core, T, topo):
         B = lambda s: T["%s%d" % (s, c)]
         K = lambda s: "%s%d" % (s, c)
         KT = lambda s: "%s%d_%d" % (s, t, c)
-        sq, dead, nsq, _, sent = lbv(t, c)
-        r1e, hit, src2 = s2v(t, c)
+        E = lambda s: CFG[s][t]
+        o = 64.0 + 32 * CFG["wr"][:t].count("A")
+        q, dead, sent = halves(T.lb, t, c)
+        up, hit, src2 = halves(T.s2, t, c)
+        wr, hit2, src3 = halves(T.s3, t, c)
         kq = T.kq[:, t * LN + i0:t * LN + i0 + w]
         kqk = "kq%d" % t
         bb, off, idx = B("bb")[:, 0:w], B("off")[:, 0:k], B("idx")
-        lf, of, eq = B("lf")[:, 0:w], B("of")[:, 0:w], B("eq")[:, 0:w]
-        sv, sg, y = B("sv")[:, 0:w], B("sg")[:, 0:w], B("yp")[:, 64:64 + w]
+        lf, eq = B("lf")[:, 0:w], B("eq")[:, 0:w]
+        sv, mv, y = B("sv")[:, 0:w], B("mv")[:, 0:w], B("yp")[:, 64:64 + w]
         ca, cc = T.ca[:, 8 * i0:8 * (i0 + w)], T.cc[:, 8 * i0:8 * (i0 + w)]
         ones = T.ones[:, 0:w]
         tag = "%d.%d " % (t, c)
-        term = lambda o, m, r: (o, mat(m), r, 64)
+        term = lambda out, m, r: (out, mat(m), r, 64)
+        ps = lambda s, n=w: T[BK[s]][:, 0:n]
 
-        if CFG["bb"] == "V":
-            ts(bb, sq, 0.125, 183.5625, ALU.mult, ALU.add, [KT("sq")], [K("bb")], 64, name=tag + "bb")
+        if E("off") == "E":
+            po = ps("off", k)
+            mm(BK["off"], [([(po, mat("I"), T.c128[:, 0:k], 64)], ["I", "c128"]),
+                           ([(po, T.base[:, 16 - r:144 - r], q[:, r:w:16], 64) for r in range(16)],
+                            ["base", "base0", KT("sq")])], tag + "mm_off")
+            ts(off, po, c_r8, -o / 8 - 0.4375, ALU.add, ALU.add, [BK["off"], "c_r8"], [K("off")], 64, [BK["off"]],
+               tag + "off")
         else:
-            act(bb, sq, AF.Identity, [KT("sq")], [K("bb")], ew(64), name=tag + "bb", scale=0.125, bias=183.5625)
-        po = T.bOF[:, 0:k]
-        mm("bOF", [([(po, mat("I"), T.c128[:, 0:k], 64)], ["I", "c128"]),
-                   ([(po, T.base[:, 16 - r:144 - r], (sq if CFG["osq"] else bb)[:, r:w:16], 64) for r in range(16)],
-                    ["base", "base0", KT("sq") if CFG["osq"] else K("bb")])], tag + "mm_off")
-        ts(off, po, c_r8, None, ALU.add, None, ["bOF", "c_r8"], [K("off")], 64, ["bOF"], tag + "off")
-        lsum = lambda o: [term(o, "I", kq), term(o, "I", sq), term(o, "nBIG", dead)]
-        lk = ["I", "nBIG", KT("sq"), KT("dead"), kqk]
-        pl, zo, zl = T.bL[:, 0:w], T.bZO[:, 0:w], T.bZL[:, 0:w]
-        mm("bL", [(lsum(pl), lk)], tag + "mm_L")
-        if CFG["lf"] == "V":
-            ts(lf, pl, 0.0, None, ALU.max, None, ["bL"], [K("lf")], 64, ["bL"], tag + "lf")
+            po, dsc = ps("off"), B("dsc")
+            mm(BK["off"], [([term(po, "I", T.dgm[:, 0:w])], ["I", "dgm"]),
+                           ([term(po, "k4", q)], ["k4", KT("sq")])], tag + "mm_off")
+            op("V", lambda: V.tensor_tensor_scan(dsc[:, 0:w], T.rst[:, 0:w], po, 0.0, ALU.add, ALU.max),
+               ["rst", BK["off"]], [K("dsc")], ew(w), bank=[BK["off"]], name=tag + "dsc")
+            ts(off, dsc[:, 15:w:16], -o / 8 - 0.4375, None, ALU.add, None, [K("dsc")], [K("off")], 64,
+               name=tag + "off")
+        if E("bb") == "V":
+            ts(bb, q, 4.0, 191.5625 - o / 8, ALU.mult, ALU.add, [KT("sq")], [K("bb")], 64, name=tag + "bb")
         else:
-            act(lf, pl, AF.Relu, ["bL"], [K("lf")], ew(64), ["bL"], tag + "lf")
+            act(bb, q, AF.Identity, [KT("sq")], [K("bb")], ew(64), name=tag + "bb", scale=4.0, bias=191.5625 - o / 8)
+        lsum = lambda out: [term(out, "I", kq), term(out, "I32", q), term(out, "nBIG", dead)]
+        lk = ["I", "I32", "nBIG", KT("sq"), KT("dead"), kqk]
+        pl, zo, zl = ps("L"), ps("ZO"), ps("ZL")
+        mm(BK["L"], [(lsum(pl), lk)], tag + "mm_L")
+        relu(E("lf"), lf, pl, -o, [BK["L"]], [K("lf")], w, [BK["L"]], tag + "lf")
         zpre = [(lsum(zl), lk), ([term(zl, "kb", bb)], ["kb", K("bb")])]
         if t > 0:
-            if CFG["of"] == "V":
+            if E("of") == "V":
+                of = B("oh")[:, 0:w]
                 op("V", lambda: V.tensor_copy(of, cc.indirect(off)), [K("cc"), K("off")], [K("of")], ("gV", w),
                    name=tag + "of")
+                oterm = ([term(zo, "I", of)], ["I", K("of")])
             else:
+                of = B("of")[:, 0:w]
                 act(of, cc.indirect(off), AF.Identity, [K("cc"), K("off")], [K("of")], ("gA", w), name=tag + "of")
-            if CFG["eqf"]:
-                op("V", lambda: V.tensor_tensor(eq, cc.indirect(off), lf, ALU.is_equal),
-                   [K("cc"), K("off"), K("lf")], [K("eq")], ("gV", w), name=tag + "eq")
-            else:
-                op("V", lambda: V.tensor_tensor(eq, of, pl, ALU.is_equal), [K("of"), "bL"], [K("eq")], ew(64),
-                   bank=["bL"], name=tag + "eq")
-            mm("bZO", [([term(zo, "kb", bb)], ["kb", K("bb")]), ([(zo, T.idf[:], of, 256)], ["idf", K("of")]),
-                       ([term(zo, "nBIG", eq)], ["nBIG", K("eq")])], tag + "mm_ZO")
-            mm("bZL", zpre + [([term(zl, "nBIG", eq)], ["nBIG", K("eq")])], tag + "mm_ZL")
-            ts(idx[:, 1:2 * w:2], zl, -196608.0, 0.0, ALU.add, ALU.max, ["bZL"], [K("idy")], 64, ["bZL"],
-               tag + "idxL")
-            ts(idx[:, 0:2 * w:2], zo, 8192.0 - 196608.0, 0.0, ALU.add, ALU.max, ["bZO"], [K("idx")], 64, ["bZO"],
+                oterm = ([(zo, T.idf[:], of, 256)], ["idf", K("of")])
+            op("V", lambda: V.tensor_tensor(eq, cc.indirect(off), lf, ALU.is_equal),
+               [K("cc"), K("off"), K("lf")], [K("eq")], ("gV", w), name=tag + "eq")
+            mm(BK["ZO"], [([term(zo, "kb", bb)], ["kb", K("bb")]), oterm,
+                          ([term(zo, "nBIG", eq)], ["nBIG", K("eq")])], tag + "mm_ZO")
+            mm(BK["ZL"], zpre + [([term(zl, "nBIG", eq)], ["nBIG", K("eq")])], tag + "mm_ZL")
+            ts(idx[:, 0:2 * w:2], zo, -196608.0, 0.0, ALU.add, ALU.max, [BK["ZO"]], [K("idx")], w, [BK["ZO"]],
                tag + "idxO")
-            m, H, hk, xv, win, wk = 2, T.hb, "hb", CFG["xv"][t][c], T.tab[:], tabk + negk + [K("idx"), K("idy")]
+            ts(idx[:, 1:2 * w:2], zl, 8192.0 - 196608.0 - o, 8192.0, ALU.add, ALU.max, [BK["ZL"]], [K("idy")], w,
+               [BK["ZL"]], tag + "idxL")
+            m, win, wk = 2, T.tab[:], tabk + negk + [K("idx"), K("idy")]
         else:
-            mm("bZL", zpre, tag + "mm_ZL")
-            ts(idx[:, 0:w], zl, -196608.0, 0.0, ALU.add, ALU.max, ["bZL"], [K("idx"), K("idy")], w, ["bZL"],
-               tag + "idx")
-            m, H, hk, xv, win, wk = 1, T.ha, "ha", CFG["xv"][0][c], T.tab[:, 0:8192], tabk + [K("idx"), K("idy")]
-        xa, sl = w - xv, 16 * m
-        G, R = B("gb"), B("rb")
-        rk = [K("r0_"), K("r1_")]
-        two = t > 0 and w > 32 and CFG["sub"][t][c]
-        for j, (a, b) in enumerate([(0, 32), (32, w)] if two else [(0, w)]):
-            hs = [j] if two else [0, 1]
-            ka, kv = ([K("g%d%s_" % (h, q)) for h in hs] for q in "AV")
-            x = max(a, min(b, xa))
-            if x > a:
-                act(G[:, sl * a:sl * x], win.indirect(idx[:, m * a:m * x]), AF.Identity, wk,
-                    ka, ("gA", sl * (x - a)), name=tag + "gA")
-            if b > x:
-                op("V", lambda x=x, b=b: V.tensor_copy(G[:, sl * x:sl * b], win.indirect(idx[:, m * x:m * b])),
-                   wk, kv, ("gV", sl * (b - x)), name=tag + "gV")
-        for j, (a, b) in enumerate([(0, 32), (32, w)] if two else [(0, w)]):
-            hs = [j] if two else [0, 1]
-            gk = [K("g%d%s_" % (h, q)) for h in hs for q in "AV"]
-            hh = [hk + str(h) for h in hs]
-            g0, h0 = G[:, sl * a:sl * b:sl], H[:, sl * a:sl * b:sl]
-            if t > 0:
-                a1, ak = B("a1")[:, a:b], [K("a%d_" % h) for h in hs]
-                op("V", lambda a1=a1, g0=g0, a=a, b=b: V.tensor_tensor(
-                    a1, ca.indirect(B("off")[:, a // 16:b // 16]), g0, ALU.add), [K("ca"), K("off")] + gk, ak,
-                   ("gV", b - a), name=tag + "a1")
-                ts(h0, a1, 0.0, None, ALU.max, None, ak, hh, 64, name=tag + "h0")
+            mm(BK["ZL"], zpre, tag + "mm_ZL")
+            ts(idx[:, 0:w], zl, -196608.0 - o, 0.0, ALU.add, ALU.max, [BK["ZL"]], [K("idx"), K("idy")], w,
+               [BK["ZL"]], tag + "idx")
+            m, win, wk = 1, T.tab[:, 8192:16384], tabk + [K("idx"), K("idy")]
+        sl = 16 * m
+        G, R = T.gb[:, 32 * i0:32 * (i0 + w)], T.rb[:, 32 * i0:32 * (i0 + w)]
+        H = T.hb[:, 32 * i0:32 * (i0 + w)] if t else T.ha
+        keys = lambda s, a, b: ["%s%d_%d" % (s, c, j) for j in range(sl * a // 32, (sl * b + 31) // 32)]
+        if t > 0:
+            ts(H[:, 0:32 * w:32], ca.indirect(off), 0.0, 512.0, ALU.max, ALU.add, [K("ca"), K("off")], [K("hb")],
+               ("gV", w), name=tag + "a0")
+        a0 = 0
+        for e, a, b, dot in pieces(CFG["cut"][t][c]):
+            if e == "A":
+                act(G[:, sl * a:sl * b], win.indirect(idx[:, m * a:m * b]), AF.Identity, wk, keys("g", a, b),
+                    ("gA", sl * (b - a)), name=tag + "gA")
             else:
-                ts(h0, g0, 0.0, None, ALU.max, None, gk, hh, 64, name=tag + "h0")
-            ms(g0, -1024.0, gk, 64, tag + "wipe")
-            op("V", lambda a=a, b=b: V.tensor_tensor_scan(R[:, sl * a:sl * b], G[:, sl * a:sl * b],
-                                                          H[:, sl * a:sl * b], 0.0, ALU.add, ALU.max),
-               gk + hh, [rk[h] for h in hs], ew((b - a) * sl // 2), name=tag + "scan")
+                op("V", lambda a=a, b=b: V.tensor_copy(G[:, sl * a:sl * b], win.indirect(idx[:, m * a:m * b])),
+                   wk, keys("g", a, b), ("gV", sl * (b - a)), name=tag + "gV")
+            if not dot:
+                continue
+            a, gk = a0, keys("g", a0, b)
+            a0 = b
+            if t == 0:
+                g0, hk = G[:, sl * a:sl * b:sl], ["ha"] + ["ha_%d" % j for j in range(a, b)]
+                ts(H[:, sl * a:sl * b:sl], g0, 0.0, None, ALU.max, None, gk + hk[:1], hk[1:], 64, name=tag + "h0")
+                if CFG["wipe"] == "V":
+                    ms(g0, -1024.0, gk, 64, tag + "wipe")
+                else:
+                    act(g0, T.ones[:, 0:b - a], AF.Identity, ["ones"], gk, ew(64), name=tag + "wipe", scale=-1024.0)
+                d0, d1, o0, o1 = G, H, ALU.add, ALU.max
+            else:
+                hk, d0, d1, o0, o1 = [K("hb")], H, G, ALU.max, ALU.add
+            op("V", lambda a=a, b=b, d0=d0, d1=d1, o0=o0, o1=o1: V.tensor_tensor_scan(
+                R[:, sl * a:sl * b], d0[:, sl * a:sl * b], d1[:, sl * a:sl * b], 0.0, o0, o1),
+               gk + hk, keys("r", a, b), ew((b - a) * sl // 2), name=tag + "scan")
+        rk = keys("r", 0, w)
         acc = R[:, sl - 1:sl * w:sl]
-        ts(y, acc, 127.0, None, ALU.min, None, rk, [K("yp")], 64, name=tag + "y")
+        ts(y, acc, 0.0, 127.0, ALU.max, ALU.min, rk, [K("yp")], 64, name=tag + "y")
         op("V", lambda: V.tensor_copy(cc.indirect(off), lf), [K("lf"), K("off")], [K("cc")], ("sV", w),
            name=tag + "scL")
+        if t == PL - 1:
+            act(ca, ca, AF.Relu, [K("ca")], [K("ca")], ew(8 * w), name=tag + "clamp")
+            ts(B("acc")[:, 0:w], acc, 0.0, None, ALU.max, None, rk, [K("acc")], 64, name=tag + "acc")
+            acc, rk = B("acc")[:, 0:w], [K("acc")]
         op("V", lambda: V.tensor_copy(ca.indirect(off), acc), rk + [K("off")], [K("ca")], ("sV", w),
            name=tag + "scA")
         if t == PL - 1:
             op("S", lambda: g.sync.dma_start(T.yc[:, 8 * i0:8 * (i0 + w)], cc), [K("cc")], [], ("dma",), "st", 16,
-               lat="small")
+               lat="copy")
             op("S", lambda: g.sync.dma_start(T.ya[:, 8 * i0:8 * (i0 + w)], ca), [K("ca")], [], ("dma",), "st", 16,
-               lat="small")
-        st, mx, mf = T.bST[:, 0:128], B("mx"), B("mf")
-        mm("bST", [([(st, mat("I"), mat("tie"), 128), (T.bST[0:w, 0:128], dead, mat("nBIG"), 128)],
-                    ["I", "tie", "nBIG", KT("dead")]),
-                   ([(st, B("yp")[:, 64:192], mat("u16"), 128), (st, B("yp")[:, 0:128], mat("v16"), 128)],
-                    [K("yp")] + uk + vk)], tag + "mm_S")
-        op("V", lambda: V.tensor_tensor_scan(mx[:], T.rst[:], st, 0.0, ALU.add, ALU.max), ["rst", "bST"],
-           [K("mx")], ew(128), bank=["bST"], name=tag + "max")
-        if CFG["bc"] == "rev":
-            op("V", lambda: V.tensor_tensor_scan(mf[:, ::-1], T.rst[:], mx[:, ::-1], 0.0, ALU.add, ALU.max),
-               ["rst", K("mx")], [K("mf")], ew(128), name=tag + "mf")
-        elif CFG["bc"] == "gV":
-            op("V", lambda: V.tensor_copy(mf[:], mx[:].indirect(T.bco[:])), ["bco", K("mx")], [K("mf")],
-               ("gV", 128), name=tag + "mf")
+               lat="copy")
+        st, mx, mf = ps("ST", 128), B("mx"), B("mf")
+        mm(BK["ST"], [([(st, mat("I"), mat("tie"), 128), (T[BK["ST"]][0:w, 0:128], dead, mat("nBIG"), 128)],
+                       ["I", "tie", "nBIG", KT("dead")]),
+                      ([(st, B("yp")[:, 64:192], mat("u16"), 128), (st, B("yp")[:, 0:128], mat("v16"), 128)],
+                       [K("yp")] + uk + vk)], tag + "mm_S")
+        op("V", lambda: V.tensor_tensor_scan(mx[:], T.rst[:], st, 0.0, ALU.add, ALU.max), ["rst", BK["ST"]],
+           [K("mx")], ew(128), bank=[BK["ST"]], name=tag + "max")
+        op("V", lambda: V.tensor_tensor_scan(mf[:, ::-1], T.rst[:], mx[:, ::-1], 0.0, ALU.add, ALU.max),
+           ["rst", K("mx")], [K("mf")], ew(128), name=tag + "mf")
+        e1, e2 = ps("E1"), ps("E2")
+        mm(BK["E1"], [([term(e1, "dtie", ones), term(e1, "nHUGE", dead)], ["dtie", "ones", "nHUGE", KT("dead")]),
+                      ([term(e1, "u4k", y)], ["u4k", K("yp")]),
+                      ([(e1, mf[:], T.idm[:, 0:w], 256), term(e1, "I32", q)], ["idm", K("mf"), "I32", KT("sq")])],
+           tag + "mm_E1")
+        mm(BK["E2"], [([term(e2, "v2k", y)], ["v2k", K("yp")]),
+                      ([(e2, mf[:], T.idm[:, 64:64 + w], 256)], ["idm", K("mf")])], tag + "mm_E2")
+        relu(E("mv"), mv, e1, 0.0, [BK["E1"]], [K("mv")], w, [BK["E1"]], tag + "mv")
+        relu(E("sv"), sv, e2, c_step, [BK["E2"], "c_step"], [K("sv")], w, [BK["E2"]], tag + "sv")
+        ex, zu, zw = ps("X"), ps("U"), ps("W")
+        for out, bank, m1 in ((ex, "X", "one"), (zu, "U", "I"), (zw, "W", "twoI")):
+            mm(BK[bank], [([term(out, "nI32", q)], ["nI32", KT("sq")]),
+                          ([term(out, m1, mv)], [m1, K("mv")]),
+                          ([term(out, "one", sv)], ["one", K("sv")])], tag + "mm_" + bank)
+        ts(hit, ex, c_hit, None, ALU.is_equal, None, [BK["X"], "c_hit"], [KT("hit")], w, [BK["X"]], tag + "h1")
+        ts(hit2, ex, c_h2, None, ALU.is_equal, None, [BK["X"], "c_h2"], [KT("hit2")], w, [BK["X"]], tag + "h2")
+        if E("up") == "V":
+            ts(up, zu, 1.0 / 32, 0.0, ALU.mult, ALU.max, [BK["U"]], [KT("up")], w, [BK["U"]], tag + "up")
         else:
-            act(mf[:], mx[:].indirect(T.bco[:]), AF.Identity, ["bco", K("mx")], [K("mf")], ("gA", 128),
-                name=tag + "mf")
-        e1, e2, ex = T.bE1[:, 0:w], T.bE2[:, 0:w], T.bX[:, 0:w]
-        mm("bE2", [([term(e2, "v2k", y)], ["v2k", K("yp")]),
-                   ([(e2, mf[:], T.idm[:, 64:64 + w], 256)], ["idm", K("mf")])], tag + "mm_E2")
-        mm("bE1", [([term(e1, "dtie", ones), term(e1, "pHUGE", dead)], ["dtie", "ones", "pHUGE", KT("dead")]),
-                   ([term(e1, "nu2k", y)], ["nu2k", K("yp")]),
-                   ([(e1, mf[:], T.idm[:, 0:w], 256)], ["idm", K("mf")])], tag + "mm_E1")
-        if CFG["sv"] == "V":
-            ts(sv, e2, c_step, 0.0, ALU.add, ALU.max, ["bE2", "c_step"], [K("sv")], 64, ["bE2"], tag + "sv")
+            act(up, zu, AF.Relu, [BK["U"]], [KT("up")], ew(w), [BK["U"]], tag + "up", scale=1.0 / 32)
+        if E("wr") == "V":
+            ts(wr, zw, 64.0 + o, -2.0, ALU.is_ge, ALU.mult, [BK["W"]], [KT("wrap")], w, [BK["W"]], tag + "wrap")
         else:
-            act(sv, e2, AF.Relu, ["bE2", "c_step"], [K("sv")], ew(64), ["bE2"], tag + "sv", bias=c_step)
-        op("V", lambda: V.tensor_tensor(nsq, e1, sq, ALU.min), ["bE1", KT("sq")], [KT("nsq")], ew(64),
-           bank=["bE1"], name=tag + "nsq")
-        if CFG["nosg"]:
-            x3, y3, src3 = s2v(t, c, T.s3)
-            mm("bX", [([term(ex, "oneI", sq)], ["oneI", KT("sq")]), ([term(ex, "one", sv)], ["one", K("sv")]),
-                      ([term(ex, "none", nsq)], ["none", KT("nsq")])], tag + "mm_x")
-            mm("bE2", [([term(e2, "m2", sq), term(e2, "one", sv)], ["m2", "one", KT("sq"), K("sv")]),
-                       ([term(e2, "nm2", nsq)], ["nm2", KT("nsq")])], tag + "mm_z")
-            ts(hit, ex, c_hit, None, ALU.is_equal, None, ["bX", "c_hit"], [KT("hit")], 64, ["bX"], tag + "h1")
-            ts(y3, ex, c_h2, None, ALU.is_equal, None, ["bX", "c_h2"], [KT("hit2")], 64, ["bX"], tag + "h2")
-            ts(r1e, e2, 0.0, None, ALU.max, None, ["bE2"], [KT("r1e")], 64, ["bE2"], tag + "up")
-            ts(x3, e2, 128.0, -64.0, ALU.is_ge, ALU.mult, ["bE2"], [KT("wrap")], 64, ["bE2"], tag + "wrap")
-            four = [KT("hit"), KT("hit2"), KT("r1e"), KT("wrap")]
-            if t < PL - 1:
-                land = lbv(t + 1, c)[3]
-                ar = "ar%d_%d" % (t + 1, c)
-
-                def hop3():
-                    g.remote_dma_fused([RemoteDMATransfer(
-                        dst_ids=[DstId(rid=rid_n, pnc=pid_n)], dma_engine_mask=m_out, remote_sem=T.sem[ar],
-                        srcs=[sent, src2, src3], dsts=[land], alu_op=1)], local_sem=T.sem.sent)
-                    return None
-                op("P", hop3, [KT("nsq"), KT("dead")] + four, [KT("hop")], ("remote", 1), "sent", popcount(m_out),
-                   name=tag + "hop")
-                op("X", None, [KT("hop")], ["sq%d_%d" % (t + 1, c), "dead%d_%d" % (t + 1, c)], ("none",), ar,
-                   popcount(m_in), lat="remote")
-            else:
-                mm("bE1", [([term(e1, "I", kq), term(e1, "nBIG", dead), term(e1, "I", nsq)],
-                            ["I", "nBIG", kqk, KT("dead"), KT("nsq")]),
-                           ([term(e1, "nBIG", hit), term(e1, "nBIG", y3), term(e1, "I", r1e), term(e1, "I", x3)],
-                            four)], tag + "mm_Y")
-                yo = T.ylf[:, i0:i0 + w]
-                if CFG["yl"] == "V":
-                    ts(yo, e1, 0.0, None, ALU.max, None, ["bE1"], [K("ylf")], 64, ["bE1"], tag + "yl")
-                else:
-                    act(yo, e1, AF.Relu, ["bE1"], [K("ylf")], ew(64), ["bE1"], tag + "yl")
-                op("S", lambda: g.sync.dma_start(T.yl[:, i0:i0 + w], yo), [K("ylf")], [], ("dma",), "st", 16,
-                   lat="small")
-            return
-        mm("bX", [([term(ex, "one", sq)], ["one", KT("sq")]), ([term(ex, "one", sv)], [K("sv")]),
-                  ([term(ex, "none", nsq)], ["none", KT("nsq")])], tag + "mm_x")
-        if sgA:
-            act(sg, ex, AF.Sign, ["bX"], [K("sg")], ew(64), ["bX"], tag + "sg", bias=-127.5)
-        else:
-            ts(sg, ex, 128.0, None, ALU.is_ge, None, ["bX"], [K("sg")], 64, ["bX"], tag + "sg")
-        pk = ["I", "nI", "one", "noneI", "nIw", "ones", KT("sq"), KT("nsq"), K("sv")]
-        mm("bE1", [([term(e1, "one", sq), term(e1, "noneI", nsq), term(e1, "one", sv)], pk),
-                   ([term(e1, "nIw", sg)], [K("sg")])], tag + "mm_R2")
-        mm("bE2", [([term(e2, "I", sq), term(e2, "nI", nsq), term(e2, "one", sv)]
-                    + ([term(e2, "nIw", ones)] if sgA else []), pk),
-                   ([term(e2, "nIw", sg)], [K("sg")])], tag + "mm_R1")
-        plain = t < PL - 1 and not CFG["fold"]
-        if plain:
-            ts(eq, e1, c_hit, None, ALU.is_equal, None, ["bE1", "c_hit"], [K("eq")], 64, ["bE1"], tag + "hit")
-            op("V", lambda: V.tensor_tensor(hit, eq, dead, ALU.max), [K("eq"), KT("dead")], [KT("hit")], ew(128),
-               name=tag + "gone")
-        else:
-            ts(hit, e1, c_hit, None, ALU.is_equal, None, ["bE1", "c_hit"], [KT("hit")], 64, ["bE1"], tag + "hit")
-        if CFG["r1e"] == "V" or t == PL - 1 or plain:
-            op("V", lambda: V.tensor_tensor(r1e, e2, nsq, ALU.max), ["bE2", KT("nsq")], [KT("r1e")], ew(64),
-               bank=["bE2"], name=tag + "r1e")
-        else:
-            act(r1e, e2, AF.Identity, ["bE2"], [KT("r1e")], ew(64), ["bE2"], tag + "r1e")
+            act(wr, zw, AF.Sign, [BK["W"]], [KT("wrap")], ew(w), [BK["W"]], tag + "wrap", scale=-1.0, bias=63.5 + o)
+        four = [KT("hit"), KT("hit2"), KT("up"), KT("wrap")]
         if t < PL - 1:
-            land = lbv(t + 1, c)[3]
+            land = halves(T.lb, t + 1, c)[2]
             ar = "ar%d_%d" % (t + 1, c)
 
             def hop():
-                if plain:
-                    g.remote_dma(land, src2, T.sem[ar], T.sem.sent, pid_n, rid_n, m_out)
-                    return None
-                g.remote_dma_fused([RemoteDMATransfer(dst_ids=[DstId(rid=rid_n, pnc=pid_n)], dma_engine_mask=m_out,
-                                                      remote_sem=T.sem[ar], srcs=[sent, src2], dsts=[land],
-                                                      alu_op=2)], local_sem=T.sem.sent)
+                g.remote_dma_fused([RemoteDMATransfer(
+                    dst_ids=[DstId(rid=rid_n, pnc=pid_n)], dma_engine_mask=m_out, remote_sem=T.sem[ar],
+                    srcs=[sent, src2, src3], dsts=[land], alu_op=1)], local_sem=T.sem.sent)
                 return None
-            op("P", hop, [KT("nsq"), KT("dead"), KT("r1e"), KT("hit")], [KT("hop")], ("remote", 1), "sent",
-               popcount(m_out), name=tag + "hop")
+            op("P", hop, [KT("sq"), KT("dead")] + four, [KT("hop")], ("remote", 1), "sent", popcount(m_out),
+               name=tag + "hop")
             op("X", None, [KT("hop")], ["sq%d_%d" % (t + 1, c), "dead%d_%d" % (t + 1, c)], ("none",), ar,
                popcount(m_in), lat="remote")
         else:
-            mm("bX", [([term(ex, "I", kq), term(ex, "nBIG", dead)], ["I", "nBIG", kqk, KT("dead")]),
-                      ([term(ex, "nBIG", hit), term(ex, "I", r1e)], [KT("hit"), KT("r1e")])], tag + "mm_Y")
+            ey = ps("Y")
+            mm(BK["Y"], [(lsum(ey), lk),
+                         ([term(ey, "nBIG", hit), term(ey, "nBIG", hit2), term(ey, "I32", up), term(ey, "I32", wr)],
+                          four)], tag + "mm_Y")
             yo = T.ylf[:, i0:i0 + w]
-            if CFG["yl"] == "V":
-                ts(yo, ex, 0.0, None, ALU.max, None, ["bX"], [K("ylf")], 64, ["bX"], tag + "yl")
-            else:
-                act(yo, ex, AF.Relu, ["bX"], [K("ylf")], ew(64), ["bX"], tag + "yl")
+            relu(CFG["yl"], yo, ey, -o - (32.0 if E("wr") == "A" else 0.0), [BK["Y"]], [K("ylf")], w, [BK["Y"]],
+                 tag + "yl")
             op("S", lambda: g.sync.dma_start(T.yl[:, i0:i0 + w], yo), [K("ylf")], [], ("dma",), "st", 16,
                lat="small")
 
@@ -510,7 +499,7 @@ def find_deps(ops):
 def busy(o, e):
     c = o["cost"]
     if c[0] == "ew":
-        return e["fix"] + max(64, c[1]) * e["cyc"]
+        return e["fixa" if o["eng"] == "A" else "fix"] + max(64, c[1]) * e["cyc"]
     if c[0] == "gV":
         return 0.05 + c[1] * e["r"] * e["cyc"]
     if c[0] == "gA":
@@ -528,16 +517,23 @@ def busy(o, e):
     return 0.0
 
 
+def latency(o, e):
+    if isinstance(o["lat"], tuple):
+        return e["load0"] + e["load"] * o["lat"][1]
+    return e[o["lat"]] if o["lat"] else 0.0
+
+
 def gap(a, b, e):
     if a["lat"]:
-        return e[a["lat"]]
+        return latency(a, e)
     if b["eng"] == "X" or (a["eng"] == "E" and b["eng"] == "E"):
         return 0.0
     return e["same"] if a["eng"] == b["eng"] else e["hop"]
 
 
-def arrange(ops, deps, e, bump=None):
+def arrange(ops, deps, e):
     n = len(ops)
+    nc = len(CFG["ch"])
     succ = [[] for _ in range(n)]
     for j in range(n):
         for d in deps[j]:
@@ -545,12 +541,10 @@ def arrange(ops, deps, e, bump=None):
     dur = [busy(o, e) for o in ops]
     prio = [0.0] * n
     for j in range(n - 1, -1, -1):
-        tail = e[ops[j]["lat"]] if ops[j]["lat"] else 0.0
+        tail = latency(ops[j], e)
         if not succ[j] and ops[j]["chunk"] is not None:
-            tail += e["lag"] * (NC - 1 - ops[j]["chunk"])
+            tail += e["lag"] * (nc - 1 - ops[j]["chunk"])
         prio[j] = dur[j] + max([tail] + [gap(ops[j], ops[s], e) + prio[s] for s in succ[j]])
-    if bump:
-        prio = [p + bump[j] for j, p in enumerate(prio)]
     left = [len(d) for d in deps]
     rdy = {}
     for j in range(n):
@@ -574,6 +568,91 @@ def arrange(ops, deps, e, bump=None):
     return order
 
 
+def refine(ops, deps, order, models, steps, hot=0.25, cold=0.02, seed=1):
+    n = len(ops)
+    rnd = np.random.RandomState(seed).random_sample(4 * steps).tolist()
+    eng = ["VAEPSX".index(o["eng"]) for o in ops]
+    succ = [[] for _ in range(n)]
+    for j in range(n):
+        for d in deps[j]:
+            succ[d].append(j)
+    last = [j for j in range(n) if not succ[j]]
+    tabs = [([busy(o, e) for o in ops], [[(d, gap(ops[d], ops[j], e)) for d in deps[j]] for j in range(n)],
+             [latency(o, e) for o in ops]) for e in models]
+
+    def run(order, a, ends):
+        out, total = [], 0.0
+        for (dur, pre, tail), old in zip(tabs, ends):
+            end, free, seen = old[:], [0.0] * 6, set()
+            for j in order[a - 1::-1] if a else []:
+                if eng[j] not in seen:
+                    seen.add(eng[j])
+                    free[eng[j]] = end[j]
+                    if len(seen) == 6:
+                        break
+            for j in order[a:]:
+                q = eng[j]
+                t = free[q] if q < 5 else 0.0
+                for d, x in pre[j]:
+                    x += end[d]
+                    if x > t:
+                        t = x
+                end[j] = free[q] = t + dur[j]
+            out.append(end)
+            total += max(end[j] + tail[j] for j in last)
+        return total / len(tabs), out
+
+    def meets(order, m, end):
+        dur, pre, tail = tabs[m]
+        before, prev = {}, {}
+        for j in order:
+            before[j] = prev.get(eng[j])
+            prev[eng[j]] = j
+        j, out = max(last, key=lambda j: end[j] + tail[j]), []
+        while j is not None:
+            t, i = end[j] - dur[j] - 1e-9, before[j]
+            if eng[j] < 5 and i is not None and end[i] >= t:
+                out.append((i, j))
+                j = i
+            else:
+                j = next((d for d, x in pre[j] if end[d] + x >= t), None)
+        return out
+
+    cur, ends = run(order, 0, [[0.0] * n] * len(tabs))
+    best, pairs = (cur, order), []
+    for s in range(steps):
+        x0, x1, x2, x3 = rnd[4 * s:4 * s + 4]
+        if not pairs:
+            m = int(x0 * len(tabs))
+            pairs = meets(order, m, ends[m])
+        i, j = pairs[int(x1 * len(pairs))]
+        a, b = order.index(i), order.index(j) + 1
+        seg = order[a:b]
+        up = x2 < 0.5
+        need = {j if up else i}
+        for x in (seg[::-1] if up else seg):
+            if x in need:
+                need.update(deps[x] if up else succ[x])
+        if (i if up else j) in need:
+            pairs.remove((i, j))
+            continue
+        new = order[:a] + [x for x in seg if (x in need) == up] + [x for x in seg if (x in need) != up] + order[b:]
+        v, e2 = run(new, a, ends)
+        if v < cur or x3 < math.exp((cur - v) / (hot * (cold / hot) ** (s / steps))):
+            order, cur, ends, pairs = new, v, e2, []
+            if v < best[0]:
+                best = (v, new)
+        elif x3 > 0.9:
+            pairs = []
+    return best[1]
+
+
+def plan(ops):
+    deps = find_deps(ops)
+    slow = dict(EST, **SLOW)
+    return refine(ops, deps, arrange(ops, deps, EST), [EST, slow], STEPS)
+
+
 ORDER = {}
 
 
@@ -583,7 +662,7 @@ def rank_program(g, core, T, topo):
     ops = build(g, core, T, topo)
     deps = find_deps(ops)
     if "o" not in ORDER:
-        ORDER["o"] = arrange(ops, deps, EST)
+        ORDER["o"] = plan(ops)
     place = {j: p for p, j in enumerate(ORDER["o"])}
     queue = {"V": g.vector, "A": g.scalar, "E": g.tensor, "P": g, "S": g.sync}
     count, known, done = {}, {q: {} for q in queue}, {}

@@ -6,20 +6,20 @@ from concourse.mybir import AluOpType as ALU, ActivationFunctionType as AF
 N, LN, PL = 6, 192, 5
 CFG = dict(
     ch=[64, 64, 64],
-    cut=[["A36V28.", "A34V30.", "A60V4."]] + [["A32.A16V16."] * 3] * 4,
-    neg="AVAAAAAA",
-    loads=4,
+    cut=[["|A16V16.A16V16."] * 3] + [["A32.V32.|A32.A32."] * 3] * 4,
+    acc=True, link=[(0, 64)],
+    loads=1,
     off="SSSSS",
     bb="AAAAA", lf="AAAAA", of="VVVVV", sv="AAAAA", mv="VVVVV", up="AAAAA", wr="AAAAA", yl="A", wipe="V",
-    banks=dict(off="b0", L="b1", ZO="b2", ZL="b3", ST="b4", E1="b5", E2="b6", X="b7", U="b6", W="b5", Y="b7"))
+    banks=dict(off="b0", L="b1", ZO="b2", ZL="b3", ST="b4", E1="b5", E2="b6", X="b7", Z="b4", Y="b5"))
 CH = CFG["ch"]
 BIG = float(2 ** 24)
-MATS = ["I", "I32", "nBIG", "nHUGE", "one", "none", "oneI", "twoI", "nI32", "kb", "k4", "dtie", "tie", "u16", "v16",
-        "u4k", "v2k"]
+MATS = ["I", "I32", "nBIG", "pHUGE", "one", "k1", "k32", "none32", "oneI32", "nI64", "kb", "k4", "dtie", "tie", "u16",
+        "v16", "nu2k", "v2k", "one16"]
 MAXC = 4
 
 SCRATCH = {
-    "tab": ("sbuf", [128, 16384], "bfloat16"),
+    "tab": ("sbuf", [128, 8192], "bfloat16"),
     "posi": ("sbuf", [128, LN], "int32"),
     "sqi": ("sbuf", [128, LN], "int32"),
     "kqi": ("sbuf", [128, LN], "int32"),
@@ -29,7 +29,7 @@ SCRATCH = {
     "pc": ("sbuf", [128, 8], "int32"),
     "rc": ("sbuf", [128, 8], "int32"),
     "col": ("sbuf", [128, 16], "float32"),
-    "m16": ("sbuf", [128, 8], "float32"),
+    "rep": ("sbuf", [128, 8], "uint16"),
     "d1": ("sbuf", [128, 128], "int32"),
     "d2": ("sbuf", [128, 128], "int32"),
     "d3": ("sbuf", [128, 128], "int32"),
@@ -45,15 +45,15 @@ SCRATCH = {
     "c128": ("sbuf", [128, 8], "bfloat16"),
     "ones": ("sbuf", [128, 64], "bfloat16"),
     "rst": ("sbuf", [128, 128], "float32"),
-    "ramp": ("sbuf", [128, 32], "int32"),
+    "ramp": ("sbuf", [128, 128], "int32"),
     "ca": ("sbuf", [128, 8 * LN], "float32"),
     "cc": ("sbuf", [128, 8 * LN], "float32"),
-    "lb": ("sbuf", [128, PL * 2 * LN], "bfloat16"),
-    "s2": ("sbuf", [128, PL * 2 * LN], "bfloat16"),
-    "s3": ("sbuf", [128, PL * 2 * LN], "bfloat16"),
+    "lb": ("sbuf", [128, PL * 3 * LN], "float16"),
+    "s2": ("sbuf", [128, PL * 2 * LN], "float16"),
+    "s3": ("sbuf", [128, PL * 2 * LN], "float16"),
     "kq": ("sbuf", [128, PL * LN], "bfloat16"),
     "ylf": ("sbuf", [128, LN], "float32"),
-    "ha": ("sbuf", [128, 64 * 16], "bfloat16"),
+    "h0": ("sbuf", [128, 1024], "float16"),
     "hb": ("sbuf", [128, LN * 32], "float16"),
     "gb": ("sbuf", [128, LN * 32], "bfloat16"),
     "rb": ("sbuf", [128, LN * 32], "float16"),
@@ -82,10 +82,11 @@ SEMAPHORES = (["V", "A", "P", "E", "lpos", "lu", "lv", "lstp", "st", "sent"] + [
               + ["hcp%d" % c for c in range(MAXC)] + ["kq%d" % t for t in range(1, PL)]
               + ["ar%d_%d" % (t, c) for t in range(1, PL) for c in range(MAXC)])
 
-EST = dict(cyc=0.00087, fix=0.02, fixa=0.03, r=1.3, sc=2.8, pe=0.00061, hop=0.2, same=0.2, remote=2.3, issue=0.5,
+EST = dict(cyc=0.00083, fix=0.02, fixa=0.03, r=1.56, sc=3.8, pe=0.00061, hop=0.2, same=0.2, remote=2.3, issue=0.5,
            load0=2.0, load=5.0, small=2.2, copy=3.2, slack=0.15, lag=2.6)
-SLOW = dict(r=1.6, cyc=0.00095, hop=0.24, same=0.24, remote=2.7, sc=3.5, pe=0.0007, fixa=0.05)
-STEPS = 100000
+MODELS = [dict(r=1.3, sc=3.0, remote=2.0),
+          dict(cyc=0.00104, r=1.6, sc=3.8, pe=0.00076, hop=0.23, same=0.23, remote=2.9, fixa=0.04, fix=0.03)]
+STEPS = 200000
 
 
 def popcount(m):
@@ -105,8 +106,9 @@ def pieces(text):
     return out
 
 
-def build(g, core, T, topo):
+def build(g, core, T, topo, pick=None):
     ops, cur = [], [None]
+    pick = pick or {}
     CH = CFG["ch"]
     NC = len(CH)
     I0 = [sum(CH[:c]) for c in range(NC)]
@@ -150,11 +152,19 @@ def build(g, core, T, topo):
     def act(out, in_, fn, rd, wr, cost, bank=(), name="", **kw):
         op("A", lambda: A.activation(out, in_, fn, **kw), rd, wr, cost, bank=bank, name=name)
 
-    def relu(eng, out, in_, bias, rd, wr, n, bank=(), name=""):
-        if eng == "V":
-            ts(out, in_, bias, 0.0, ALU.add, ALU.max, rd, wr, n, bank, name)
-        else:
-            act(out, in_, AF.Relu, rd, wr, ew(n), bank, name, bias=bias)
+    def either(name, first, on_v, on_a, rd, wr, cost_v, cost_a, bank=(), inc=1):
+        e = pick.get(name, first)
+        op(e, on_v if e == "V" else on_a, rd, wr, cost_v if e == "V" else cost_a, inc=inc, bank=bank, name=name)
+        ops[-1]["both"] = {"V": cost_v, "A": cost_a}
+        return e
+
+    def relu(first, out, in_, bias, rd, wr, n, bank=(), name=""):
+        either(name, first, lambda: V.tensor_scalar(out, in_, bias, 0.0, ALU.add, ALU.max),
+               lambda: A.activation(out, in_, AF.Relu, bias=bias), rd, wr, ew(n), ew(n), bank)
+
+    def line(first, out, in_, scale, bias, rd, wr, cost_v, cost_a, name):
+        either(name, first, lambda: V.tensor_scalar(out, in_, scale, bias, ALU.mult, ALU.add),
+               lambda: A.activation(out, in_, AF.Identity, scale=scale, bias=bias), rd, wr, cost_v, cost_a)
 
     def ms(ap, val, wr, n, name=""):
         op("V", lambda: V.memset(ap, val), [], wr, ew(n), name=name)
@@ -164,66 +174,63 @@ def build(g, core, T, topo):
 
     nl = CFG["loads"]
     lw = 8192 // nl
-    for h in range(nl):
-        op("S", lambda h=h: g.sync.dma_start(T.tab[:, 8192 + lw * h:8192 + lw * (h + 1)],
-                                             T.feat[:, lw * h:lw * (h + 1)]),
-           [], ["tab%d" % h], ("dma",), "ltab%d" % h, 16, lat=("load", (h + 1) / nl))
     op("A", lambda: A.dma_start(T.posi[:], T.pos[:]), [], ["posi"], ("dma",), "lpos", 16, lat="small")
-    op("A", lambda: A.dma_start(T.ub[:], T.u[:]), [], ["ub"], ("dma",), "lu", 16, lat="small")
-    op("A", lambda: A.dma_start(T.vb[:], T.v[:]), [], ["vb"], ("dma",), "lv", 16, lat="small")
-    op("A", lambda: A.dma_start(T.stp[:, 0:1], T.step[:]), [], ["stp"], ("dma",), "lstp", 16, lat="small")
-    for h in range(8):
-        src, dst = T.tab[:, 8192 + 1024 * h:8192 + 1024 * (h + 1)], T.tab[:, 1024 * h:1024 * (h + 1)]
-        rd = ["tab%d" % (h * nl // 8)]
-        if CFG["neg"][h] == "V":
-            ts(dst, src, -1.0, -32.0, ALU.mult, ALU.add, rd, ["neg%d" % h], 512)
-        else:
-            act(dst, src, AF.Identity, rd, ["neg%d" % h], ew(1024), scale=-1.0, bias=-32.0)
+    loads = [("tab%d" % h, "ltab%d" % h, T.tab[:, lw * h:lw * (h + 1)], T.feat[:, lw * h:lw * (h + 1)],
+              (h + 1) / nl) for h in range(nl)]
+    loads += [("ub", "lu", T.ub[:], T.u[:], 1.05), ("vb", "lv", T.vb[:], T.v[:], 1.05),
+              ("stp", "lstp", T.stp[:, 0:1], T.step[:], 1.05)]
+
+    def load_all():
+        for _, sem, dst, src, _ in loads:
+            g.sync.dma_start(dst, src).then_inc(T.sem[sem], 16)
+    op("S", load_all, [], ["loads"], ("none",), "st", 0)
+    for key, sem, _, _, part in loads:
+        op("X", None, ["loads"], [key], ("none",), sem, 16, lat=("load", part))
     tabk = ["tab%d" % h for h in range(nl)]
-    negk = ["neg%d" % h for h in range(8)]
 
     op("P", lambda: g.iota(T.d1[:], [[-1, 128]], 0, 1), [], ["d1"], ("pool", 128))
     op("P", lambda: g.iota(T.d2[:], [[-16, 8], [0, 16]], 0, 1), [], ["d2"], ("pool", 128))
     op("P", lambda: g.iota(T.pc[:, 0:1], [[0, 1]], 0, 1), [], ["pc"], ("pool", 1))
-    op("P", lambda: g.iota(T.ramp[:], [[-32, 32]], 512, 0), [], ["ramp"], ("pool", 32))
+    op("P", lambda: g.iota(T.ramp[:], [[0, 8], [-32, 16]], 512, 0), [], ["ramp"], ("pool", 128))
     fill(mat("tie"), [[0, 8], [-1, 16]], 15, ["tie"], 128)
     fill(T.ones[:], [[0, 64]], 1, ["ones"], 64)
-    ms(T.ha[:], 0.0, ["ha"], 512)
     for c in range(NC):
         a, b = 8 * I0[c], 8 * (I0[c] + CH[c])
         ms(T["yp%d" % c][:], 0.0, ["yp%d" % c], 96)
         fill(T.cc[:, a:b], [[0, b - a]], 0, ["cc%d" % c], b - a)
         fill(T.ca[:, a:b], [[0, b - a]], 0, ["ca%d" % c], b - a)
-    ts(T.hb[:, 0:32], T.ramp[:], 0.0, None, ALU.max, None, ["ramp"], ["hb0"], 64)
-    n = 32
-    while n < 32 * CH[0]:
-        m = min(n, 32 * CH[0] - n)
-        op("V", lambda n=n, m=m: V.tensor_copy(T.hb[:, n:n + m], T.hb[:, 0:m]), ["hb0"], ["hb0"], ew(m // 2))
-        n += m
-    for c in range(1, NC):
-        op("S", lambda c=c: g.sync.dma_start(T.hb[:, 32 * I0[c]:32 * (I0[c] + CH[c])], T.hb[:, 0:32 * CH[c]]),
-           ["hb0", tabk[-1]], ["hb%d" % c], ("dma",), "hcp%d" % c, 16, lat="copy")
+    op("V", lambda: V.tensor_copy(T.h0[:, 0:128], T.ramp[:]), ["ramp"], ["h0"], ew(128))
+    for n in (128, 256, 512):
+        line("A", T.h0[:, n:2 * n], T.h0[:, 0:n], 1.0, 0.0, ["h0"], ["h0"], ew(n // 2), ew(n), "h0_%d" % n)
+    for c in range(NC):
+        for h in range(2):
+            a, n = 32 * I0[c] + 16 * CH[c] * h, 16 * CH[c]
+            line("A", T.hb[:, a:a + n], T.h0[:, 0:n], 1.0, 0.0, ["h0"], ["hb%d" % c], ew(n // 2), ew(n),
+                 "hb%d_%d" % (c, h))
 
-    c_r8, c_king, c_hit, c_step, c_tie, c_pm, c_t2, c_h2 = (T.col[:, j:j + 1] for j in range(8))
+    c_r8, c_king, c_hit, c_step, c_tie, c_pm, c_t2, c_h2, c_k1, c_k2, c_rf = (T.col[:, j:j + 1] for j in range(11))
     ts(mat("I"), T.d1[:], 0.0, None, ALU.is_equal, None, ["d1"], ["I"], 128)
     ts(T.idf[:], T.d1[:], 0.0, None, ALU.is_equal, None, ["d1"], ["idf"], 128)
-    ts(c_pm, T.pc[:, 0:1], 64.0, 128.0, ALU.is_ge, ALU.mult, ["pc"], ["c_pm0"], 64)
-    ts(c_t2, c_pm, -256.0, None, ALU.add, None, ["c_pm0"], ["c_pm"], 64)
+    ts(c_pm, T.pc[:, 0:1], 64.0, -256.0, ALU.is_ge, ALU.mult, ["pc"], ["c_pm0"], 64)
+    ts(c_t2, c_pm, 128.0, None, ALU.add, None, ["c_pm0"], ["c_pm"], 64)
     ts(T.idm[:], T.idf[:], c_t2, None, ALU.mult, None, ["idf", "c_pm"], ["idm"], 128)
-    for nm, s in (("I32", 32.0), ("nI32", -32.0), ("nBIG", -BIG), ("nHUGE", -256 * BIG)):
+    for nm, s in (("I32", 32.0), ("nI64", -64.0), ("nBIG", -BIG), ("pHUGE", 128 * BIG)):
         ts(mat(nm), mat("I"), s, None, ALU.mult, None, ["I"], [nm], 64)
     ts(mat("kb"), T.d2[:], 0.0, 1024.0, ALU.is_equal, ALU.mult, ["d2"], ["kb"], 128)
     ts(T.d3[:], T.d2[:], 4, None, ALU.arith_shift_right, None, ["d2"], ["d3"], 128)
     ts(mat("one"), T.d3[:], 0.0, None, ALU.is_equal, None, ["d3"], ["one"], 128)
-    ts(mat("twoI"), mat("I"), 2.0, None, ALU.mult, None, ["I"], ["twoI"], 64)
+    ts(mat("none32"), mat("one"), -32.0, None, ALU.mult, None, ["one"], ["none32"], 64)
+    op("V", lambda: V.tensor_tensor(mat("oneI32"), mat("nI64"), mat("none32"), ALU.subtract), ["nI64", "none32"],
+       ["oneI1"], ew(256))
+    op("V", lambda: V.tensor_tensor(mat("oneI32"), mat("oneI32"), mat("I32"), ALU.add), ["oneI1", "I32"],
+       ["oneI32"], ew(256))
     ts(T.rc[:, 0:1], T.pc[:, 0:1], 15, None, ALU.bitwise_and, None, ["pc"], ["rc"], 64)
     ts(c_king, T.rc[:, 0:1], 0.0, None, ALU.is_equal, None, ["rc"], ["c_king"], 64)
     ts(c_hit, c_king, -1024.0, None, ALU.mult, None, ["c_king"], ["c_hit"], 64)
     ts(c_h2, c_king, -1096.0, 64.0, ALU.mult, ALU.add, ["c_king"], ["c_h2"], 64)
-    ts(T.m16[:], mat("one")[:, 0::16], 16.0, None, ALU.mult, None, ["one"], ["m16"], 64)
     ts(c_tie, T.rc[:, 0:1], -128.0, 1920.0, ALU.mult, ALU.add, ["rc"], ["c_tie"], 64)
     ts(c_step, T.stp[:, 0:1], c_tie, None, ALU.add, None, ["stp", "c_tie"], ["c_step"], 64)
-    ts(mat("dtie"), mat("I"), c_tie, 2.0, ALU.mult, ALU.mult, ["I", "c_tie"], ["dtie"], 64)
+    ts(mat("dtie"), mat("I"), c_tie, -1.0, ALU.mult, ALU.mult, ["I", "c_tie"], ["dtie"], 64)
     if "E" in CFG["off"]:
         fill(T.c128[:, 0:4], [[128, 4]], 0, ["c128"], 4)
         fill(T.base[:, 0:16], [[0, 16]], 0, ["base0"], 16)
@@ -235,26 +242,35 @@ def build(g, core, T, topo):
         ts(T.d5[:], T.d4[:], 15, None, ALU.bitwise_and, None, ["d4"], ["d5"], 64)
         ts(T.d6[:], T.d5[:], 0.0, -4096.0, ALU.not_equal, ALU.mult, ["d5"], ["d6"], 64)
         op("V", lambda: V.tensor_tensor(T.dgm[:], T.d6[:], T.x8[:], ALU.add), ["d6", "x8"], ["dgm"], ew(128))
-        ts(mat("k4"), mat("kb"), 1.0 / 256, None, ALU.mult, None, ["kb"], ["k4"], 64)
+        ts(mat("k4"), mat("kb"), 4.0 / 1024, None, ALU.mult, None, ["kb"], ["k4"], 64)
     ms(T.rst[:], 0.0, ["rst"], 128)
     ms(T.rst[:, 0::16], -float(2 ** 26), ["rst"], 64)
-    for gq in range(8):
-        for nm, src, key in (("u16", T.ub, "ub"), ("v16", T.vb, "vb")):
-            act(matc(nm, 16 * gq, 16 * gq + 16), src[:], AF.Identity, [key, "m16"], ["%s_%d" % (nm, gq)], ew(64),
-                scale=T.m16[:, gq:gq + 1])
-    uk, vk = (["%s_%d" % (nm, gq) for gq in range(8)] for nm in ("u16", "v16"))
-    ts(mat("u4k"), mat("u16"), 256.0, None, ALU.mult, None, uk, ["u4k"], 64)
-    ts(mat("v2k"), mat("v16"), 128.0, None, ALU.mult, None, vk, ["v2k"], 64)
+    ts(c_rf, T.rc[:, 0:1], 1.0, None, ALU.mult, None, ["rc"], ["c_rf"], 64)
+    ts(T.rep[:], T.ones[:, 0:8], c_rf, None, ALU.mult, None, ["ones", "c_rf"], ["rep"], 64)
+    ts(mat("one16"), mat("one"), 16.0, None, ALU.mult, None, ["one"], ["one16"], 64)
+    for nm, src, key in (("u16", T.ub, "ub"), ("v16", T.vb, "vb")):
+        op("V", lambda nm=nm, src=src: V.tensor_tensor(mat(nm), src[:].indirect(T.rep[:]), mat("one16"), ALU.mult),
+           [key, "rep", "one16"], [nm], ("gV", 128))
+    uk, vk = ["u16"], ["v16"]
+    line("A", mat("nu2k"), mat("u16"), -128.0, 0.0, uk, ["nu2k"], ew(64), ew(128), "nu2k")
+    line("A", mat("v2k"), mat("v16"), 128.0, 0.0, vk, ["v2k"], ew(64), ew(128), "v2k")
+
+    def slot(t, c):
+        w, b = CH[c], 3 * (t * LN + I0[c])
+        x, y, z = T.lb[:, b:b + w], T.lb[:, b + w:b + 2 * w], T.lb[:, b + 2 * w:b + 3 * w]
+        lo, hi = T.lb[:, b:b + 2 * w], T.lb[:, b + w:b + 3 * w]
+        return (z, y, x, hi, lo) if t % 2 == 0 else (x, y, z, lo, hi)
 
     def halves(buf, t, c):
         w, b = CH[c], 2 * (t * LN + I0[c])
-        return buf[:, b:b + w], buf[:, b + w:b + 2 * w], buf[:, b:b + 2 * w]
+        x, y = buf[:, b:b + w], buf[:, b + w:b + 2 * w]
+        return (x, y, buf[:, b:b + 2 * w]) if t % 2 == 0 else (y, x, buf[:, b:b + 2 * w])
 
     ts(T.sqi[:], T.posi[:], 63, None, ALU.bitwise_and, None, ["posi"], ["sqi"], LN)
     ts(T.kqi[:], T.posi[:], 960, None, ALU.bitwise_and, None, ["posi"], ["kqi"], LN)
     op("V", lambda: V.tensor_copy(T.kq[:, 0:LN], T.kqi[:]), ["kqi"], ["kq0"], ew(LN))
     for c in range(NC):
-        q, dead = halves(T.lb, 0, c)[0:2]
+        q, dead = slot(0, c)[0:2]
         a, b = I0[c], I0[c] + CH[c]
         ts(q, T.sqi[:, a:b], 64.0, 1.0 / 32, ALU.add, ALU.mult, ["sqi"], ["sq0_%d" % c], 64)
         ts(dead, T.posi[:, a:b], 64.0, None, ALU.is_lt, None, ["posi"], ["dead0_%d" % c], 64)
@@ -277,7 +293,7 @@ def build(g, core, T, topo):
             rid, pid = topo.addr(d)[0:2]
             g.remote_dma(T.kq[:, t * LN:(t + 1) * LN], T.kq[:, 0:LN], T.sem["kq%d" % t], T.sem.sent, pid, rid, mk[d])
         return None
-    op("P", send_kq, ["kq0"], ["kqsent"], ("remote", 4), "sent", sum(popcount(m) for m in kq_masks(core).values()))
+    op("P", send_kq, ["kq0", tabk[-1], "stp"], ["kqsent"], ("remote", 4), "sent", sum(popcount(m) for m in kq_masks(core).values()))
     for t in range(1, PL):
         src = cores[(rank - t) % N]
         op("X", None, ["kqsent"], ["kq%d" % t], ("none",), "kq%d" % t, popcount(kq_masks(src)[core]), lat="remote")
@@ -293,8 +309,8 @@ def build(g, core, T, topo):
         K = lambda s: "%s%d" % (s, c)
         KT = lambda s: "%s%d_%d" % (s, t, c)
         E = lambda s: CFG[s][t]
-        o = 64.0 + 32 * CFG["wr"][:t].count("A")
-        q, dead, sent = halves(T.lb, t, c)
+        o = shift[c]
+        q, dead, nq, _, sent = slot(t, c)
         up, hit, src2 = halves(T.s2, t, c)
         wr, hit2, src3 = halves(T.s3, t, c)
         kq = T.kq[:, t * LN + i0:t * LN + i0 + w]
@@ -323,10 +339,7 @@ def build(g, core, T, topo):
                ["rst", BK["off"]], [K("dsc")], ew(w), bank=[BK["off"]], name=tag + "dsc")
             ts(off, dsc[:, 15:w:16], -o / 8 - 0.4375, None, ALU.add, None, [K("dsc")], [K("off")], 64,
                name=tag + "off")
-        if E("bb") == "V":
-            ts(bb, q, 4.0, 191.5625 - o / 8, ALU.mult, ALU.add, [KT("sq")], [K("bb")], 64, name=tag + "bb")
-        else:
-            act(bb, q, AF.Identity, [KT("sq")], [K("bb")], ew(64), name=tag + "bb", scale=4.0, bias=191.5625 - o / 8)
+        line(E("bb"), bb, q, 4.0, 191.5625 - o / 8, [KT("sq")], [K("bb")], ew(64), ew(64), tag + "bb")
         lsum = lambda out: [term(out, "I", kq), term(out, "I32", q), term(out, "nBIG", dead)]
         lk = ["I", "I32", "nBIG", KT("sq"), KT("dead"), kqk]
         pl, zo, zl = ps("L"), ps("ZO"), ps("ZL")
@@ -334,78 +347,64 @@ def build(g, core, T, topo):
         relu(E("lf"), lf, pl, -o, [BK["L"]], [K("lf")], w, [BK["L"]], tag + "lf")
         zpre = [(lsum(zl), lk), ([term(zl, "kb", bb)], ["kb", K("bb")])]
         if t > 0:
-            if E("of") == "V":
-                of = B("oh")[:, 0:w]
-                op("V", lambda: V.tensor_copy(of, cc.indirect(off)), [K("cc"), K("off")], [K("of")], ("gV", w),
-                   name=tag + "of")
-                oterm = ([term(zo, "I", of)], ["I", K("of")])
-            else:
-                of = B("of")[:, 0:w]
-                act(of, cc.indirect(off), AF.Identity, [K("cc"), K("off")], [K("of")], ("gA", w), name=tag + "of")
-                oterm = ([(zo, T.idf[:], of, 256)], ["idf", K("of")])
+            of = B("oh")[:, 0:w]
+            either(tag + "of", E("of"), lambda: V.tensor_copy(of, cc.indirect(off)),
+                   lambda: A.activation(of, cc.indirect(off), AF.Identity), [K("cc"), K("off")], [K("of")],
+                   ("gV", w), ("gA", w))
+            oterm = ([term(zo, "I", of)], ["I", K("of")])
             op("V", lambda: V.tensor_tensor(eq, cc.indirect(off), lf, ALU.is_equal),
                [K("cc"), K("off"), K("lf")], [K("eq")], ("gV", w), name=tag + "eq")
             mm(BK["ZO"], [([term(zo, "kb", bb)], ["kb", K("bb")]), oterm,
                           ([term(zo, "nBIG", eq)], ["nBIG", K("eq")])], tag + "mm_ZO")
             mm(BK["ZL"], zpre + [([term(zl, "nBIG", eq)], ["nBIG", K("eq")])], tag + "mm_ZL")
-            ts(idx[:, 0:2 * w:2], zo, -196608.0, 0.0, ALU.add, ALU.max, [BK["ZO"]], [K("idx")], w, [BK["ZO"]],
-               tag + "idxO")
-            ts(idx[:, 1:2 * w:2], zl, 8192.0 - 196608.0 - o, 8192.0, ALU.add, ALU.max, [BK["ZL"]], [K("idy")], w,
-               [BK["ZL"]], tag + "idxL")
-            m, win, wk = 2, T.tab[:], tabk + negk + [K("idx"), K("idy")]
+            relu("A", idx[:, 0:w], zo, -196608.0, [BK["ZO"]], [K("idxO")], w, [BK["ZO"]], tag + "idxO")
         else:
             mm(BK["ZL"], zpre, tag + "mm_ZL")
-            ts(idx[:, 0:w], zl, -196608.0 - o, 0.0, ALU.add, ALU.max, [BK["ZL"]], [K("idx"), K("idy")], w,
-               [BK["ZL"]], tag + "idx")
-            m, win, wk = 1, T.tab[:, 8192:16384], tabk + [K("idx"), K("idy")]
-        sl = 16 * m
-        G, R = T.gb[:, 32 * i0:32 * (i0 + w)], T.rb[:, 32 * i0:32 * (i0 + w)]
-        H = T.hb[:, 32 * i0:32 * (i0 + w)] if t else T.ha
-        keys = lambda s, a, b: ["%s%d_%d" % (s, c, j) for j in range(sl * a // 32, (sl * b + 31) // 32)]
-        if t > 0:
-            ts(H[:, 0:32 * w:32], ca.indirect(off), 0.0, 512.0, ALU.max, ALU.add, [K("ca"), K("off")], [K("hb")],
-               ("gV", w), name=tag + "a0")
-        a0 = 0
-        for e, a, b, dot in pieces(CFG["cut"][t][c]):
-            if e == "A":
-                act(G[:, sl * a:sl * b], win.indirect(idx[:, m * a:m * b]), AF.Identity, wk, keys("g", a, b),
-                    ("gA", sl * (b - a)), name=tag + "gA")
-            else:
-                op("V", lambda a=a, b=b: V.tensor_copy(G[:, sl * a:sl * b], win.indirect(idx[:, m * a:m * b])),
-                   wk, keys("g", a, b), ("gV", sl * (b - a)), name=tag + "gV")
-            if not dot:
-                continue
-            a, gk = a0, keys("g", a0, b)
-            a0 = b
-            if t == 0:
-                g0, hk = G[:, sl * a:sl * b:sl], ["ha"] + ["ha_%d" % j for j in range(a, b)]
-                ts(H[:, sl * a:sl * b:sl], g0, 0.0, None, ALU.max, None, gk + hk[:1], hk[1:], 64, name=tag + "h0")
-                if CFG["wipe"] == "V":
-                    ms(g0, -1024.0, gk, 64, tag + "wipe")
+        relu("V", idx[:, 64:64 + w], zl, -196608.0 - o, [BK["ZL"]], [K("idxL")], w, [BK["ZL"]], tag + "idxL")
+        keys = lambda s, h, a, b: ["%s%s%d_%d" % (s, h, c, j) for j in range(a // 2, (b + 1) // 2)]
+        for h, text in zip("OL", CFG["cut"][t][c].split("|")):
+            x0, sign = (32 * i0, -1.0) if h == "O" else (32 * i0 + 16 * w, 1.0)
+            G, R = T.gb[:, x0:x0 + 16 * w], T.rb[:, x0:x0 + 16 * w]
+            H, hk = T.hb[:, x0:x0 + 16 * w] if t else T.h0[:, 0:16 * w], keys("h", h, 0, w)
+            if t and h == "O":
+                if CFG["acc"]:
+                    line("A", H[:, 0::16], ca.indirect(off), 1.0, 512.0, [K("ca"), K("off"), K("hb")], hk,
+                         ("gV", w), ("gA", w), tag + "a0")
                 else:
-                    act(g0, T.ones[:, 0:b - a], AF.Identity, ["ones"], gk, ew(64), name=tag + "wipe", scale=-1024.0)
-                d0, d1, o0, o1 = G, H, ALU.add, ALU.max
-            else:
-                hk, d0, d1, o0, o1 = [K("hb")], H, G, ALU.max, ALU.add
-            op("V", lambda a=a, b=b, d0=d0, d1=d1, o0=o0, o1=o1: V.tensor_tensor_scan(
-                R[:, sl * a:sl * b], d0[:, sl * a:sl * b], d1[:, sl * a:sl * b], 0.0, o0, o1),
-               gk + hk, keys("r", a, b), ew((b - a) * sl // 2), name=tag + "scan")
-        rk = keys("r", 0, w)
-        acc = R[:, sl - 1:sl * w:sl]
+                    ts(H[:, 0::16], ca.indirect(off), 0.0, 512.0, ALU.max, ALU.add, [K("ca"), K("off"), K("hb")], hk,
+                       ("gV", w), name=tag + "a0")
+            elif t:
+                for a, b in CFG["link"]:
+                    a, b = a * w // 64, b * w // 64
+                    ts(H[:, 16 * a:16 * b:16], RO[:, 16 * a + 15:16 * b:16], 0.0, 512.0, ALU.max, ALU.add,
+                       keys("r", "O", a, b) + [K("hb")], keys("h", h, a, b), 64, name=tag + "link")
+            RO, a0, x1 = R, 0, 64 * (h == "L")
+            for e, a, b, dot in pieces(text):
+                line(e, G[:, 16 * a:16 * b], T.tab[:].indirect(idx[:, x1 + a:x1 + b]), sign, -32.0,
+                     tabk + [K("idx" + h)], keys("g", h, a, b), ("gV", 16 * (b - a)), ("gA", 16 * (b - a)),
+                     tag + "g%s%d" % (h, a))
+                if dot:
+                    a, a0 = a0, b
+                    op("V", lambda a=a, b=b, G=G, R=R, H=H: V.tensor_tensor_scan(
+                        R[:, 16 * a:16 * b], H[:, 16 * a:16 * b], G[:, 16 * a:16 * b], 0.0, ALU.max, ALU.add),
+                       keys("g", h, a, b) + (keys("h", h, a, b) if t else ["h0"]), keys("r", h, a, b),
+                       ew((b - a) * 8), name=tag + "scan" + h)
+        rk = keys("r", "L", 0, w)
+        acc = R[:, 15::16]
         ts(y, acc, 0.0, 127.0, ALU.max, ALU.min, rk, [K("yp")], 64, name=tag + "y")
         op("V", lambda: V.tensor_copy(cc.indirect(off), lf), [K("lf"), K("off")], [K("cc")], ("sV", w),
            name=tag + "scL")
-        if t == PL - 1:
-            act(ca, ca, AF.Relu, [K("ca")], [K("ca")], ew(8 * w), name=tag + "clamp")
-            ts(B("acc")[:, 0:w], acc, 0.0, None, ALU.max, None, rk, [K("acc")], 64, name=tag + "acc")
+        if CFG["acc"]:
+            relu("A", B("acc")[:, 0:w], acc, 0.0, rk, [K("acc")], w, name=tag + "acc")
             acc, rk = B("acc")[:, 0:w], [K("acc")]
         op("V", lambda: V.tensor_copy(ca.indirect(off), acc), rk + [K("off")], [K("ca")], ("sV", w),
            name=tag + "scA")
         if t == PL - 1:
-            op("S", lambda: g.sync.dma_start(T.yc[:, 8 * i0:8 * (i0 + w)], cc), [K("cc")], [], ("dma",), "st", 16,
-               lat="copy")
-            op("S", lambda: g.sync.dma_start(T.ya[:, 8 * i0:8 * (i0 + w)], ca), [K("ca")], [], ("dma",), "st", 16,
-               lat="copy")
+            if not CFG["acc"]:
+                relu("A", ca, ca, 0.0, [K("ca")], [K("ca")], 8 * w, name=tag + "clamp")
+            for dst, src, key in ((T.yc, cc, K("cc")), (T.ya, ca, K("ca"))):
+                op("S", lambda dst=dst, src=src: g.sync.dma_start(dst[:, 8 * i0:8 * (i0 + w)], src),
+                   [key, "sq%d_%d" % (t, NC - 1)], [], ("dma",), "st", 16, lat="copy")
         st, mx, mf = ps("ST", 128), B("mx"), B("mf")
         mm(BK["ST"], [([(st, mat("I"), mat("tie"), 128), (T[BK["ST"]][0:w, 0:128], dead, mat("nBIG"), 128)],
                        ["I", "tie", "nBIG", KT("dead")]),
@@ -416,32 +415,31 @@ def build(g, core, T, topo):
         op("V", lambda: V.tensor_tensor_scan(mf[:, ::-1], T.rst[:], mx[:, ::-1], 0.0, ALU.add, ALU.max),
            ["rst", K("mx")], [K("mf")], ew(128), name=tag + "mf")
         e1, e2 = ps("E1"), ps("E2")
-        mm(BK["E1"], [([term(e1, "dtie", ones), term(e1, "nHUGE", dead)], ["dtie", "ones", "nHUGE", KT("dead")]),
-                      ([term(e1, "u4k", y)], ["u4k", K("yp")]),
-                      ([(e1, mf[:], T.idm[:, 0:w], 256), term(e1, "I32", q)], ["idm", K("mf"), "I32", KT("sq")])],
-           tag + "mm_E1")
+        mm(BK["E1"], [([term(e1, "dtie", ones), term(e1, "pHUGE", dead)], ["dtie", "ones", "pHUGE", KT("dead")]),
+                      ([term(e1, "nu2k", y)], ["nu2k", K("yp")]),
+                      ([(e1, mf[:], T.idm[:, 0:w], 256)], ["idm", K("mf")])], tag + "mm_E1")
         mm(BK["E2"], [([term(e2, "v2k", y)], ["v2k", K("yp")]),
                       ([(e2, mf[:], T.idm[:, 64:64 + w], 256)], ["idm", K("mf")])], tag + "mm_E2")
-        relu(E("mv"), mv, e1, 0.0, [BK["E1"]], [K("mv")], w, [BK["E1"]], tag + "mv")
+        op("V", lambda: V.tensor_tensor(nq, e1, q, ALU.min), [BK["E1"], KT("sq")], [KT("nq")], ew(w),
+           bank=[BK["E1"]], name=tag + "nq")
         relu(E("sv"), sv, e2, c_step, [BK["E2"], "c_step"], [K("sv")], w, [BK["E2"]], tag + "sv")
-        ex, zu, zw = ps("X"), ps("U"), ps("W")
-        for out, bank, m1 in ((ex, "X", "one"), (zu, "U", "I"), (zw, "W", "twoI")):
-            mm(BK[bank], [([term(out, "nI32", q)], ["nI32", KT("sq")]),
-                          ([term(out, m1, mv)], [m1, K("mv")]),
+        ex, ez = ps("X"), ps("Z")
+        for out, bank, m0, m1 in ((ex, "X", "oneI32", "none32"), (ez, "Z", "I32", "nI64")):
+            mm(BK[bank], [([term(out, m0, q)], [m0, KT("sq")]),
+                          ([term(out, m1, nq)], [m1, KT("nq")]),
                           ([term(out, "one", sv)], ["one", K("sv")])], tag + "mm_" + bank)
         ts(hit, ex, c_hit, None, ALU.is_equal, None, [BK["X"], "c_hit"], [KT("hit")], w, [BK["X"]], tag + "h1")
         ts(hit2, ex, c_h2, None, ALU.is_equal, None, [BK["X"], "c_h2"], [KT("hit2")], w, [BK["X"]], tag + "h2")
-        if E("up") == "V":
-            ts(up, zu, 1.0 / 32, 0.0, ALU.mult, ALU.max, [BK["U"]], [KT("up")], w, [BK["U"]], tag + "up")
-        else:
-            act(up, zu, AF.Relu, [BK["U"]], [KT("up")], ew(w), [BK["U"]], tag + "up", scale=1.0 / 32)
-        if E("wr") == "V":
-            ts(wr, zw, 64.0 + o, -2.0, ALU.is_ge, ALU.mult, [BK["W"]], [KT("wrap")], w, [BK["W"]], tag + "wrap")
-        else:
-            act(wr, zw, AF.Sign, [BK["W"]], [KT("wrap")], ew(w), [BK["W"]], tag + "wrap", scale=-1.0, bias=63.5 + o)
-        four = [KT("hit"), KT("hit2"), KT("up"), KT("wrap")]
+        if either(tag + "up", E("up"),
+                  lambda: [V.tensor_scalar(up, ez, 1.0 / 32, 0.0, ALU.mult, ALU.max),
+                           V.tensor_scalar(wr, ez, 64.0 + o, -2.0, ALU.is_ge, ALU.mult)],
+                  lambda: [A.activation(up, ez, AF.Relu, scale=1.0 / 32),
+                           A.activation(wr, ez, AF.Sign, scale=-1.0, bias=63.5 + o)],
+                  [BK["Z"]], [KT("up")], ("two", w), ("two", w), [BK["Z"]], 2) == "A":
+            shift[c] += 32
+        four = [KT("hit"), KT("hit2"), KT("up")]
         if t < PL - 1:
-            land = halves(T.lb, t + 1, c)[2]
+            land = slot(t + 1, c)[3]
             ar = "ar%d_%d" % (t + 1, c)
 
             def hop():
@@ -449,21 +447,21 @@ def build(g, core, T, topo):
                     dst_ids=[DstId(rid=rid_n, pnc=pid_n)], dma_engine_mask=m_out, remote_sem=T.sem[ar],
                     srcs=[sent, src2, src3], dsts=[land], alu_op=1)], local_sem=T.sem.sent)
                 return None
-            op("P", hop, [KT("sq"), KT("dead")] + four, [KT("hop")], ("remote", 1), "sent", popcount(m_out),
+            op("P", hop, [KT("nq"), KT("dead")] + four, [KT("hop")], ("remote", 1), "sent", popcount(m_out),
                name=tag + "hop")
             op("X", None, [KT("hop")], ["sq%d_%d" % (t + 1, c), "dead%d_%d" % (t + 1, c)], ("none",), ar,
                popcount(m_in), lat="remote")
         else:
             ey = ps("Y")
-            mm(BK["Y"], [(lsum(ey), lk),
+            mm(BK["Y"], [([term(ey, "I", kq), term(ey, "nBIG", dead), term(ey, "I32", nq)], lk + [KT("nq")]),
                          ([term(ey, "nBIG", hit), term(ey, "nBIG", hit2), term(ey, "I32", up), term(ey, "I32", wr)],
                           four)], tag + "mm_Y")
             yo = T.ylf[:, i0:i0 + w]
-            relu(CFG["yl"], yo, ey, -o - (32.0 if E("wr") == "A" else 0.0), [BK["Y"]], [K("ylf")], w, [BK["Y"]],
-                 tag + "yl")
+            relu(CFG["yl"], yo, ey, -shift[c], [BK["Y"]], [K("ylf")], w, [BK["Y"]], tag + "yl")
             op("S", lambda: g.sync.dma_start(T.yl[:, i0:i0 + w], yo), [K("ylf")], [], ("dma",), "st", 16,
                lat="small")
 
+    shift = [64.0] * NC
     for t in range(PL):
         for c in range(NC):
             ply(t, c)
@@ -473,6 +471,7 @@ def build(g, core, T, topo):
 def find_deps(ops):
     lastw, readers, lastb = {}, {}, {}
     deps = []
+    who = [j if "both" in o else o["eng"] for j, o in enumerate(ops)]
     for j, o in enumerate(ops):
         d = set()
         for key in o["rd"]:
@@ -483,7 +482,7 @@ def find_deps(ops):
                 d.add(lastw[key])
             d.update(readers.get(key, []))
         for key in o["bank"]:
-            d.update(x for x in lastb.get(key, []) if ops[x]["eng"] != o["eng"])
+            d.update(x for x in lastb.get(key, []) if who[x] != who[j])
         d.discard(j)
         deps.append(sorted(d))
         for key in o["rd"]:
@@ -492,7 +491,7 @@ def find_deps(ops):
             lastw[key] = j
             readers[key] = []
         for key in o["bank"]:
-            lastb[key] = [x for x in lastb.get(key, []) if ops[x]["eng"] == o["eng"]] + [j]
+            lastb[key] = [x for x in lastb.get(key, []) if who[x] == who[j]] + [j]
     return deps
 
 
@@ -500,6 +499,8 @@ def busy(o, e):
     c = o["cost"]
     if c[0] == "ew":
         return e["fixa" if o["eng"] == "A" else "fix"] + max(64, c[1]) * e["cyc"]
+    if c[0] == "two":
+        return 2 * busy(dict(o, cost=("ew", c[1])), e)
     if c[0] == "gV":
         return 0.05 + c[1] * e["r"] * e["cyc"]
     if c[0] == "gA":
@@ -568,7 +569,7 @@ def arrange(ops, deps, e):
     return order
 
 
-def refine(ops, deps, order, models, steps, hot=0.25, cold=0.02, seed=1):
+def refine(ops, deps, order, models, steps, hot=0.15, cold=0.03, seed=2, turn=0.2):
     n = len(ops)
     rnd = np.random.RandomState(seed).random_sample(4 * steps).tolist()
     eng = ["VAEPSX".index(o["eng"]) for o in ops]
@@ -579,10 +580,20 @@ def refine(ops, deps, order, models, steps, hot=0.25, cold=0.02, seed=1):
     last = [j for j in range(n) if not succ[j]]
     tabs = [([busy(o, e) for o in ops], [[(d, gap(ops[d], ops[j], e)) for d in deps[j]] for j in range(n)],
              [latency(o, e) for o in ops]) for e in models]
+    both = {j: [[busy(dict(o, eng=q, cost=o["both"][q]), e) for e in models] for q in "VA"]
+            for j, o in enumerate(ops) if "both" in o}
+    movable = sorted(both)
 
-    def run(order, a, ends):
+    def flip(j):
+        eng[j] = 1 - eng[j]
+        for tab, d in zip(tabs, both[j][eng[j]]):
+            tab[0][j] = d
+
+    def run(order, a, ends, most=1e9):
         out, total = [], 0.0
         for (dur, pre, tail), old in zip(tabs, ends):
+            if total - sum(max(e[j] + tb[2][j] for j in last) for tb, e in zip(tabs, ends[:len(out)])) > most:
+                return 1e9, None
             end, free, seen = old[:], [0.0] * 6, set()
             for j in order[a - 1::-1] if a else []:
                 if eng[j] not in seen:
@@ -619,16 +630,29 @@ def refine(ops, deps, order, models, steps, hot=0.25, cold=0.02, seed=1):
         return out
 
     cur, ends = run(order, 0, [[0.0] * n] * len(tabs))
-    best, pairs = (cur, order), []
+    best, pairs = (cur, order, eng[:]), []
     for s in range(steps):
         x0, x1, x2, x3 = rnd[4 * s:4 * s + 4]
         if not pairs:
             m = int(x0 * len(tabs))
             pairs = meets(order, m, ends[m])
         i, j = pairs[int(x1 * len(pairs))]
+        room = -math.log(x3) * hot * (cold / hot) ** (s / steps)
+        if x2 < turn:
+            c = movable[int(x1 * len(movable))] if x2 < turn / 6 else i if x2 < turn / 2 else j
+            if c in both:
+                flip(c)
+                v, e2 = run(order, order.index(c), ends, room * len(tabs) + 0.1)
+                if v < cur + room:
+                    cur, ends, pairs = v, e2, []
+                    if v < best[0]:
+                        best = (v, order, eng[:])
+                else:
+                    flip(c)
+            continue
         a, b = order.index(i), order.index(j) + 1
         seg = order[a:b]
-        up = x2 < 0.5
+        up = x2 < (1 + turn) / 2
         need = {j if up else i}
         for x in (seg[::-1] if up else seg):
             if x in need:
@@ -637,20 +661,19 @@ def refine(ops, deps, order, models, steps, hot=0.25, cold=0.02, seed=1):
             pairs.remove((i, j))
             continue
         new = order[:a] + [x for x in seg if (x in need) == up] + [x for x in seg if (x in need) != up] + order[b:]
-        v, e2 = run(new, a, ends)
-        if v < cur or x3 < math.exp((cur - v) / (hot * (cold / hot) ** (s / steps))):
+        v, e2 = run(new, a, ends, room * len(tabs) + 0.1)
+        if v < cur + room:
             order, cur, ends, pairs = new, v, e2, []
             if v < best[0]:
-                best = (v, new)
+                best = (v, new, eng[:])
         elif x3 > 0.9:
             pairs = []
-    return best[1]
+    return best[1], {ops[j]["name"]: "VA"[best[2][j]] for j in movable}
 
 
 def plan(ops):
     deps = find_deps(ops)
-    slow = dict(EST, **SLOW)
-    return refine(ops, deps, arrange(ops, deps, EST), [EST, slow], STEPS)
+    return refine(ops, deps, arrange(ops, deps, EST), [dict(EST, **m) for m in MODELS], STEPS)
 
 
 ORDER = {}
@@ -659,10 +682,10 @@ ORDER = {}
 def rank_program(g, core, T, topo):
     if T.rank_of(core) is None:
         return
-    ops = build(g, core, T, topo)
-    deps = find_deps(ops)
     if "o" not in ORDER:
-        ORDER["o"] = plan(ops)
+        ORDER["o"], ORDER["pick"] = plan(build(g, core, T, topo))
+    ops = build(g, core, T, topo, ORDER["pick"])
+    deps = find_deps(ops)
     place = {j: p for p, j in enumerate(ORDER["o"])}
     queue = {"V": g.vector, "A": g.scalar, "E": g.tensor, "P": g, "S": g.sync}
     count, known, done = {}, {q: {} for q in queue}, {}
@@ -684,8 +707,8 @@ def rank_program(g, core, T, topo):
                 if kn.get(s2, 0) < v2:
                     kn[s2] = v2
         ins = o["fn"]()
-        if ins is not None:
-            ins.then_inc(T.sem[o["sem"]], o["inc"])
+        for x in ins if isinstance(ins, list) else [] if ins is None else [ins]:
+            x.then_inc(T.sem[o["sem"]], 1 if isinstance(ins, list) else o["inc"])
         done[j] = (o["sem"], count[o["sem"]], dict(kn))
     for s, val in count.items():
         if max(kn.get(s, 0) for kn in known.values()) < val:

@@ -6,29 +6,29 @@ from concourse.mybir import AluOpType as ALU, ActivationFunctionType as AF
 N, LN, PL = 6, 192, 5
 CFG = dict(
     ch=[64, 64, 64],
-    cut=[["|A16V16.A16V16."] * 3] + [["A32.V32.|A32.A32."] * 3] * 4,
-    acc=True, link=[(0, 64)],
-    loads=1,
-    off="SSSSS",
-    bb="AAAAA", lf="AAAAA", of="VVVVV", sv="AAAAA", mv="VVVVV", up="AAAAA", wr="AAAAA", yl="A", wipe="V",
-    banks=dict(off="b0", L="b1", ZO="b2", ZL="b3", ST="b4", E1="b5", E2="b6", X="b7", Z="b4", Y="b5"))
-CH = CFG["ch"]
+    cut=[["|A32.V32."] * 3] + [["A32.V32.|A32.A32."] * 3] * 4,
+    banks=dict(off="b0", ZO="b2", ZL="b3", ST="b4", E1="b5", E2="b6", X="b7", Y="b1"))
 BIG = float(2 ** 24)
-MATS = ["I", "I32", "nBIG", "pHUGE", "one", "k1", "k32", "none32", "oneI32", "nI64", "kb", "k4", "dtie", "tie", "u16",
-        "v16", "nu2k", "v2k", "one16"]
+SCALED = dict(nBIG=("I", -BIG), n4k=("I", -4096.0), C17=("I", 1.5 * 2 ** 17), nC17=("I", -1.5 * 2 ** 17),
+              C33=("I", 1.5 * 2 ** 33), nC33=("I", -1.5 * 2 ** 33), n448=("I", -448.0), half=("I", 31.5 / 4096),
+              unit=("I", 1.0 / 4096), n3unit=("I", -3.0 / 4096), n3=("I", -3.0), none=("one", -1.0),
+              step=("one", 1.0 / 4096), nstep=("one", -1.0 / 4096), k8=("king", -1.0 / 8), q8=("king", -512.0),
+              k128=("king", -128.0), q128=("king", -128.0 * 4096))
+MATS = ["I", "one", "king", "stay", "one3", "dtie", "tie", "u16", "v16", "v2k"] + list(SCALED)
 MAXC = 4
 
 SCRATCH = {
     "tab": ("sbuf", [128, 8192], "bfloat16"),
     "posi": ("sbuf", [128, LN], "int32"),
-    "sqi": ("sbuf", [128, LN], "int32"),
     "kqi": ("sbuf", [128, LN], "int32"),
-    "ub": ("sbuf", [128, 16], "bfloat16"),
-    "vb": ("sbuf", [128, 16], "bfloat16"),
+    "qa": ("sbuf", [128, LN], "float16"),
+    "qb": ("sbuf", [128, LN], "float16"),
+    "ub": ("sbuf", [128, 32], "bfloat16"),
+    "vb": ("sbuf", [128, 32], "bfloat16"),
     "stp": ("sbuf", [128, 8], "int32"),
     "pc": ("sbuf", [128, 8], "int32"),
     "rc": ("sbuf", [128, 8], "int32"),
-    "col": ("sbuf", [128, 16], "float32"),
+    "col": ("sbuf", [128, 8], "float32"),
     "rep": ("sbuf", [128, 8], "uint16"),
     "d1": ("sbuf", [128, 128], "int32"),
     "d2": ("sbuf", [128, 128], "int32"),
@@ -39,18 +39,16 @@ SCRATCH = {
     "dgm": ("sbuf", [128, 64], "bfloat16"),
     "x8": ("sbuf", [128, 64], "bfloat16"),
     "mat": ("sbuf", [128, 128 * len(MATS)], "bfloat16"),
-    "idf": ("sbuf", [128, 128], "float32"),
     "idm": ("sbuf", [128, 128], "float32"),
-    "base": ("sbuf", [128, 144], "bfloat16"),
-    "c128": ("sbuf", [128, 8], "bfloat16"),
     "ones": ("sbuf", [128, 64], "bfloat16"),
     "rst": ("sbuf", [128, 128], "float32"),
     "ramp": ("sbuf", [128, 128], "int32"),
     "ca": ("sbuf", [128, 8 * LN], "float32"),
     "cc": ("sbuf", [128, 8 * LN], "float32"),
-    "lb": ("sbuf", [128, PL * 3 * LN], "float16"),
-    "s2": ("sbuf", [128, PL * 2 * LN], "float16"),
-    "s3": ("sbuf", [128, PL * 2 * LN], "float16"),
+    "q": ("sbuf", [128, PL * LN], "float16"),
+    "nq": ("sbuf", [128, PL * LN], "float16"),
+    "up": ("sbuf", [128, PL * LN], "float16"),
+    "hit": ("sbuf", [128, PL * LN], "float16"),
     "kq": ("sbuf", [128, PL * LN], "bfloat16"),
     "ylf": ("sbuf", [128, LN], "float32"),
     "h0": ("sbuf", [128, 1024], "float16"),
@@ -63,30 +61,28 @@ for _b in range(8):
 for _c in range(MAXC):
     SCRATCH.update({
         "acc%d" % _c: ("sbuf", [128, 64], "float16"),
-        "bb%d" % _c: ("sbuf", [128, 64], "bfloat16"),
         "dsc%d" % _c: ("sbuf", [128, 64], "float32"),
         "off%d" % _c: ("sbuf", [128, 8], "uint16"),
         "idx%d" % _c: ("sbuf", [128, 128], "uint16"),
-        "lf%d" % _c: ("sbuf", [128, 64], "float32"),
-        "of%d" % _c: ("sbuf", [128, 64], "float32"),
-        "oh%d" % _c: ("sbuf", [128, 64], "float16"),
+        "lf%d" % _c: ("sbuf", [128, 64], "float16"),
+        "of%d" % _c: ("sbuf", [128, 64], "float16"),
         "eq%d" % _c: ("sbuf", [128, 64], "bfloat16"),
         "yp%d" % _c: ("sbuf", [128, 192], "bfloat16"),
         "mx%d" % _c: ("sbuf", [128, 128], "float32"),
         "mf%d" % _c: ("sbuf", [128, 128], "float32"),
         "sv%d" % _c: ("sbuf", [128, 64], "bfloat16"),
-        "mv%d" % _c: ("sbuf", [128, 64], "bfloat16"),
     })
 
-SEMAPHORES = (["V", "A", "P", "E", "lpos", "lu", "lv", "lstp", "st", "sent"] + ["ltab%d" % h for h in range(4)]
-              + ["hcp%d" % c for c in range(MAXC)] + ["kq%d" % t for t in range(1, PL)]
+SEMAPHORES = (["V", "A", "P", "E", "lpos", "lu", "lv", "lstp", "ltab", "st", "sent"]
+              + ["kq%d" % t for t in range(1, PL)]
               + ["ar%d_%d" % (t, c) for t in range(1, PL) for c in range(MAXC)])
 
 EST = dict(cyc=0.00083, fix=0.02, fixa=0.03, r=1.56, sc=3.8, pe=0.00061, hop=0.2, same=0.2, remote=2.3, issue=0.5,
            load0=2.0, load=5.0, small=2.2, copy=3.2, slack=0.15, lag=2.6)
-MODELS = [dict(r=1.3, sc=3.0, remote=2.0),
-          dict(cyc=0.00104, r=1.6, sc=3.8, pe=0.00076, hop=0.23, same=0.23, remote=2.9, fixa=0.04, fix=0.03)]
-STEPS = 200000
+MODELS = [dict(r=1.3, sc=3.0, remote=1.9),
+          dict(cyc=0.0009, pe=0.00066, r=1.4, sc=3.4, hop=0.25, same=0.25, remote=2.8, issue=0.6),
+          dict(cyc=0.00114, pe=0.00084, r=1.8, sc=4.4, hop=0.22, same=0.22, fixa=0.04, fix=0.03)]
+STEPS = 75000
 
 
 def popcount(m):
@@ -129,12 +125,12 @@ def build(g, core, T, topo, pick=None):
         k = MATS.index(name)
         return T.mat[:, 128 * k:128 * (k + 1)]
 
-    def matc(name, a, b):
-        k = MATS.index(name)
-        return T.mat[:, 128 * k + a:128 * k + b]
-
-    def mm(bank, parts, name):
+    def mm(role, parts, name, n=None):
+        bank = BK[role]
         for p, (terms, rd) in enumerate(parts):
+            rd = list(rd) + [x[0] for x in terms if len(x) == 2]
+            terms = [x if len(x) == 4 else (T[bank][:, 0:n], mat(x[0]), x[1], 64) for x in terms]
+
             def fn(p=p, terms=terms):
                 last = None
                 for j, (o, l, r, _) in enumerate(terms):
@@ -142,21 +138,19 @@ def build(g, core, T, topo, pick=None):
                 return last
             op("E", fn, rd, [bank], ("pe", sum(x[3] for x in terms)), bank=[bank], name=name + str(p))
 
-    def ts(out, in0, s1, s2, o0, o1, rd, wr, n, bank=(), name=""):
-        cost = n if isinstance(n, tuple) else ew(n)
+    def ts(out, in0, s1, s2, o0, o1, rd, wr, n, name=""):
         if o1 is None:
-            op("V", lambda: V.tensor_scalar(out, in0, s1, None, o0), rd, wr, cost, bank=bank, name=name)
+            op("V", lambda: V.tensor_scalar(out, in0, s1, None, o0), rd, wr, ew(n), name=name)
         else:
-            op("V", lambda: V.tensor_scalar(out, in0, s1, s2, o0, o1), rd, wr, cost, bank=bank, name=name)
+            op("V", lambda: V.tensor_scalar(out, in0, s1, s2, o0, o1), rd, wr, ew(n), name=name)
 
-    def act(out, in_, fn, rd, wr, cost, bank=(), name="", **kw):
-        op("A", lambda: A.activation(out, in_, fn, **kw), rd, wr, cost, bank=bank, name=name)
+    def tt(out, in0, in1, alu, rd, wr, cost, bank=(), name=""):
+        op("V", lambda: V.tensor_tensor(out, in0, in1, alu), rd, wr, cost, bank=bank, name=name)
 
-    def either(name, first, on_v, on_a, rd, wr, cost_v, cost_a, bank=(), inc=1):
+    def either(name, first, on_v, on_a, rd, wr, cost_v, cost_a, bank=()):
         e = pick.get(name, first)
-        op(e, on_v if e == "V" else on_a, rd, wr, cost_v if e == "V" else cost_a, inc=inc, bank=bank, name=name)
+        op(e, on_v if e == "V" else on_a, rd, wr, cost_v if e == "V" else cost_a, bank=bank, name=name)
         ops[-1]["both"] = {"V": cost_v, "A": cost_a}
-        return e
 
     def relu(first, out, in_, bias, rd, wr, n, bank=(), name=""):
         either(name, first, lambda: V.tensor_scalar(out, in_, bias, 0.0, ALU.add, ALU.max),
@@ -166,114 +160,86 @@ def build(g, core, T, topo, pick=None):
         either(name, first, lambda: V.tensor_scalar(out, in_, scale, bias, ALU.mult, ALU.add),
                lambda: A.activation(out, in_, AF.Identity, scale=scale, bias=bias), rd, wr, cost_v, cost_a)
 
-    def ms(ap, val, wr, n, name=""):
-        op("V", lambda: V.memset(ap, val), [], wr, ew(n), name=name)
+    def ms(ap, val, wr, n):
+        op("V", lambda: V.memset(ap, val), [], wr, ew(n))
 
-    def fill(ap, pat, base, wr, n):
-        op("P", lambda: g.iota(ap, pat, base, 0, allow_small_or_imprecise_dtypes=True), [], wr, ("pool", n))
+    def iota(ap, pat, base, mult, wr, n):
+        op("P", lambda: g.iota(ap, pat, base, mult, allow_small_or_imprecise_dtypes=True), [], wr, ("pool", n))
 
-    nl = CFG["loads"]
-    lw = 8192 // nl
     op("A", lambda: A.dma_start(T.posi[:], T.pos[:]), [], ["posi"], ("dma",), "lpos", 16, lat="small")
-    loads = [("tab%d" % h, "ltab%d" % h, T.tab[:, lw * h:lw * (h + 1)], T.feat[:, lw * h:lw * (h + 1)],
-              (h + 1) / nl) for h in range(nl)]
-    loads += [("ub", "lu", T.ub[:], T.u[:], 1.05), ("vb", "lv", T.vb[:], T.v[:], 1.05),
-              ("stp", "lstp", T.stp[:, 0:1], T.step[:], 1.05)]
+    loads = [("ltab", T.tab[:, 1024 * b + 64:1024 * (b + 1)], T.feat[:, 1024 * b + 64:1024 * (b + 1)])
+             for b in range(8)]
+    loads += [("lu", T.ub[:, 16:32], T.u[:]), ("lv", T.vb[:, 16:32], T.v[:]), ("lstp", T.stp[:, 0:1], T.step[:])]
 
     def load_all():
-        for _, sem, dst, src, _ in loads:
+        for sem, dst, src in loads:
             g.sync.dma_start(dst, src).then_inc(T.sem[sem], 16)
     op("S", load_all, [], ["loads"], ("none",), "st", 0)
-    for key, sem, _, _, part in loads:
-        op("X", None, ["loads"], [key], ("none",), sem, 16, lat=("load", part))
-    tabk = ["tab%d" % h for h in range(nl)]
+    for key, sem, n, part in (("tab", "ltab", 8, 1.0), ("ub", "lu", 1, 1.05), ("vb", "lv", 1, 1.05),
+                              ("stp", "lstp", 1, 1.05)):
+        op("X", None, ["loads"], [key], ("none",), sem, 16 * n, lat=("load", part))
+    for b in range(8):
+        ms(T.tab[:, 1024 * b:1024 * b + 64], 0.0, ["tab%d" % b], 64)
+    tabk = ["tab"] + ["tab%d" % b for b in range(8)]
 
-    op("P", lambda: g.iota(T.d1[:], [[-1, 128]], 0, 1), [], ["d1"], ("pool", 128))
-    op("P", lambda: g.iota(T.d2[:], [[-16, 8], [0, 16]], 0, 1), [], ["d2"], ("pool", 128))
-    op("P", lambda: g.iota(T.pc[:, 0:1], [[0, 1]], 0, 1), [], ["pc"], ("pool", 1))
-    op("P", lambda: g.iota(T.ramp[:], [[0, 8], [-32, 16]], 512, 0), [], ["ramp"], ("pool", 128))
-    fill(mat("tie"), [[0, 8], [-1, 16]], 15, ["tie"], 128)
-    fill(T.ones[:], [[0, 64]], 1, ["ones"], 64)
+    iota(T.d1[:], [[-1, 128]], 0, 1, ["d1"], 128)
+    iota(T.d2[:], [[-16, 8], [0, 16]], 0, 1, ["d2"], 128)
+    iota(T.pc[:, 0:1], [[0, 1]], 0, 1, ["pc"], 1)
+    iota(T.ramp[:], [[0, 8], [-32, 16]], 512, 0, ["ramp"], 128)
+    iota(T.d4[:], [[-1, 64]], 64, 1, ["d4"], 64)
+    iota(T.x8[:], [[8, 64]], 0, 0, ["x8"], 64)
+    iota(mat("tie"), [[0, 8], [-1, 16]], 15, 0, ["tie"], 128)
+    iota(T.ones[:], [[0, 64]], 1, 0, ["ones"], 64)
     for c in range(NC):
         a, b = 8 * I0[c], 8 * (I0[c] + CH[c])
         ms(T["yp%d" % c][:], 0.0, ["yp%d" % c], 96)
-        fill(T.cc[:, a:b], [[0, b - a]], 0, ["cc%d" % c], b - a)
-        fill(T.ca[:, a:b], [[0, b - a]], 0, ["ca%d" % c], b - a)
+        iota(T.cc[:, a:b], [[0, b - a]], 0, 0, ["cc%d" % c], b - a)
+        iota(T.ca[:, a:b], [[0, b - a]], 0, 0, ["ca%d" % c], b - a)
     op("V", lambda: V.tensor_copy(T.h0[:, 0:128], T.ramp[:]), ["ramp"], ["h0"], ew(128))
     for n in (128, 256, 512):
         line("A", T.h0[:, n:2 * n], T.h0[:, 0:n], 1.0, 0.0, ["h0"], ["h0"], ew(n // 2), ew(n), "h0_%d" % n)
     for c in range(NC):
         for h in range(2):
             a, n = 32 * I0[c] + 16 * CH[c] * h, 16 * CH[c]
-            line("A", T.hb[:, a:a + n], T.h0[:, 0:n], 1.0, 0.0, ["h0"], ["hb%d" % c], ew(n // 2), ew(n),
+            line("A", T.hb[:, a:a + n], T.h0[:, 0:n], 1.0, 0.0, ["h0"], ["hb%s%d" % ("OL"[h], c)], ew(n // 2), ew(n),
                  "hb%d_%d" % (c, h))
 
-    c_r8, c_king, c_hit, c_step, c_tie, c_pm, c_t2, c_h2, c_k1, c_k2, c_rf = (T.col[:, j:j + 1] for j in range(11))
+    c_stay, c_step, c_tie, c_far, c_back, c_rep = (T.col[:, j:j + 1] for j in range(6))
     ts(mat("I"), T.d1[:], 0.0, None, ALU.is_equal, None, ["d1"], ["I"], 128)
-    ts(T.idf[:], T.d1[:], 0.0, None, ALU.is_equal, None, ["d1"], ["idf"], 128)
-    ts(c_pm, T.pc[:, 0:1], 64.0, -256.0, ALU.is_ge, ALU.mult, ["pc"], ["c_pm0"], 64)
-    ts(c_t2, c_pm, 128.0, None, ALU.add, None, ["c_pm0"], ["c_pm"], 64)
-    ts(T.idm[:], T.idf[:], c_t2, None, ALU.mult, None, ["idf", "c_pm"], ["idm"], 128)
-    for nm, s in (("I32", 32.0), ("nI64", -64.0), ("nBIG", -BIG), ("pHUGE", 128 * BIG)):
-        ts(mat(nm), mat("I"), s, None, ALU.mult, None, ["I"], [nm], 64)
-    ts(mat("kb"), T.d2[:], 0.0, 1024.0, ALU.is_equal, ALU.mult, ["d2"], ["kb"], 128)
+    ts(mat("king"), T.d2[:], 0.0, None, ALU.is_equal, None, ["d2"], ["king"], 128)
     ts(T.d3[:], T.d2[:], 4, None, ALU.arith_shift_right, None, ["d2"], ["d3"], 128)
     ts(mat("one"), T.d3[:], 0.0, None, ALU.is_equal, None, ["d3"], ["one"], 128)
-    ts(mat("none32"), mat("one"), -32.0, None, ALU.mult, None, ["one"], ["none32"], 64)
-    op("V", lambda: V.tensor_tensor(mat("oneI32"), mat("nI64"), mat("none32"), ALU.subtract), ["nI64", "none32"],
-       ["oneI1"], ew(256))
-    op("V", lambda: V.tensor_tensor(mat("oneI32"), mat("oneI32"), mat("I32"), ALU.add), ["oneI1", "I32"],
-       ["oneI32"], ew(256))
+    for nm, (src, s) in SCALED.items():
+        line("A", mat(nm), mat(src), s, 0.0, [src], [nm], ew(64), ew(128), nm)
+    tt(mat("one3"), mat("one"), mat("n3"), ALU.add, ["one", "n3"], ["one3"], ew(256))
+    ts(c_far, T.pc[:, 0:1], 64.0, -127.0, ALU.is_ge, ALU.mult, ["pc"], ["c_far"], 64)
+    ts(c_back, c_far, -1.0, None, ALU.add, None, ["c_far"], ["c_back"], 64)
+    ts(T.idm[:], mat("I"), c_back, None, ALU.mult, None, ["I", "c_back"], ["idm"], 128)
     ts(T.rc[:, 0:1], T.pc[:, 0:1], 15, None, ALU.bitwise_and, None, ["pc"], ["rc"], 64)
-    ts(c_king, T.rc[:, 0:1], 0.0, None, ALU.is_equal, None, ["rc"], ["c_king"], 64)
-    ts(c_hit, c_king, -1024.0, None, ALU.mult, None, ["c_king"], ["c_hit"], 64)
-    ts(c_h2, c_king, -1096.0, 64.0, ALU.mult, ALU.add, ["c_king"], ["c_h2"], 64)
+    ts(c_stay, T.rc[:, 0:1], 0.0, 2.0, ALU.is_equal, ALU.add, ["rc"], ["c_stay"], 64)
+    ts(mat("stay"), mat("I"), c_stay, None, ALU.mult, None, ["I", "c_stay"], ["stay0"], 64)
+    tt(mat("stay"), mat("stay"), mat("one"), ALU.add, ["stay0", "one"], ["stay"], ew(256))
     ts(c_tie, T.rc[:, 0:1], -128.0, 1920.0, ALU.mult, ALU.add, ["rc"], ["c_tie"], 64)
     ts(c_step, T.stp[:, 0:1], c_tie, None, ALU.add, None, ["stp", "c_tie"], ["c_step"], 64)
-    ts(mat("dtie"), mat("I"), c_tie, -1.0, ALU.mult, ALU.mult, ["I", "c_tie"], ["dtie"], 64)
-    if "E" in CFG["off"]:
-        fill(T.c128[:, 0:4], [[128, 4]], 0, ["c128"], 4)
-        fill(T.base[:, 0:16], [[0, 16]], 0, ["base0"], 16)
-        ts(c_r8, T.rc[:, 0:1], 8.0, None, ALU.mult, None, ["rc"], ["c_r8"], 64)
-        ts(T.base[:, 16:144], mat("I"), c_king, 4.0, ALU.mult, ALU.mult, ["I", "c_king"], ["base"], 64)
-    if "S" in CFG["off"]:
-        op("P", lambda: g.iota(T.d4[:], [[-1, 64]], 64, 1), [], ["d4"], ("pool", 64))
-        fill(T.x8[:], [[8, 64]], 0, ["x8"], 64)
-        ts(T.d5[:], T.d4[:], 15, None, ALU.bitwise_and, None, ["d4"], ["d5"], 64)
-        ts(T.d6[:], T.d5[:], 0.0, -4096.0, ALU.not_equal, ALU.mult, ["d5"], ["d6"], 64)
-        op("V", lambda: V.tensor_tensor(T.dgm[:], T.d6[:], T.x8[:], ALU.add), ["d6", "x8"], ["dgm"], ew(128))
-        ts(mat("k4"), mat("kb"), 4.0 / 1024, None, ALU.mult, None, ["kb"], ["k4"], 64)
+    ts(mat("dtie"), mat("I"), c_tie, 1.0 / 128, ALU.mult, ALU.mult, ["I", "c_tie"], ["dtie"], 64)
+    ts(T.d5[:], T.d4[:], 15, None, ALU.bitwise_and, None, ["d4"], ["d5"], 64)
+    ts(T.d6[:], T.d5[:], 0.0, -4096.0, ALU.not_equal, ALU.mult, ["d5"], ["d6"], 64)
+    tt(T.dgm[:], T.d6[:], T.x8[:], ALU.add, ["d6", "x8"], ["dgm"], ew(128))
     ms(T.rst[:], 0.0, ["rst"], 128)
     ms(T.rst[:, 0::16], -float(2 ** 26), ["rst"], 64)
-    ts(c_rf, T.rc[:, 0:1], 1.0, None, ALU.mult, None, ["rc"], ["c_rf"], 64)
-    ts(T.rep[:], T.ones[:, 0:8], c_rf, None, ALU.mult, None, ["ones", "c_rf"], ["rep"], 64)
-    ts(mat("one16"), mat("one"), 16.0, None, ALU.mult, None, ["one"], ["one16"], 64)
+    ts(c_rep, T.rc[:, 0:1], 16.0, None, ALU.add, None, ["rc"], ["c_rep"], 64)
+    ts(T.rep[:], mat("one")[:, 0::16], c_rep, None, ALU.mult, None, ["one", "c_rep"], ["rep"], 64)
     for nm, src, key in (("u16", T.ub, "ub"), ("v16", T.vb, "vb")):
-        op("V", lambda nm=nm, src=src: V.tensor_tensor(mat(nm), src[:].indirect(T.rep[:]), mat("one16"), ALU.mult),
-           [key, "rep", "one16"], [nm], ("gV", 128))
-    uk, vk = ["u16"], ["v16"]
-    line("A", mat("nu2k"), mat("u16"), -128.0, 0.0, uk, ["nu2k"], ew(64), ew(128), "nu2k")
-    line("A", mat("v2k"), mat("v16"), 128.0, 0.0, vk, ["v2k"], ew(64), ew(128), "v2k")
+        ms(src[:, 0:16], 0.0, [key + "0"], 64)
+        line("A", mat(nm), src[:].indirect(T.rep[:]), 16.0, 0.0, [key, key + "0", "rep"], [nm], ("gV", 128),
+             ("gA", 128), nm)
+    line("A", mat("v2k"), mat("v16"), 128.0, 0.0, ["v16"], ["v2k"], ew(64), ew(128), "v2k")
 
-    def slot(t, c):
-        w, b = CH[c], 3 * (t * LN + I0[c])
-        x, y, z = T.lb[:, b:b + w], T.lb[:, b + w:b + 2 * w], T.lb[:, b + 2 * w:b + 3 * w]
-        lo, hi = T.lb[:, b:b + 2 * w], T.lb[:, b + w:b + 3 * w]
-        return (z, y, x, hi, lo) if t % 2 == 0 else (x, y, z, lo, hi)
-
-    def halves(buf, t, c):
-        w, b = CH[c], 2 * (t * LN + I0[c])
-        x, y = buf[:, b:b + w], buf[:, b + w:b + 2 * w]
-        return (x, y, buf[:, b:b + 2 * w]) if t % 2 == 0 else (y, x, buf[:, b:b + 2 * w])
-
-    ts(T.sqi[:], T.posi[:], 63, None, ALU.bitwise_and, None, ["posi"], ["sqi"], LN)
     ts(T.kqi[:], T.posi[:], 960, None, ALU.bitwise_and, None, ["posi"], ["kqi"], LN)
     op("V", lambda: V.tensor_copy(T.kq[:, 0:LN], T.kqi[:]), ["kqi"], ["kq0"], ew(LN))
-    for c in range(NC):
-        q, dead = slot(0, c)[0:2]
-        a, b = I0[c], I0[c] + CH[c]
-        ts(q, T.sqi[:, a:b], 64.0, 1.0 / 32, ALU.add, ALU.mult, ["sqi"], ["sq0_%d" % c], 64)
-        ts(dead, T.posi[:, a:b], 64.0, None, ALU.is_lt, None, ["posi"], ["dead0_%d" % c], 64)
+    ts(T.qa[:], T.posi[:], -1.0 / 4096, None, ALU.mult, None, ["posi"], ["qa"], LN)
+    ts(T.qb[:], T.posi[:], 64.0, None, ALU.is_lt, None, ["posi"], ["qb"], LN)
+    tt(T.q[:, 0:LN], T.qa[:], T.qb[:], ALU.add, ["qa", "qb"], ["q0_%d" % c for c in range(NC)], ew(2 * LN))
 
     def kq_masks(src):
         r = T.rank_of(src)
@@ -292,8 +258,8 @@ def build(g, core, T, topo, pick=None):
             d = cores[(rank + t) % N]
             rid, pid = topo.addr(d)[0:2]
             g.remote_dma(T.kq[:, t * LN:(t + 1) * LN], T.kq[:, 0:LN], T.sem["kq%d" % t], T.sem.sent, pid, rid, mk[d])
-        return None
-    op("P", send_kq, ["kq0", tabk[-1], "stp"], ["kqsent"], ("remote", 4), "sent", sum(popcount(m) for m in kq_masks(core).values()))
+    op("P", send_kq, ["kq0", "tab", "stp"], ["kqsent"], ("remote", 4), "sent",
+       sum(popcount(m) for m in kq_masks(core).values()))
     for t in range(1, PL):
         src = cores[(rank - t) % N]
         op("X", None, ["kqsent"], ["kq%d" % t], ("none",), "kq%d" % t, popcount(kq_masks(src)[core]), lat="remote")
@@ -304,80 +270,47 @@ def build(g, core, T, topo, pick=None):
     def ply(t, c):
         w, i0 = CH[c], I0[c]
         cur[0] = c
-        k = w // 16
         B = lambda s: T["%s%d" % (s, c)]
         K = lambda s: "%s%d" % (s, c)
         KT = lambda s: "%s%d_%d" % (s, t, c)
-        E = lambda s: CFG[s][t]
-        o = shift[c]
-        q, dead, nq, _, sent = slot(t, c)
-        up, hit, src2 = halves(T.s2, t, c)
-        wr, hit2, src3 = halves(T.s3, t, c)
-        kq = T.kq[:, t * LN + i0:t * LN + i0 + w]
-        kqk = "kq%d" % t
-        bb, off, idx = B("bb")[:, 0:w], B("off")[:, 0:k], B("idx")
-        lf, eq = B("lf")[:, 0:w], B("eq")[:, 0:w]
-        sv, mv, y = B("sv")[:, 0:w], B("mv")[:, 0:w], B("yp")[:, 64:64 + w]
+        q, nq, up, hit, kq = (T[s][:, t * LN + i0:t * LN + i0 + w] for s in ("q", "nq", "up", "hit", "kq"))
+        qk, kk = KT("q"), "kq%d" % t
+        off, idx, dsc = B("off")[:, 0:w // 16], B("idx"), B("dsc")[:, 0:w]
+        lf, of, eq, sv, y = B("lf")[:, 0:w], B("of")[:, 0:w], B("eq")[:, 0:w], B("sv")[:, 0:w], B("yp")[:, 64:64 + w]
         ca, cc = T.ca[:, 8 * i0:8 * (i0 + w)], T.cc[:, 8 * i0:8 * (i0 + w)]
         ones = T.ones[:, 0:w]
         tag = "%d.%d " % (t, c)
-        term = lambda out, m, r: (out, mat(m), r, 64)
         ps = lambda s, n=w: T[BK[s]][:, 0:n]
 
-        if E("off") == "E":
-            po = ps("off", k)
-            mm(BK["off"], [([(po, mat("I"), T.c128[:, 0:k], 64)], ["I", "c128"]),
-                           ([(po, T.base[:, 16 - r:144 - r], q[:, r:w:16], 64) for r in range(16)],
-                            ["base", "base0", KT("sq")])], tag + "mm_off")
-            ts(off, po, c_r8, -o / 8 - 0.4375, ALU.add, ALU.add, [BK["off"], "c_r8"], [K("off")], 64, [BK["off"]],
-               tag + "off")
-        else:
-            po, dsc = ps("off"), B("dsc")
-            mm(BK["off"], [([term(po, "I", T.dgm[:, 0:w])], ["I", "dgm"]),
-                           ([term(po, "k4", q)], ["k4", KT("sq")])], tag + "mm_off")
-            op("V", lambda: V.tensor_tensor_scan(dsc[:, 0:w], T.rst[:, 0:w], po, 0.0, ALU.add, ALU.max),
-               ["rst", BK["off"]], [K("dsc")], ew(w), bank=[BK["off"]], name=tag + "dsc")
-            ts(off, dsc[:, 15:w:16], -o / 8 - 0.4375, None, ALU.add, None, [K("dsc")], [K("off")], 64,
-               name=tag + "off")
-        line(E("bb"), bb, q, 4.0, 191.5625 - o / 8, [KT("sq")], [K("bb")], ew(64), ew(64), tag + "bb")
-        lsum = lambda out: [term(out, "I", kq), term(out, "I32", q), term(out, "nBIG", dead)]
-        lk = ["I", "I32", "nBIG", KT("sq"), KT("dead"), kqk]
-        pl, zo, zl = ps("L"), ps("ZO"), ps("ZL")
-        mm(BK["L"], [(lsum(pl), lk)], tag + "mm_L")
-        relu(E("lf"), lf, pl, -o, [BK["L"]], [K("lf")], w, [BK["L"]], tag + "lf")
-        zpre = [(lsum(zl), lk), ([term(zl, "kb", bb)], ["kb", K("bb")])]
-        if t > 0:
-            of = B("oh")[:, 0:w]
-            either(tag + "of", E("of"), lambda: V.tensor_copy(of, cc.indirect(off)),
+        mm("off", [([("I", T.dgm[:, 0:w]), ("k8", kq)], ["dgm", kk]), ([("q8", q)], [qk])], tag + "mm_off", w)
+        op("V", lambda: V.tensor_tensor_scan(dsc, T.rst[:, 0:w], ps("off"), 0.0, ALU.add, ALU.max),
+           ["rst", BK["off"]], [K("dsc")], ew(w), bank=[BK["off"]], name=tag + "dsc")
+        line("V", off, dsc[:, 15::16], 1.0, -0.4375, [K("dsc")], [K("off")], ew(64), ew(64), tag + "off")
+        either(tag + "lf", "A", lambda: V.tensor_scalar(lf, q, -4096.0, 0.0, ALU.mult, ALU.max),
+               lambda: A.activation(lf, q, AF.Relu, scale=-4096.0), [qk], [K("lf")], ew(64), ew(64))
+        bucket = [([("k128", kq), ("n448", ones)], [kk, "ones"]), ([("q128", q), ("C33", ones), ("nC33", ones)], [qk])]
+        same = [([("nBIG", eq)], [K("eq")])] if t else []
+        if t:
+            either(tag + "of", "A", lambda: V.tensor_copy(of, cc.indirect(off)),
                    lambda: A.activation(of, cc.indirect(off), AF.Identity), [K("cc"), K("off")], [K("of")],
                    ("gV", w), ("gA", w))
-            oterm = ([term(zo, "I", of)], ["I", K("of")])
-            op("V", lambda: V.tensor_tensor(eq, cc.indirect(off), lf, ALU.is_equal),
-               [K("cc"), K("off"), K("lf")], [K("eq")], ("gV", w), name=tag + "eq")
-            mm(BK["ZO"], [([term(zo, "kb", bb)], ["kb", K("bb")]), oterm,
-                          ([term(zo, "nBIG", eq)], ["nBIG", K("eq")])], tag + "mm_ZO")
-            mm(BK["ZL"], zpre + [([term(zl, "nBIG", eq)], ["nBIG", K("eq")])], tag + "mm_ZL")
-            relu("A", idx[:, 0:w], zo, -196608.0, [BK["ZO"]], [K("idxO")], w, [BK["ZO"]], tag + "idxO")
-        else:
-            mm(BK["ZL"], zpre, tag + "mm_ZL")
-        relu("V", idx[:, 64:64 + w], zl, -196608.0 - o, [BK["ZL"]], [K("idxL")], w, [BK["ZL"]], tag + "idxL")
-        keys = lambda s, h, a, b: ["%s%s%d_%d" % (s, h, c, j) for j in range(a // 2, (b + 1) // 2)]
+            tt(eq, cc.indirect(off), lf, ALU.is_equal, [K("cc"), K("off"), K("lf")], [K("eq")], ("gV", w),
+               name=tag + "eq")
+            mm("ZO", bucket + [([("I", of)], [K("of")])] + same, tag + "mm_ZO", w)
+            relu("A", idx[:, 0:w], ps("ZO"), 0.0, [BK["ZO"]], [K("idxO")], w, [BK["ZO"]], tag + "idxO")
+        mm("ZL", bucket + [([("I", lf)], [K("lf")])] + same, tag + "mm_ZL", w)
+        relu("V", idx[:, 64:64 + w], ps("ZL"), 0.0, [BK["ZL"]], [K("idxL")], w, [BK["ZL"]], tag + "idxL")
+        keys = lambda s, h, a, b: ["%s%s%d_%d" % (s, h, c, j) for j in range(a // 8, (b + 7) // 8)]
         for h, text in zip("OL", CFG["cut"][t][c].split("|")):
             x0, sign = (32 * i0, -1.0) if h == "O" else (32 * i0 + 16 * w, 1.0)
             G, R = T.gb[:, x0:x0 + 16 * w], T.rb[:, x0:x0 + 16 * w]
-            H, hk = T.hb[:, x0:x0 + 16 * w] if t else T.h0[:, 0:16 * w], keys("h", h, 0, w)
+            H, hk = (T.hb[:, x0:x0 + 16 * w], K("hb" + h)) if t else (T.h0[:, 0:16 * w], "h0")
             if t and h == "O":
-                if CFG["acc"]:
-                    line("A", H[:, 0::16], ca.indirect(off), 1.0, 512.0, [K("ca"), K("off"), K("hb")], hk,
-                         ("gV", w), ("gA", w), tag + "a0")
-                else:
-                    ts(H[:, 0::16], ca.indirect(off), 0.0, 512.0, ALU.max, ALU.add, [K("ca"), K("off"), K("hb")], hk,
-                       ("gV", w), name=tag + "a0")
+                line("A", H[:, 0::16], ca.indirect(off), 1.0, 512.0, [K("ca"), K("off")], [hk], ("gV", w), ("gA", w),
+                     tag + "a0")
             elif t:
-                for a, b in CFG["link"]:
-                    a, b = a * w // 64, b * w // 64
-                    ts(H[:, 16 * a:16 * b:16], RO[:, 16 * a + 15:16 * b:16], 0.0, 512.0, ALU.max, ALU.add,
-                       keys("r", "O", a, b) + [K("hb")], keys("h", h, a, b), 64, name=tag + "link")
+                ts(H[:, 0::16], RO[:, 15::16], 0.0, 512.0, ALU.max, ALU.add, keys("r", "O", 0, w), [hk], 64,
+                   name=tag + "link")
             RO, a0, x1 = R, 0, 64 * (h == "L")
             for e, a, b, dot in pieces(text):
                 line(e, G[:, 16 * a:16 * b], T.tab[:].indirect(idx[:, x1 + a:x1 + b]), sign, -32.0,
@@ -387,81 +320,57 @@ def build(g, core, T, topo, pick=None):
                     a, a0 = a0, b
                     op("V", lambda a=a, b=b, G=G, R=R, H=H: V.tensor_tensor_scan(
                         R[:, 16 * a:16 * b], H[:, 16 * a:16 * b], G[:, 16 * a:16 * b], 0.0, ALU.max, ALU.add),
-                       keys("g", h, a, b) + (keys("h", h, a, b) if t else ["h0"]), keys("r", h, a, b),
-                       ew((b - a) * 8), name=tag + "scan" + h)
-        rk = keys("r", "L", 0, w)
-        acc = R[:, 15::16]
-        ts(y, acc, 0.0, 127.0, ALU.max, ALU.min, rk, [K("yp")], 64, name=tag + "y")
-        op("V", lambda: V.tensor_copy(cc.indirect(off), lf), [K("lf"), K("off")], [K("cc")], ("sV", w),
-           name=tag + "scL")
-        if CFG["acc"]:
-            relu("A", B("acc")[:, 0:w], acc, 0.0, rk, [K("acc")], w, name=tag + "acc")
-            acc, rk = B("acc")[:, 0:w], [K("acc")]
-        op("V", lambda: V.tensor_copy(ca.indirect(off), acc), rk + [K("off")], [K("ca")], ("sV", w),
-           name=tag + "scA")
-        if t == PL - 1:
-            if not CFG["acc"]:
-                relu("A", ca, ca, 0.0, [K("ca")], [K("ca")], 8 * w, name=tag + "clamp")
-            for dst, src, key in ((T.yc, cc, K("cc")), (T.ya, ca, K("ca"))):
-                op("S", lambda dst=dst, src=src: g.sync.dma_start(dst[:, 8 * i0:8 * (i0 + w)], src),
-                   [key, "sq%d_%d" % (t, NC - 1)], [], ("dma",), "st", 16, lat="copy")
-        st, mx, mf = ps("ST", 128), B("mx"), B("mf")
-        mm(BK["ST"], [([(st, mat("I"), mat("tie"), 128), (T[BK["ST"]][0:w, 0:128], dead, mat("nBIG"), 128)],
-                       ["I", "tie", "nBIG", KT("dead")]),
-                      ([(st, B("yp")[:, 64:192], mat("u16"), 128), (st, B("yp")[:, 0:128], mat("v16"), 128)],
-                       [K("yp")] + uk + vk)], tag + "mm_S")
+                       keys("g", h, a, b) + [hk], keys("r", h, a, b), ew((b - a) * 8), name=tag + "scan" + h)
+        rk, acc = keys("r", "L", 0, w), B("acc")[:, 0:w]
+        ts(y, R[:, 15::16], 0.0, 127.0, ALU.max, ALU.min, rk, [K("yp")], 64, name=tag + "y")
+        relu("A", acc, R[:, 15::16], 0.0, rk, [K("acc")], w, name=tag + "acc")
+        for dst, src, key, out in ((cc, lf, "lf", T.yc), (ca, acc, "acc", T.ya)):
+            ck = K("cc" if key == "lf" else "ca")
+            op("V", lambda dst=dst, src=src: V.tensor_copy(dst.indirect(off), src), [K(key), K("off")], [ck],
+               ("sV", w), name=tag + "sc_" + key)
+            if t == PL - 1:
+                op("S", lambda dst=dst, out=out: g.sync.dma_start(out[:, 8 * i0:8 * (i0 + w)], dst),
+                   [ck, "q%d_%d" % (t, NC - 1)], [], ("dma",), "st", 16, lat="copy")
+        st, mx, mf, yp = ps("ST", 128), B("mx"), B("mf"), B("yp")
+        top = T[BK["ST"]][0:w, 0:128]
+        mm("ST", [([(st, mat("I"), mat("tie"), 128), (top, lf, mat("n4k"), 128), (top, q, mat("nBIG"), 128)],
+                   ["I", "tie", "n4k", "nBIG", qk, K("lf")]),
+                  ([(st, yp[:, 64:192], mat("u16"), 128), (st, yp[:, 0:128], mat("v16"), 128)],
+                   [K("yp"), "u16", "v16"])], tag + "mm_S")
         op("V", lambda: V.tensor_tensor_scan(mx[:], T.rst[:], st, 0.0, ALU.add, ALU.max), ["rst", BK["ST"]],
            [K("mx")], ew(128), bank=[BK["ST"]], name=tag + "max")
         op("V", lambda: V.tensor_tensor_scan(mf[:, ::-1], T.rst[:], mx[:, ::-1], 0.0, ALU.add, ALU.max),
            ["rst", K("mx")], [K("mf")], ew(128), name=tag + "mf")
-        e1, e2 = ps("E1"), ps("E2")
-        mm(BK["E1"], [([term(e1, "dtie", ones), term(e1, "pHUGE", dead)], ["dtie", "ones", "pHUGE", KT("dead")]),
-                      ([term(e1, "nu2k", y)], ["nu2k", K("yp")]),
-                      ([(e1, mf[:], T.idm[:, 0:w], 256)], ["idm", K("mf")])], tag + "mm_E1")
-        mm(BK["E2"], [([term(e2, "v2k", y)], ["v2k", K("yp")]),
-                      ([(e2, mf[:], T.idm[:, 64:64 + w], 256)], ["idm", K("mf")])], tag + "mm_E2")
-        op("V", lambda: V.tensor_tensor(nq, e1, q, ALU.min), [BK["E1"], KT("sq")], [KT("nq")], ew(w),
-           bank=[BK["E1"]], name=tag + "nq")
-        relu(E("sv"), sv, e2, c_step, [BK["E2"], "c_step"], [K("sv")], w, [BK["E2"]], tag + "sv")
-        ex, ez = ps("X"), ps("Z")
-        for out, bank, m0, m1 in ((ex, "X", "oneI32", "none32"), (ez, "Z", "I32", "nI64")):
-            mm(BK[bank], [([term(out, m0, q)], [m0, KT("sq")]),
-                          ([term(out, m1, nq)], [m1, KT("nq")]),
-                          ([term(out, "one", sv)], ["one", K("sv")])], tag + "mm_" + bank)
-        ts(hit, ex, c_hit, None, ALU.is_equal, None, [BK["X"], "c_hit"], [KT("hit")], w, [BK["X"]], tag + "h1")
-        ts(hit2, ex, c_h2, None, ALU.is_equal, None, [BK["X"], "c_h2"], [KT("hit2")], w, [BK["X"]], tag + "h2")
-        if either(tag + "up", E("up"),
-                  lambda: [V.tensor_scalar(up, ez, 1.0 / 32, 0.0, ALU.mult, ALU.max),
-                           V.tensor_scalar(wr, ez, 64.0 + o, -2.0, ALU.is_ge, ALU.mult)],
-                  lambda: [A.activation(up, ez, AF.Relu, scale=1.0 / 32),
-                           A.activation(wr, ez, AF.Sign, scale=-1.0, bias=63.5 + o)],
-                  [BK["Z"]], [KT("up")], ("two", w), ("two", w), [BK["Z"]], 2) == "A":
-            shift[c] += 32
-        four = [KT("hit"), KT("hit2"), KT("up")]
+        e1, e2, ex = ps("E1"), ps("E2"), ps("X")
+        mm("E1", [([("dtie", ones), ("n4k", lf), ("nBIG", q)], ["ones", qk, K("lf")]), ([("u16", y)], [K("yp")]),
+                  ([(e1, mf[:], T.idm[:, 0:w], 256)], ["idm", K("mf")])], tag + "mm_E1", w)
+        mm("E2", [([("v2k", y)], [K("yp")]), ([(e2, mf[:], T.idm[:, 64:64 + w], 256)], ["idm", K("mf")])],
+           tag + "mm_E2", w)
+        tt(nq, e1, q, ALU.max, [BK["E1"], qk], [KT("nq")], ew(w), [BK["E1"]], tag + "nq")
+        relu("A", sv, e2, c_step, [BK["E2"], "c_step"], [K("sv")], w, [BK["E2"]], tag + "sv")
+        mm("X", [([("one3", q), ("n3unit", lf), ("half", ones), ("unit", kq)], [qk, kk, "ones", K("lf")]),
+                 ([("none", nq)], [KT("nq")]),
+                 ([("nstep", sv), ("C17", ones), ("nC17", ones), ("none", q), ("stay", nq), ("step", sv)],
+                  [K("sv")])], tag + "mm_X", w)
+        op("V", lambda: [V.tensor_tensor(hit, ex, q, ALU.is_equal),
+                         V.tensor_scalar(up, ex, -1.0, 0.0, ALU.mult, ALU.min)],
+           [BK["X"], qk], [KT("up")], ("two", w), inc=2, bank=[BK["X"]], name=tag + "up")
         if t < PL - 1:
-            land = slot(t + 1, c)[3]
-            ar = "ar%d_%d" % (t + 1, c)
+            land, ar = T.q[:, (t + 1) * LN + i0:(t + 1) * LN + i0 + w], "ar%d_%d" % (t + 1, c)
 
             def hop():
                 g.remote_dma_fused([RemoteDMATransfer(
                     dst_ids=[DstId(rid=rid_n, pnc=pid_n)], dma_engine_mask=m_out, remote_sem=T.sem[ar],
-                    srcs=[sent, src2, src3], dsts=[land], alu_op=1)], local_sem=T.sem.sent)
-                return None
-            op("P", hop, [KT("nq"), KT("dead")] + four, [KT("hop")], ("remote", 1), "sent", popcount(m_out),
-               name=tag + "hop")
-            op("X", None, [KT("hop")], ["sq%d_%d" % (t + 1, c), "dead%d_%d" % (t + 1, c)], ("none",), ar,
-               popcount(m_in), lat="remote")
+                    srcs=[nq, up, hit], dsts=[land], alu_op=1)], local_sem=T.sem.sent)
+            op("P", hop, [KT("nq"), KT("up")], [KT("hop")], ("remote", 1), "sent", popcount(m_out), name=tag + "hop")
+            op("X", None, [KT("hop")], ["q%d_%d" % (t + 1, c)], ("none",), ar, popcount(m_in), lat="remote")
         else:
-            ey = ps("Y")
-            mm(BK["Y"], [([term(ey, "I", kq), term(ey, "nBIG", dead), term(ey, "I32", nq)], lk + [KT("nq")]),
-                         ([term(ey, "nBIG", hit), term(ey, "nBIG", hit2), term(ey, "I32", up), term(ey, "I32", wr)],
-                          four)], tag + "mm_Y")
+            mm("Y", [([("n4k", nq)], [KT("nq")]), ([("n4k", up), ("n4k", hit)], [KT("up")])], tag + "mm_Y", w)
             yo = T.ylf[:, i0:i0 + w]
-            relu(CFG["yl"], yo, ey, -shift[c], [BK["Y"]], [K("ylf")], w, [BK["Y"]], tag + "yl")
+            relu("A", yo, ps("Y"), 0.0, [BK["Y"]], [K("ylf")], w, [BK["Y"]], tag + "yl")
             op("S", lambda: g.sync.dma_start(T.yl[:, i0:i0 + w], yo), [K("ylf")], [], ("dma",), "st", 16,
                lat="small")
 
-    shift = [64.0] * NC
     for t in range(PL):
         for c in range(NC):
             ply(t, c)
@@ -569,15 +478,23 @@ def arrange(ops, deps, e):
     return order
 
 
-def refine(ops, deps, order, models, steps, hot=0.15, cold=0.03, seed=2, turn=0.2):
+def refine(ops, deps, order, models, steps, hot=0.1, cold=0.02, seed=10, turn=0.3):
     n = len(ops)
     rnd = np.random.RandomState(seed).random_sample(4 * steps).tolist()
     eng = ["VAEPSX".index(o["eng"]) for o in ops]
+    above, near = [], []
+    for j in range(n):
+        far = 0
+        for d in deps[j]:
+            far |= above[d]
+        near.append([d for d in deps[j] if not far >> d & 1])
+        above.append(far | sum(1 << d for d in near[j]))
+    deps = near
     succ = [[] for _ in range(n)]
     for j in range(n):
         for d in deps[j]:
             succ[d].append(j)
-    last = [j for j in range(n) if not succ[j]]
+    last = [j for j in range(n) if ops[j]["eng"] == "S" and not succ[j]]
     tabs = [([busy(o, e) for o in ops], [[(d, gap(ops[d], ops[j], e)) for d in deps[j]] for j in range(n)],
              [latency(o, e) for o in ops]) for e in models]
     both = {j: [[busy(dict(o, eng=q, cost=o["both"][q]), e) for e in models] for q in "VA"]
@@ -590,18 +507,18 @@ def refine(ops, deps, order, models, steps, hot=0.15, cold=0.03, seed=2, turn=0.
             tab[0][j] = d
 
     def run(order, a, ends, most=1e9):
-        out, total = [], 0.0
-        for (dur, pre, tail), old in zip(tabs, ends):
-            if total - sum(max(e[j] + tb[2][j] for j in last) for tb, e in zip(tabs, ends[:len(out)])) > most:
-                return 1e9, None
-            end, free, seen = old[:], [0.0] * 6, set()
-            for j in order[a - 1::-1] if a else []:
-                if eng[j] not in seen:
-                    seen.add(eng[j])
-                    free[eng[j]] = end[j]
-                    if len(seen) == 6:
-                        break
-            for j in order[a:]:
+        out, worse, ahead, seen, rest = [], 0.0, [], set(), order[a:]
+        for j in order[a - 1::-1] if a else []:
+            if eng[j] not in seen:
+                seen.add(eng[j])
+                ahead.append(j)
+                if len(seen) == 6:
+                    break
+        for (dur, pre, tail), (was, old) in zip(tabs, ends):
+            end, free = old[:], [0.0] * 6
+            for j in ahead:
+                free[eng[j]] = end[j]
+            for j in rest:
                 q = eng[j]
                 t = free[q] if q < 5 else 0.0
                 for d, x in pre[j]:
@@ -609,9 +526,11 @@ def refine(ops, deps, order, models, steps, hot=0.15, cold=0.03, seed=2, turn=0.
                     if x > t:
                         t = x
                 end[j] = free[q] = t + dur[j]
-            out.append(end)
-            total += max(end[j] + tail[j] for j in last)
-        return total / len(tabs), out
+            out.append((max(end[j] + tail[j] for j in last), end))
+            worse += out[-1][0] - was
+            if worse > most + (0.1 if len(out) < len(tabs) else 0.0):
+                return None
+        return out
 
     def meets(order, m, end):
         dur, pre, tail = tabs[m]
@@ -629,44 +548,41 @@ def refine(ops, deps, order, models, steps, hot=0.15, cold=0.03, seed=2, turn=0.
                 j = next((d for d, x in pre[j] if end[d] + x >= t), None)
         return out
 
-    cur, ends = run(order, 0, [[0.0] * n] * len(tabs))
-    best, pairs = (cur, order, eng[:]), []
+    ends = run(order, 0, [(0.0, [0.0] * n)] * len(tabs))
+    best, pairs = (1e9, order, eng[:]), []
     for s in range(steps):
         x0, x1, x2, x3 = rnd[4 * s:4 * s + 4]
         if not pairs:
             m = int(x0 * len(tabs))
-            pairs = meets(order, m, ends[m])
+            pairs = meets(order, m, ends[m][1])
         i, j = pairs[int(x1 * len(pairs))]
-        room = -math.log(x3) * hot * (cold / hot) ** (s / steps)
+        room = -math.log(x3) * hot * (cold / hot) ** (s / steps) * len(tabs)
         if x2 < turn:
             c = movable[int(x1 * len(movable))] if x2 < turn / 6 else i if x2 < turn / 2 else j
-            if c in both:
+            if c not in both:
+                continue
+            flip(c)
+            new, e2 = order, run(order, order.index(c), ends, room)
+            if e2 is None:
                 flip(c)
-                v, e2 = run(order, order.index(c), ends, room * len(tabs) + 0.1)
-                if v < cur + room:
-                    cur, ends, pairs = v, e2, []
-                    if v < best[0]:
-                        best = (v, order, eng[:])
-                else:
-                    flip(c)
-            continue
-        a, b = order.index(i), order.index(j) + 1
-        seg = order[a:b]
-        up = x2 < (1 + turn) / 2
-        need = {j if up else i}
-        for x in (seg[::-1] if up else seg):
-            if x in need:
-                need.update(deps[x] if up else succ[x])
-        if (i if up else j) in need:
-            pairs.remove((i, j))
-            continue
-        new = order[:a] + [x for x in seg if (x in need) == up] + [x for x in seg if (x in need) != up] + order[b:]
-        v, e2 = run(new, a, ends, room * len(tabs) + 0.1)
-        if v < cur + room:
-            order, cur, ends, pairs = new, v, e2, []
-            if v < best[0]:
-                best = (v, new, eng[:])
-        elif x3 > 0.9:
+        else:
+            a, b = order.index(i), order.index(j) + 1
+            seg = order[a:b]
+            up = x2 < (1 + turn) / 2
+            need = {j if up else i}
+            for x in (seg[::-1] if up else seg):
+                if x in need:
+                    need.update(deps[x] if up else succ[x])
+            if (i if up else j) in need:
+                pairs.remove((i, j))
+                continue
+            new = order[:a] + [x for x in seg if (x in need) == up] + [x for x in seg if (x in need) != up] + order[b:]
+            e2 = run(new, a, ends, room)
+        if e2 is not None:
+            order, ends, pairs = new, e2, []
+            if sum(x[0] for x in ends) < best[0]:
+                best = (sum(x[0] for x in ends), order, eng[:])
+        elif x0 > 0.9:
             pairs = []
     return best[1], {ops[j]["name"]: "VA"[best[2][j]] for j in movable}
 

import math
import numpy as np
from concourse.bass import DstId, RemoteDMATransfer
from concourse.mybir import AluOpType as ALU, ActivationFunctionType as AF

N, LN, PL = 6, 192, 5
CFG = dict(
    ch=[64, 64, 64],
    cut=[["|A32.V32."] * 3] + [["A32.V32.|A32.A32."] * 3] * 4,
    banks=dict(off="b0", ZO="b2", ZL="b3", ST="b4", E1="b5", E2="b6", X="b7", Y="b1"))
BIG = float(2 ** 24)
SCALED = dict(nBIG=("I", -BIG), n4k=("I", -4096.0), C17=("I", 1.5 * 2 ** 17), nC17=("I", -1.5 * 2 ** 17),
              C33=("I", 1.5 * 2 ** 33), nC33=("I", -1.5 * 2 ** 33), n448=("I", -448.0), half=("I", 31.5 / 4096),
              unit=("I", 1.0 / 4096), n3unit=("I", -3.0 / 4096), n3=("I", -3.0), none=("one", -1.0),
              step=("one", 1.0 / 4096), nstep=("one", -1.0 / 4096), k8=("king", -1.0 / 8), q8=("king", -512.0),
              k128=("king", -128.0), q128=("king", -128.0 * 4096))
MATS = ["I", "one", "king", "stay", "one3", "dtie", "tie", "u16", "v16", "v2k"] + list(SCALED)
MAXC = 4

SCRATCH = {
    "tab": ("sbuf", [128, 8192], "bfloat16"),
    "posi": ("sbuf", [128, LN], "int32"),
    "kqi": ("sbuf", [128, LN], "int32"),
    "qa": ("sbuf", [128, LN], "float16"),
    "qb": ("sbuf", [128, LN], "float16"),
    "ub": ("sbuf", [128, 32], "bfloat16"),
    "vb": ("sbuf", [128, 32], "bfloat16"),
    "stp": ("sbuf", [128, 8], "int32"),
    "pc": ("sbuf", [128, 8], "int32"),
    "rc": ("sbuf", [128, 8], "int32"),
    "col": ("sbuf", [128, 8], "float32"),
    "rep": ("sbuf", [128, 8], "uint16"),
    "d1": ("sbuf", [128, 128], "int32"),
    "d2": ("sbuf", [128, 128], "int32"),
    "d3": ("sbuf", [128, 128], "int32"),
    "d4": ("sbuf", [128, 64], "int32"),
    "d5": ("sbuf", [128, 64], "int32"),
    "d6": ("sbuf", [128, 64], "float32"),
    "dgm": ("sbuf", [128, 64], "bfloat16"),
    "x8": ("sbuf", [128, 64], "bfloat16"),
    "mat": ("sbuf", [128, 128 * len(MATS)], "bfloat16"),
    "idm": ("sbuf", [128, 128], "float32"),
    "ones": ("sbuf", [128, 64], "bfloat16"),
    "rst": ("sbuf", [128, 128], "float32"),
    "ramp": ("sbuf", [128, 128], "int32"),
    "ca": ("sbuf", [128, 8 * LN], "float32"),
    "cc": ("sbuf", [128, 8 * LN], "float32"),
    "q": ("sbuf", [128, PL * LN], "float16"),
    "nq": ("sbuf", [128, PL * LN], "float16"),
    "up": ("sbuf", [128, PL * LN], "float16"),
    "hit": ("sbuf", [128, PL * LN], "float16"),
    "kq": ("sbuf", [128, PL * LN], "bfloat16"),
    "ylf": ("sbuf", [128, LN], "float32"),
    "h0": ("sbuf", [128, 1024], "float16"),
    "hb": ("sbuf", [128, LN * 32], "float16"),
    "gb": ("sbuf", [128, LN * 32], "bfloat16"),
    "rb": ("sbuf", [128, LN * 32], "float16"),
}
for _b in range(8):
    SCRATCH["b%d" % _b] = ("psum", [128, 512], "float32")
for _c in range(MAXC):
    SCRATCH.update({
        "acc%d" % _c: ("sbuf", [128, 64], "float16"),
        "dsc%d" % _c: ("sbuf", [128, 64], "float32"),
        "off%d" % _c: ("sbuf", [128, 8], "uint16"),
        "idx%d" % _c: ("sbuf", [128, 128], "uint16"),
        "lf%d" % _c: ("sbuf", [128, 64], "float16"),
        "of%d" % _c: ("sbuf", [128, 64], "float16"),
        "eq%d" % _c: ("sbuf", [128, 64], "bfloat16"),
        "yp%d" % _c: ("sbuf", [128, 192], "bfloat16"),
        "mx%d" % _c: ("sbuf", [128, 128], "float32"),
        "mf%d" % _c: ("sbuf", [128, 128], "float32"),
        "sv%d" % _c: ("sbuf", [128, 64], "bfloat16"),
    })

SEMAPHORES = (["V", "A", "P", "E", "lpos", "lu", "lv", "lstp", "ltab", "st", "sent"]
              + ["kq%d" % t for t in range(1, PL)]
              + ["ar%d_%d" % (t, c) for t in range(1, PL) for c in range(MAXC)])

EST = dict(cyc=0.00083, fix=0.02, fixa=0.03, r=1.56, sc=3.8, pe=0.00061, hop=0.2, same=0.2, remote=2.3, issue=0.5,
           load0=2.0, load=5.0, small=2.2, copy=3.2, slack=0.15, lag=2.6)
MODELS = [dict(r=1.3, sc=3.0, remote=1.9),
          dict(cyc=0.0009, pe=0.00066, r=1.4, sc=3.4, hop=0.25, same=0.25, remote=2.8, issue=0.6),
          dict(cyc=0.00114, pe=0.00084, r=1.8, sc=4.4, hop=0.22, same=0.22, fixa=0.04, fix=0.03)]
STEPS = 75000


def popcount(m):
    return bin(m).count("1")


def pieces(text):
    out, a, j = [], 0, 0
    while j < len(text):
        e, k = text[j], j + 1
        while k < len(text) and text[k].isdigit():
            k += 1
        b = a + int(text[j + 1:k])
        dot = k < len(text) and text[k] == "."
        out.append((e, a, b, dot))
        a, j = b, k + dot
    return out


def build(g, core, T, topo, pick=None):
    ops, cur = [], [None]
    pick = pick or {}
    CH = CFG["ch"]
    NC = len(CH)
    I0 = [sum(CH[:c]) for c in range(NC)]
    rank = T.rank_of(core)
    cores = T.cores
    nxt, prv = cores[(rank + 1) % N], cores[(rank - 1) % N]
    V, A, PE = g.vector, g.scalar, g.tensor
    BK = CFG["banks"]

    def op(eng, fn, rd, wr, cost, sem=None, inc=1, bank=(), lat=None, name=""):
        ops.append(dict(eng=eng, fn=fn, rd=list(rd), wr=list(wr), cost=cost, sem=sem or eng, inc=inc,
                        bank=list(bank), lat=lat, name=name or (wr[0] if wr else ""), chunk=cur[0]))

    def ew(n):
        return ("ew", n)

    def mat(name):
        k = MATS.index(name)
        return T.mat[:, 128 * k:128 * (k + 1)]

    def mm(role, parts, name, n=None):
        bank = BK[role]
        for p, (terms, rd) in enumerate(parts):
            rd = list(rd) + [x[0] for x in terms if len(x) == 2]
            terms = [x if len(x) == 4 else (T[bank][:, 0:n], mat(x[0]), x[1], 64) for x in terms]

            def fn(p=p, terms=terms):
                last = None
                for j, (o, l, r, _) in enumerate(terms):
                    last = PE.matmul(o, l, r, p == 0 and j == 0, p == len(parts) - 1 and j == len(terms) - 1)
                return last
            op("E", fn, rd, [bank], ("pe", sum(x[3] for x in terms)), bank=[bank], name=name + str(p))

    def ts(out, in0, s1, s2, o0, o1, rd, wr, n, name=""):
        if o1 is None:
            op("V", lambda: V.tensor_scalar(out, in0, s1, None, o0), rd, wr, ew(n), name=name)
        else:
            op("V", lambda: V.tensor_scalar(out, in0, s1, s2, o0, o1), rd, wr, ew(n), name=name)

    def tt(out, in0, in1, alu, rd, wr, cost, bank=(), name=""):
        op("V", lambda: V.tensor_tensor(out, in0, in1, alu), rd, wr, cost, bank=bank, name=name)

    def either(name, first, on_v, on_a, rd, wr, cost_v, cost_a, bank=()):
        e = pick.get(name, first)
        op(e, on_v if e == "V" else on_a, rd, wr, cost_v if e == "V" else cost_a, bank=bank, name=name)
        ops[-1]["both"] = {"V": cost_v, "A": cost_a}

    def relu(first, out, in_, bias, rd, wr, n, bank=(), name=""):
        either(name, first, lambda: V.tensor_scalar(out, in_, bias, 0.0, ALU.add, ALU.max),
               lambda: A.activation(out, in_, AF.Relu, bias=bias), rd, wr, ew(n), ew(n), bank)

    def line(first, out, in_, scale, bias, rd, wr, cost_v, cost_a, name):
        either(name, first, lambda: V.tensor_scalar(out, in_, scale, bias, ALU.mult, ALU.add),
               lambda: A.activation(out, in_, AF.Identity, scale=scale, bias=bias), rd, wr, cost_v, cost_a)

    def ms(ap, val, wr, n):
        op("V", lambda: V.memset(ap, val), [], wr, ew(n))

    def iota(ap, pat, base, mult, wr, n):
        op("P", lambda: g.iota(ap, pat, base, mult, allow_small_or_imprecise_dtypes=True), [], wr, ("pool", n))

    op("A", lambda: A.dma_start(T.posi[:], T.pos[:]), [], ["posi"], ("dma",), "lpos", 16, lat="small")
    loads = [("ltab", T.tab[:, 1024 * b + 64:1024 * (b + 1)], T.feat[:, 1024 * b + 64:1024 * (b + 1)])
             for b in range(8)]
    loads += [("lu", T.ub[:, 16:32], T.u[:]), ("lv", T.vb[:, 16:32], T.v[:]), ("lstp", T.stp[:, 0:1], T.step[:])]

    def load_all():
        for sem, dst, src in loads:
            g.sync.dma_start(dst, src).then_inc(T.sem[sem], 16)
    op("S", load_all, [], ["loads"], ("none",), "st", 0)
    for key, sem, n, part in (("tab", "ltab", 8, 1.0), ("ub", "lu", 1, 1.05), ("vb", "lv", 1, 1.05),
                              ("stp", "lstp", 1, 1.05)):
        op("X", None, ["loads"], [key], ("none",), sem, 16 * n, lat=("load", part))
    for b in range(8):
        ms(T.tab[:, 1024 * b:1024 * b + 64], 0.0, ["tab%d" % b], 64)
    tabk = ["tab"] + ["tab%d" % b for b in range(8)]

    iota(T.d1[:], [[-1, 128]], 0, 1, ["d1"], 128)
    iota(T.d2[:], [[-16, 8], [0, 16]], 0, 1, ["d2"], 128)
    iota(T.pc[:, 0:1], [[0, 1]], 0, 1, ["pc"], 1)
    iota(T.ramp[:], [[0, 8], [-32, 16]], 512, 0, ["ramp"], 128)
    iota(T.d4[:], [[-1, 64]], 64, 1, ["d4"], 64)
    iota(T.x8[:], [[8, 64]], 0, 0, ["x8"], 64)
    iota(mat("tie"), [[0, 8], [-1, 16]], 15, 0, ["tie"], 128)
    iota(T.ones[:], [[0, 64]], 1, 0, ["ones"], 64)
    for c in range(NC):
        a, b = 8 * I0[c], 8 * (I0[c] + CH[c])
        ms(T["yp%d" % c][:], 0.0, ["yp%d" % c], 96)
        iota(T.cc[:, a:b], [[0, b - a]], 0, 0, ["cc%d" % c], b - a)
        iota(T.ca[:, a:b], [[0, b - a]], 0, 0, ["ca%d" % c], b - a)
    op("V", lambda: V.tensor_copy(T.h0[:, 0:128], T.ramp[:]), ["ramp"], ["h0"], ew(128))
    for n in (128, 256, 512):
        line("A", T.h0[:, n:2 * n], T.h0[:, 0:n], 1.0, 0.0, ["h0"], ["h0"], ew(n // 2), ew(n), "h0_%d" % n)
    for c in range(NC):
        for h in range(2):
            a, n = 32 * I0[c] + 16 * CH[c] * h, 16 * CH[c]
            line("A", T.hb[:, a:a + n], T.h0[:, 0:n], 1.0, 0.0, ["h0"], ["hb%s%d" % ("OL"[h], c)], ew(n // 2), ew(n),
                 "hb%d_%d" % (c, h))

    c_stay, c_step, c_tie, c_far, c_back, c_rep = (T.col[:, j:j + 1] for j in range(6))
    ts(mat("I"), T.d1[:], 0.0, None, ALU.is_equal, None, ["d1"], ["I"], 128)
    ts(mat("king"), T.d2[:], 0.0, None, ALU.is_equal, None, ["d2"], ["king"], 128)
    ts(T.d3[:], T.d2[:], 4, None, ALU.arith_shift_right, None, ["d2"], ["d3"], 128)
    ts(mat("one"), T.d3[:], 0.0, None, ALU.is_equal, None, ["d3"], ["one"], 128)
    for nm, (src, s) in SCALED.items():
        line("A", mat(nm), mat(src), s, 0.0, [src], [nm], ew(64), ew(128), nm)
    tt(mat("one3"), mat("one"), mat("n3"), ALU.add, ["one", "n3"], ["one3"], ew(256))
    ts(c_far, T.pc[:, 0:1], 64.0, -127.0, ALU.is_ge, ALU.mult, ["pc"], ["c_far"], 64)
    ts(c_back, c_far, -1.0, None, ALU.add, None, ["c_far"], ["c_back"], 64)
    ts(T.idm[:], mat("I"), c_back, None, ALU.mult, None, ["I", "c_back"], ["idm"], 128)
    ts(T.rc[:, 0:1], T.pc[:, 0:1], 15, None, ALU.bitwise_and, None, ["pc"], ["rc"], 64)
    ts(c_stay, T.rc[:, 0:1], 0.0, 2.0, ALU.is_equal, ALU.add, ["rc"], ["c_stay"], 64)
    ts(mat("stay"), mat("I"), c_stay, None, ALU.mult, None, ["I", "c_stay"], ["stay0"], 64)
    tt(mat("stay"), mat("stay"), mat("one"), ALU.add, ["stay0", "one"], ["stay"], ew(256))
    ts(c_tie, T.rc[:, 0:1], -128.0, 1920.0, ALU.mult, ALU.add, ["rc"], ["c_tie"], 64)
    ts(c_step, T.stp[:, 0:1], c_tie, None, ALU.add, None, ["stp", "c_tie"], ["c_step"], 64)
    ts(mat("dtie"), mat("I"), c_tie, 1.0 / 128, ALU.mult, ALU.mult, ["I", "c_tie"], ["dtie"], 64)
    ts(T.d5[:], T.d4[:], 15, None, ALU.bitwise_and, None, ["d4"], ["d5"], 64)
    ts(T.d6[:], T.d5[:], 0.0, -4096.0, ALU.not_equal, ALU.mult, ["d5"], ["d6"], 64)
    tt(T.dgm[:], T.d6[:], T.x8[:], ALU.add, ["d6", "x8"], ["dgm"], ew(128))
    ms(T.rst[:], 0.0, ["rst"], 128)
    ms(T.rst[:, 0::16], -float(2 ** 26), ["rst"], 64)
    ts(c_rep, T.rc[:, 0:1], 16.0, None, ALU.add, None, ["rc"], ["c_rep"], 64)
    ts(T.rep[:], mat("one")[:, 0::16], c_rep, None, ALU.mult, None, ["one", "c_rep"], ["rep"], 64)
    for nm, src, key in (("u16", T.ub, "ub"), ("v16", T.vb, "vb")):
        ms(src[:, 0:16], 0.0, [key + "0"], 64)
        line("A", mat(nm), src[:].indirect(T.rep[:]), 16.0, 0.0, [key, key + "0", "rep"], [nm], ("gV", 128),
             ("gA", 128), nm)
    line("A", mat("v2k"), mat("v16"), 128.0, 0.0, ["v16"], ["v2k"], ew(64), ew(128), "v2k")

    ts(T.kqi[:], T.posi[:], 960, None, ALU.bitwise_and, None, ["posi"], ["kqi"], LN)
    op("V", lambda: V.tensor_copy(T.kq[:, 0:LN], T.kqi[:]), ["kqi"], ["kq0"], ew(LN))
    ts(T.qa[:], T.posi[:], -1.0 / 4096, None, ALU.mult, None, ["posi"], ["qa"], LN)
    ts(T.qb[:], T.posi[:], 64.0, None, ALU.is_lt, None, ["posi"], ["qb"], LN)
    tt(T.q[:, 0:LN], T.qa[:], T.qb[:], ALU.add, ["qa", "qb"], ["q0_%d" % c for c in range(NC)], ew(2 * LN))

    def kq_masks(src):
        r = T.rank_of(src)
        dst = [cores[(r + t) % N] for t in range(1, PL)]
        far = [d for d in dst if topo.chip(d) != topo.chip(src)]
        narrow = topo.mask(src, far[0]) if far else 0
        out = {}
        for d in dst:
            m = topo.mask(src, d)
            out[d] = m if m == narrow else m & ~narrow
        return out

    def send_kq():
        mk = kq_masks(core)
        for t in range(1, PL):
            d = cores[(rank + t) % N]
            rid, pid = topo.addr(d)[0:2]
            g.remote_dma(T.kq[:, t * LN:(t + 1) * LN], T.kq[:, 0:LN], T.sem["kq%d" % t], T.sem.sent, pid, rid, mk[d])
    op("P", send_kq, ["kq0", "tab", "stp"], ["kqsent"], ("remote", 4), "sent",
       sum(popcount(m) for m in kq_masks(core).values()))
    for t in range(1, PL):
        src = cores[(rank - t) % N]
        op("X", None, ["kqsent"], ["kq%d" % t], ("none",), "kq%d" % t, popcount(kq_masks(src)[core]), lat="remote")

    m_out, m_in = topo.mask(core, nxt), topo.mask(prv, core)
    rid_n, pid_n = topo.addr(nxt)[0:2]

    def ply(t, c):
        w, i0 = CH[c], I0[c]
        cur[0] = c
        B = lambda s: T["%s%d" % (s, c)]
        K = lambda s: "%s%d" % (s, c)
        KT = lambda s: "%s%d_%d" % (s, t, c)
        q, nq, up, hit, kq = (T[s][:, t * LN + i0:t * LN + i0 + w] for s in ("q", "nq", "up", "hit", "kq"))
        qk, kk = KT("q"), "kq%d" % t
        off, idx, dsc = B("off")[:, 0:w // 16], B("idx"), B("dsc")[:, 0:w]
        lf, of, eq, sv, y = B("lf")[:, 0:w], B("of")[:, 0:w], B("eq")[:, 0:w], B("sv")[:, 0:w], B("yp")[:, 64:64 + w]
        ca, cc = T.ca[:, 8 * i0:8 * (i0 + w)], T.cc[:, 8 * i0:8 * (i0 + w)]
        ones = T.ones[:, 0:w]
        tag = "%d.%d " % (t, c)
        ps = lambda s, n=w: T[BK[s]][:, 0:n]

        mm("off", [([("I", T.dgm[:, 0:w]), ("k8", kq)], ["dgm", kk]), ([("q8", q)], [qk])], tag + "mm_off", w)
        op("V", lambda: V.tensor_tensor_scan(dsc, T.rst[:, 0:w], ps("off"), 0.0, ALU.add, ALU.max),
           ["rst", BK["off"]], [K("dsc")], ew(w), bank=[BK["off"]], name=tag + "dsc")
        line("V", off, dsc[:, 15::16], 1.0, -0.4375, [K("dsc")], [K("off")], ew(64), ew(64), tag + "off")
        either(tag + "lf", "A", lambda: V.tensor_scalar(lf, q, -4096.0, 0.0, ALU.mult, ALU.max),
               lambda: A.activation(lf, q, AF.Relu, scale=-4096.0), [qk], [K("lf")], ew(64), ew(64))
        bucket = [([("k128", kq), ("n448", ones)], [kk, "ones"]), ([("q128", q), ("C33", ones), ("nC33", ones)], [qk])]
        same = [([("nBIG", eq)], [K("eq")])] if t else []
        if t:
            either(tag + "of", "A", lambda: V.tensor_copy(of, cc.indirect(off)),
                   lambda: A.activation(of, cc.indirect(off), AF.Identity), [K("cc"), K("off")], [K("of")],
                   ("gV", w), ("gA", w))
            tt(eq, cc.indirect(off), lf, ALU.is_equal, [K("cc"), K("off"), K("lf")], [K("eq")], ("gV", w),
               name=tag + "eq")
            mm("ZO", bucket + [([("I", of)], [K("of")])] + same, tag + "mm_ZO", w)
            relu("A", idx[:, 0:w], ps("ZO"), 0.0, [BK["ZO"]], [K("idxO")], w, [BK["ZO"]], tag + "idxO")
        mm("ZL", bucket + [([("I", lf)], [K("lf")])] + same, tag + "mm_ZL", w)
        relu("V", idx[:, 64:64 + w], ps("ZL"), 0.0, [BK["ZL"]], [K("idxL")], w, [BK["ZL"]], tag + "idxL")
        keys = lambda s, h, a, b: ["%s%s%d_%d" % (s, h, c, j) for j in range(a // 8, (b + 7) // 8)]
        for h, text in zip("OL", CFG["cut"][t][c].split("|")):
            x0, sign = (32 * i0, -1.0) if h == "O" else (32 * i0 + 16 * w, 1.0)
            G, R = T.gb[:, x0:x0 + 16 * w], T.rb[:, x0:x0 + 16 * w]
            H, hk = (T.hb[:, x0:x0 + 16 * w], K("hb" + h)) if t else (T.h0[:, 0:16 * w], "h0")
            if t and h == "O":
                line("A", H[:, 0::16], ca.indirect(off), 1.0, 512.0, [K("ca"), K("off")], [hk], ("gV", w), ("gA", w),
                     tag + "a0")
            elif t:
                ts(H[:, 0::16], RO[:, 15::16], 0.0, 512.0, ALU.max, ALU.add, keys("r", "O", 0, w), [hk], 64,
                   name=tag + "link")
            RO, a0, x1 = R, 0, 64 * (h == "L")
            for e, a, b, dot in pieces(text):
                line(e, G[:, 16 * a:16 * b], T.tab[:].indirect(idx[:, x1 + a:x1 + b]), sign, -32.0,
                     tabk + [K("idx" + h)], keys("g", h, a, b), ("gV", 16 * (b - a)), ("gA", 16 * (b - a)),
                     tag + "g%s%d" % (h, a))
                if dot:
                    a, a0 = a0, b
                    op("V", lambda a=a, b=b, G=G, R=R, H=H: V.tensor_tensor_scan(
                        R[:, 16 * a:16 * b], H[:, 16 * a:16 * b], G[:, 16 * a:16 * b], 0.0, ALU.max, ALU.add),
                       keys("g", h, a, b) + [hk], keys("r", h, a, b), ew((b - a) * 8), name=tag + "scan" + h)
        rk, acc = keys("r", "L", 0, w), B("acc")[:, 0:w]
        ts(y, R[:, 15::16], 0.0, 127.0, ALU.max, ALU.min, rk, [K("yp")], 64, name=tag + "y")
        relu("A", acc, R[:, 15::16], 0.0, rk, [K("acc")], w, name=tag + "acc")
        for dst, src, key, out in ((cc, lf, "lf", T.yc), (ca, acc, "acc", T.ya)):
            ck = K("cc" if key == "lf" else "ca")
            op("V", lambda dst=dst, src=src: V.tensor_copy(dst.indirect(off), src), [K(key), K("off")], [ck],
               ("sV", w), name=tag + "sc_" + key)
            if t == PL - 1:
                op("S", lambda dst=dst, out=out: g.sync.dma_start(out[:, 8 * i0:8 * (i0 + w)], dst),
                   [ck, "q%d_%d" % (t, NC - 1)], [], ("dma",), "st", 16, lat="copy")
        st, mx, mf, yp = ps("ST", 128), B("mx"), B("mf"), B("yp")
        top = T[BK["ST"]][0:w, 0:128]
        mm("ST", [([(st, mat("I"), mat("tie"), 128), (top, lf, mat("n4k"), 128), (top, q, mat("nBIG"), 128)],
                   ["I", "tie", "n4k", "nBIG", qk, K("lf")]),
                  ([(st, yp[:, 64:192], mat("u16"), 128), (st, yp[:, 0:128], mat("v16"), 128)],
                   [K("yp"), "u16", "v16"])], tag + "mm_S")
        op("V", lambda: V.tensor_tensor_scan(mx[:], T.rst[:], st, 0.0, ALU.add, ALU.max), ["rst", BK["ST"]],
           [K("mx")], ew(128), bank=[BK["ST"]], name=tag + "max")
        op("V", lambda: V.tensor_tensor_scan(mf[:, ::-1], T.rst[:], mx[:, ::-1], 0.0, ALU.add, ALU.max),
           ["rst", K("mx")], [K("mf")], ew(128), name=tag + "mf")
        e1, e2, ex = ps("E1"), ps("E2"), ps("X")
        mm("E1", [([("dtie", ones), ("n4k", lf), ("nBIG", q)], ["ones", qk, K("lf")]), ([("u16", y)], [K("yp")]),
                  ([(e1, mf[:], T.idm[:, 0:w], 256)], ["idm", K("mf")])], tag + "mm_E1", w)
        mm("E2", [([("v2k", y)], [K("yp")]), ([(e2, mf[:], T.idm[:, 64:64 + w], 256)], ["idm", K("mf")])],
           tag + "mm_E2", w)
        tt(nq, e1, q, ALU.max, [BK["E1"], qk], [KT("nq")], ew(w), [BK["E1"]], tag + "nq")
        relu("A", sv, e2, c_step, [BK["E2"], "c_step"], [K("sv")], w, [BK["E2"]], tag + "sv")
        mm("X", [([("one3", q), ("n3unit", lf), ("half", ones), ("unit", kq)], [qk, kk, "ones", K("lf")]),
                 ([("none", nq)], [KT("nq")]),
                 ([("nstep", sv), ("C17", ones), ("nC17", ones), ("none", q), ("stay", nq), ("step", sv)],
                  [K("sv")])], tag + "mm_X", w)
        op("V", lambda: [V.tensor_tensor(hit, ex, q, ALU.is_equal),
                         V.tensor_scalar(up, ex, -1.0, 0.0, ALU.mult, ALU.min)],
           [BK["X"], qk], [KT("up")], ("two", w), inc=2, bank=[BK["X"]], name=tag + "up")
        if t < PL - 1:
            land, ar = T.q[:, (t + 1) * LN + i0:(t + 1) * LN + i0 + w], "ar%d_%d" % (t + 1, c)

            def hop():
                g.remote_dma_fused([RemoteDMATransfer(
                    dst_ids=[DstId(rid=rid_n, pnc=pid_n)], dma_engine_mask=m_out, remote_sem=T.sem[ar],
                    srcs=[nq, up, hit], dsts=[land], alu_op=1)], local_sem=T.sem.sent)
            op("P", hop, [KT("nq"), KT("up")], [KT("hop")], ("remote", 1), "sent", popcount(m_out), name=tag + "hop")
            op("X", None, [KT("hop")], ["q%d_%d" % (t + 1, c)], ("none",), ar, popcount(m_in), lat="remote")
        else:
            mm("Y", [([("n4k", nq)], [KT("nq")]), ([("n4k", up), ("n4k", hit)], [KT("up")])], tag + "mm_Y", w)
            yo = T.ylf[:, i0:i0 + w]
            relu("A", yo, ps("Y"), 0.0, [BK["Y"]], [K("ylf")], w, [BK["Y"]], tag + "yl")
            op("S", lambda: g.sync.dma_start(T.yl[:, i0:i0 + w], yo), [K("ylf")], [], ("dma",), "st", 16,
               lat="small")

    for t in range(PL):
        for c in range(NC):
            ply(t, c)
    return ops


def find_deps(ops):
    lastw, readers, lastb = {}, {}, {}
    deps = []
    who = [j if "both" in o else o["eng"] for j, o in enumerate(ops)]
    for j, o in enumerate(ops):
        d = set()
        for key in o["rd"]:
            if key in lastw:
                d.add(lastw[key])
        for key in o["wr"]:
            if key in lastw:
                d.add(lastw[key])
            d.update(readers.get(key, []))
        for key in o["bank"]:
            d.update(x for x in lastb.get(key, []) if who[x] != who[j])
        d.discard(j)
        deps.append(sorted(d))
        for key in o["rd"]:
            readers.setdefault(key, []).append(j)
        for key in o["wr"]:
            lastw[key] = j
            readers[key] = []
        for key in o["bank"]:
            lastb[key] = [x for x in lastb.get(key, []) if who[x] == who[j]] + [j]
    return deps


def busy(o, e):
    c = o["cost"]
    if c[0] == "ew":
        return e["fixa" if o["eng"] == "A" else "fix"] + max(64, c[1]) * e["cyc"]
    if c[0] == "two":
        return 2 * busy(dict(o, cost=("ew", c[1])), e)
    if c[0] == "gV":
        return 0.05 + c[1] * e["r"] * e["cyc"]
    if c[0] == "gA":
        return 0.065 + c[1] * e["r"] * e["cyc"]
    if c[0] == "sV":
        return 0.05 + c[1] * e["sc"] * e["cyc"]
    if c[0] == "pe":
        return c[1] * e["pe"]
    if c[0] == "pool":
        return 0.13 + 2 * c[1] * e["cyc"]
    if c[0] == "remote":
        return c[1] * e["issue"]
    if c[0] == "dma":
        return 0.06
    return 0.0


def latency(o, e):
    if isinstance(o["lat"], tuple):
        return e["load0"] + e["load"] * o["lat"][1]
    return e[o["lat"]] if o["lat"] else 0.0


def gap(a, b, e):
    if a["lat"]:
        return latency(a, e)
    if b["eng"] == "X" or (a["eng"] == "E" and b["eng"] == "E"):
        return 0.0
    return e["same"] if a["eng"] == b["eng"] else e["hop"]


def arrange(ops, deps, e):
    n = len(ops)
    nc = len(CFG["ch"])
    succ = [[] for _ in range(n)]
    for j in range(n):
        for d in deps[j]:
            succ[d].append(j)
    dur = [busy(o, e) for o in ops]
    prio = [0.0] * n
    for j in range(n - 1, -1, -1):
        tail = latency(ops[j], e)
        if not succ[j] and ops[j]["chunk"] is not None:
            tail += e["lag"] * (nc - 1 - ops[j]["chunk"])
        prio[j] = dur[j] + max([tail] + [gap(ops[j], ops[s], e) + prio[s] for s in succ[j]])
    left = [len(d) for d in deps]
    rdy = {}
    for j in range(n):
        if not left[j]:
            rdy.setdefault(ops[j]["eng"], {})[j] = 0.0
    free, end, order = {}, [0.0] * n, []
    while len(order) < n:
        first = {q: max(min(r.values()), free.get(q, 0.0)) for q, r in rdy.items() if r}
        eng = min(first, key=lambda q: first[q])
        lim = first[eng] + e["slack"]
        j = max((x for x, v in rdy[eng].items() if v <= lim), key=lambda x: prio[x])
        end[j] = max(rdy[eng][j], free.get(eng, 0.0)) + dur[j]
        if eng != "X":
            free[eng] = end[j]
        order.append(j)
        del rdy[eng][j]
        for s in succ[j]:
            left[s] -= 1
            if not left[s]:
                rdy.setdefault(ops[s]["eng"], {})[s] = max(end[d] + gap(ops[d], ops[s], e) for d in deps[s])
    return order


def refine(ops, deps, order, models, steps, hot=0.1, cold=0.02, seed=10, turn=0.3):
    n = len(ops)
    rnd = np.random.RandomState(seed).random_sample(4 * steps).tolist()
    eng = ["VAEPSX".index(o["eng"]) for o in ops]
    above, near = [], []
    for j in range(n):
        far = 0
        for d in deps[j]:
            far |= above[d]
        near.append([d for d in deps[j] if not far >> d & 1])
        above.append(far | sum(1 << d for d in near[j]))
    deps = near
    succ = [[] for _ in range(n)]
    for j in range(n):
        for d in deps[j]:
            succ[d].append(j)
    last = [j for j in range(n) if ops[j]["eng"] == "S" and not succ[j]]
    tabs = [([busy(o, e) for o in ops], [[(d, gap(ops[d], ops[j], e)) for d in deps[j]] for j in range(n)],
             [latency(o, e) for o in ops]) for e in models]
    both = {j: [[busy(dict(o, eng=q, cost=o["both"][q]), e) for e in models] for q in "VA"]
            for j, o in enumerate(ops) if "both" in o}
    movable = sorted(both)

    def flip(j):
        eng[j] = 1 - eng[j]
        for tab, d in zip(tabs, both[j][eng[j]]):
            tab[0][j] = d

    def run(order, a, ends, most=1e9):
        out, worse, ahead, seen, rest = [], 0.0, [], set(), order[a:]
        for j in order[a - 1::-1] if a else []:
            if eng[j] not in seen:
                seen.add(eng[j])
                ahead.append(j)
                if len(seen) == 6:
                    break
        for (dur, pre, tail), (was, old) in zip(tabs, ends):
            end, free = old[:], [0.0] * 6
            for j in ahead:
                free[eng[j]] = end[j]
            for j in rest:
                q = eng[j]
                t = free[q] if q < 5 else 0.0
                for d, x in pre[j]:
                    x += end[d]
                    if x > t:
                        t = x
                end[j] = free[q] = t + dur[j]
            out.append((max(end[j] + tail[j] for j in last), end))
            worse += out[-1][0] - was
            if worse > most + (0.1 if len(out) < len(tabs) else 0.0):
                return None
        return out

    def meets(order, m, end):
        dur, pre, tail = tabs[m]
        before, prev = {}, {}
        for j in order:
            before[j] = prev.get(eng[j])
            prev[eng[j]] = j
        j, out = max(last, key=lambda j: end[j] + tail[j]), []
        while j is not None:
            t, i = end[j] - dur[j] - 1e-9, before[j]
            if eng[j] < 5 and i is not None and end[i] >= t:
                out.append((i, j))
                j = i
            else:
                j = next((d for d, x in pre[j] if end[d] + x >= t), None)
        return out

    ends = run(order, 0, [(0.0, [0.0] * n)] * len(tabs))
    best, pairs = (1e9, order, eng[:]), []
    for s in range(steps):
        x0, x1, x2, x3 = rnd[4 * s:4 * s + 4]
        if not pairs:
            m = int(x0 * len(tabs))
            pairs = meets(order, m, ends[m][1])
        i, j = pairs[int(x1 * len(pairs))]
        room = -math.log(x3) * hot * (cold / hot) ** (s / steps) * len(tabs)
        if x2 < turn:
            c = movable[int(x1 * len(movable))] if x2 < turn / 6 else i if x2 < turn / 2 else j
            if c not in both:
                continue
            flip(c)
            new, e2 = order, run(order, order.index(c), ends, room)
            if e2 is None:
                flip(c)
        else:
            a, b = order.index(i), order.index(j) + 1
            seg = order[a:b]
            up = x2 < (1 + turn) / 2
            need = {j if up else i}
            for x in (seg[::-1] if up else seg):
                if x in need:
                    need.update(deps[x] if up else succ[x])
            if (i if up else j) in need:
                pairs.remove((i, j))
                continue
            new = order[:a] + [x for x in seg if (x in need) == up] + [x for x in seg if (x in need) != up] + order[b:]
            e2 = run(new, a, ends, room)
        if e2 is not None:
            order, ends, pairs = new, e2, []
            if sum(x[0] for x in ends) < best[0]:
                best = (sum(x[0] for x in ends), order, eng[:])
        elif x0 > 0.9:
            pairs = []
    return best[1], {ops[j]["name"]: "VA"[best[2][j]] for j in movable}


def plan(ops):
    deps = find_deps(ops)
    return refine(ops, deps, arrange(ops, deps, EST), [dict(EST, **m) for m in MODELS], STEPS)


ORDER = {}


def rank_program(g, core, T, topo):
    if T.rank_of(core) is None:
        return
    if "o" not in ORDER:
        ORDER["o"], ORDER["pick"] = plan(build(g, core, T, topo))
    ops = build(g, core, T, topo, ORDER["pick"])
    deps = find_deps(ops)
    place = {j: p for p, j in enumerate(ORDER["o"])}
    queue = {"V": g.vector, "A": g.scalar, "E": g.tensor, "P": g, "S": g.sync}
    count, known, done = {}, {q: {} for q in queue}, {}
    for j in ORDER["o"]:
        o = ops[j]
        count[o["sem"]] = count.get(o["sem"], 0) + o["inc"]
        if o["eng"] == "X":
            done[j] = (o["sem"], count[o["sem"]], {})
            continue
        kn = known[o["eng"]]
        for d in sorted(deps[j], key=lambda x: -place[x]):
            if o["eng"] == "E" and ops[d]["eng"] == "E":
                continue
            s, val, clock = done[d]
            if kn.get(s, 0) < val:
                queue[o["eng"]].wait_ge(T.sem[s], val)
                kn[s] = val
            for s2, v2 in clock.items():
                if kn.get(s2, 0) < v2:
                    kn[s2] = v2
        ins = o["fn"]()
        for x in ins if isinstance(ins, list) else [] if ins is None else [ins]:
            x.then_inc(T.sem[o["sem"]], 1 if isinstance(ins, list) else o["inc"])
        done[j] = (o["sem"], count[o["sem"]], dict(kn))
    for s, val in count.items():
        if max(kn.get(s, 0) for kn in known.values()) < val:
            g.wait_ge(T.sem[s], val)
